import numpy as np
import ml_dtypes


def mxq(x, axis, fmt="e4m3"):
    dtype, down = {"e4m3": (ml_dtypes.float8_e4m3fn, 7), "e5m2": (ml_dtypes.float8_e5m2, 14)}[fmt]
    v = np.moveaxis(np.asarray(x, np.float32).astype(ml_dtypes.bfloat16).astype(np.float64), axis, -1)
    blocks = v.reshape(v.shape[:-1] + (-1, 32))
    amax = np.abs(blocks).max(-1, keepdims=True)
    byte = np.maximum(np.where(amax > 0, np.frexp(amax)[1] - 1 + 127, 0) - down, 1)
    scale = np.exp2(byte - 127.0)
    codes = (blocks / scale).astype(np.float32).astype(dtype).astype(np.float64)
    return np.moveaxis((codes * scale).reshape(v.shape), -1, axis)


WIDE = False


def mx_kscale(k):
    if not WIDE:
        return np.ones(k)
    levels = np.array([24, -24, 12, -12, 0])
    if k % 512:
        return np.exp2(np.random.permutation(np.resize(levels, k // 32))).repeat(32)
    a = np.empty((k // 512, 16))
    for p in range(k // 512):
        a[p, :8] = np.random.permutation(np.resize(levels, 8))
        for g in range(8):
            far = levels[np.abs(levels - a[p, g]) >= 10]
            a[p, g + 8] = far[np.random.randint(len(far))]
    return np.exp2(a.ravel()).repeat(32)


def f64(x):
    return np.asarray(x).astype(np.float64)


def striped(idx):
    return np.tile(idx.reshape(-1, 16).T, (8, 1)).astype(np.uint16)


def unstriped(offs):
    return offs[:16].T.reshape(-1).astype(np.int64)


E2M1 = np.array([0.0, 0.5, 1.0, 1.5, 2.0, 3.0, 4.0, 6.0, -0.0, -0.5, -1.0, -1.5, -2.0, -3.0, -4.0, -6.0])


def pack_weight(w, fmt):
    k, n = w.shape
    w = f64(np.asarray(w, np.float32).astype(ml_dtypes.bfloat16)).reshape(k // 32, 32, n)
    amax = np.abs(w).max(1)
    if fmt == "e4m3":
        byte = np.frexp(amax)[1] - 1 + 127 - 7
    else:
        mant, ex = np.frexp(amax / 6.0)
        byte = np.where(mant > 0.5, ex, ex - 1) + 127
    byte = np.clip(np.where(amax > 0, byte, 1), 1, 254)
    scaled = (w * np.exp2(127.0 - byte)[:, None, :]).reshape(k, n).astype(np.float32)
    by_word = np.ascontiguousarray(scaled.reshape(k // 512, 128, 4, n).transpose(0, 1, 3, 2))
    if fmt == "e4m3":
        words = by_word.astype(ml_dtypes.float8_e4m3fn).view(np.uint8)
    else:
        c = by_word.astype(ml_dtypes.float4_e2m1fn).view(np.uint8) & 0xF
        words = (c[..., 0::2] | (c[..., 1::2] << 4)).reshape(k // 512, 128, 2 * n)
    return np.ascontiguousarray(words), np.ascontiguousarray(byte.astype(np.uint8).reshape(k // 512, 16, n))


def unpack_weight(words, scales, fmt):
    g, _, n = scales.shape
    words = np.ascontiguousarray(words).reshape(g, 128, n, -1)
    if fmt == "e4m3":
        vals = words.view(ml_dtypes.float8_e4m3fn).astype(np.float64)
    else:
        nib = np.empty((g, 128, n, 4), np.uint8)
        nib[..., 0::2] = words & 0xF
        nib[..., 1::2] = words >> 4
        vals = E2M1[nib]
    vals = vals * np.repeat(np.exp2(scales.astype(np.float64) - 127.0), 8, axis=1)[..., None]
    return vals.transpose(0, 1, 3, 2).reshape(g * 512, n)


def sigm(f):
    return 1.0 / (1.0 + np.exp(-np.maximum(f, -700.0)))


K, M, N, T, J = 512, 512, 512, 2048, 1024


def setup_inputs():
    n = np.random.standard_normal
    s = mx_kscale(K)[:, None]
    s2 = mx_kscale(M)[:, None]
    h = np.tanh(n((N, T)))
    p_tab = pack_weight(h * s2, "e4m3")
    p_wz = pack_weight(n((K, N)) / np.sqrt(K) / s, "e2m1")
    p_uz = pack_weight(n((M, N)) / np.sqrt(M) / s2, "e4m3")
    p_wn = pack_weight(n((K, N)) / np.sqrt(K) / s, "e2m1")
    p_un = pack_weight(n((M, N)) / np.sqrt(M) / s2, "e4m3")
    return {
        "x": (n((K, J)) * s).astype(np.float32),
        "tab_words": p_tab[0],
        "tab_scales": p_tab[1],
        "wz_words": p_wz[0],
        "wz_scales": p_wz[1],
        "uz_words": p_uz[0],
        "uz_scales": p_uz[1],
        "wn_words": p_wn[0],
        "wn_scales": p_wn[1],
        "un_words": p_un[0],
        "un_scales": p_un[1],
        "bz": (0.3 * n(N)).astype(np.float32),
        "bn": (0.3 * n(N)).astype(np.float32),
        "hT": (h).astype(np.float32),
        "wgo": np.tile(np.random.uniform(0.5, 2.0, J), (128, 1)).astype(np.float32),
        "offs": striped(np.random.permutation(T)[:J]),
    }


def reference(x, tab_words, tab_scales, wz_words, wz_scales, uz_words, uz_scales, wn_words, wn_scales, un_words, un_scales, bz, bn, hT, wgo, offs):
    idx = unstriped(offs)
    x_ = mxq(f64(x), 0, "e4m3")
    tab_ = unpack_weight(tab_words, tab_scales, "e4m3")[:, idx]
    wz_ = unpack_weight(wz_words, wz_scales, "e2m1")
    uz_ = unpack_weight(uz_words, uz_scales, "e4m3")
    wn_ = unpack_weight(wn_words, wn_scales, "e2m1")
    un_ = unpack_weight(un_words, un_scales, "e4m3")
    sz = wz_.T @ x_ + uz_.T @ tab_
    z = sigm(sz + f64(bz)[:, None])
    xn = wn_.T @ x_
    hn = un_.T @ tab_
    cd = np.tanh(xn + f64(bn)[:, None] + z * hn)
    out = np.zeros((N, T))
    out[:, idx] = f64(wgo)[0] * (f64(hT)[:, idx] + z * (cd - f64(hT)[:, idx]))
    return out

@@ -1,0 +1,145 @@
+from contextlib import ExitStack
+
+import concourse.mybir as mybir
+
+K, M, N, T, J = 512, 512, 512, 2048, 1024
+FLOPS = 2 * (2 * K + 2 * M) * N * J
+
+F32 = mybir.dt.float32
+BF16 = mybir.dt.bfloat16
+I32 = mybir.dt.int32
+U32 = mybir.dt.uint32
+U16 = mybir.dt.uint16
+U8 = mybir.dt.uint8
+FP8X4 = mybir.dt.float8_e4m3fn_x4
+FP4X4 = mybir.dt.float4_e2m1fn_x4
+ACT = mybir.ActivationFunctionType
+ALU = mybir.AluOpType
+
+P = 128
+PACK = 4
+JH = 512
+HALVES = J // JH
+CHUNKS = N // P
+
+
+def tile_list_tgn_mgu_kernel(
+    tc, x, tab_words, tab_scales, wz_words, wz_scales, uz_words, uz_scales,
+    wn_words, wn_scales, un_words, un_scales, bz, bn, hT, wgo, offs, out,
+):
+    nc = tc.nc
+    with ExitStack() as ctx:
+        keep = ctx.enter_context(tc.tile_pool(name="keep", bufs=1))
+        work = ctx.enter_context(tc.tile_pool(name="work", bufs=4))
+        psum = ctx.enter_context(tc.psum_pool(name="psum", bufs=1))
+
+        offsets = keep.tile([P, J // 16], U16, name="offsets")
+        nc.sync.dma_start(offsets[:], offs)
+
+        def load_scale_rows(plane, rows):
+            for q in range(4):
+                nc.sync.dma_start(plane[32 * q : 32 * q + 4, :], rows[0, 4 * q : 4 * q + 4, :].bitcast(I32))
+
+        tab_s = keep.tile([P, T // 4], I32, name="tab_s", align_bytes=64)
+        w_s = keep.tile([P, 4, N // 4], I32, name="w_s", align_bytes=64)
+        nc.gpsimd.memset(tab_s[:], 0)
+        nc.gpsimd.memset(w_s[:], 0)
+        load_scale_rows(tab_s, tab_scales)
+        tab_w = keep.tile([P, T], I32, name="tab_w", align_bytes=64)
+        nc.sync.dma_start(tab_w[:], tab_words[0].rearrange("p t i -> p (t i)").bitcast(I32))
+
+        x_rows = x.rearrange("(p i) j -> p i j", i=PACK)
+        x_raw = [keep.tile([P, PACK, JH], F32, name=f"x_raw{h}") for h in range(HALVES)]
+        h_sb = [keep.tile([P, T], F32, name=f"h_sb{c}") for c in range(CHUNKS)]
+        nc.sync.dma_start(x_raw[0][:], x_rows[:, :, 0:JH])
+
+        wz_w = keep.tile([P, N // 2], I32, name="wz_w", align_bytes=64)
+        uz_w = keep.tile([P, N], I32, name="uz_w", align_bytes=64)
+        wn_w = keep.tile([P, N // 2], I32, name="wn_w", align_bytes=64)
+        un_w = keep.tile([P, N], I32, name="un_w", align_bytes=64)
+        nc.sync.dma_start(wz_w[:], wz_words[0].bitcast(I32))
+        nc.sync.dma_start(uz_w[:], uz_words[0].rearrange("p n i -> p (n i)").bitcast(I32))
+        load_scale_rows(w_s[:, 0, :], wz_scales)
+        load_scale_rows(w_s[:, 1, :], uz_scales)
+        bz_sb = keep.tile([P, CHUNKS], F32, name="bz_sb")
+        bn_sb = keep.tile([P, CHUNKS], F32, name="bn_sb")
+        with nc.allow_non_contiguous_dma(reason="one bias value to a partition"):
+            nc.scalar.dma_start(bz_sb[:], bz.rearrange("(c p) -> p c", p=P))
+            nc.scalar.dma_start(bn_sb[:], bn.rearrange("(c p) -> p c", p=P))
+        nc.sync.dma_start(un_w[:], un_words[0].rearrange("p n i -> p (n i)").bitcast(I32))
+        nc.sync.dma_start(wn_w[:], wn_words[0].bitcast(I32))
+        load_scale_rows(w_s[:, 3, :], un_scales)
+        load_scale_rows(w_s[:, 2, :], wn_scales)
+        nc.sync.dma_start(h_sb[0][:], hT[0:P, :])
+        nc.sync.dma_start(x_raw[1][:], x_rows[:, :, JH:J])
+        nc.sync.dma_start(h_sb[1][:], hT[P : 2 * P, :])
+        wgo_sb = keep.tile([P, J], F32, name="wgo_sb")
+        nc.sync.dma_start(wgo_sb[:], wgo)
+        nc.sync.dma_start(h_sb[2][:], hT[2 * P : 3 * P, :])
+        nc.sync.dma_start(h_sb[3][:], hT[3 * P : 4 * P, :])
+
+        def part(h):
+            return offsets[:, h * (JH // 16) : (h + 1) * (JH // 16)]
+
+        v_s, v_w, x_s, x_w = [], [], [], []
+        for h in range(HALVES):
+            gs = keep.tile([P, JH], U8, name=f"v_s{h}", align_bytes=64)
+            gw = keep.tile([P, JH], U32, name=f"v_w{h}", align_bytes=64)
+            nc.vector.tensor_copy(gs[:], tab_s[:].bitcast(U8).indirect(part(h)))
+            nc.vector.tensor_copy(gw[:], tab_w[:].bitcast(U32).indirect(part(h)))
+            v_s.append(gs)
+            v_w.append(gw)
+        for h in range(HALVES):
+            xb = keep.tile([P, JH, PACK], BF16, name=f"xb{h}", align_bytes=64)
+            nc.scalar.copy(
+                out=xb[:].rearrange("p (a b) i -> p a i b", b=4),
+                in_=x_raw[h][:].rearrange("p i (a b) -> p a i b", b=4),
+            )
+            qs = keep.tile([P, JH], U8, name=f"x_s{h}", align_bytes=64)
+            qw = keep.tile([P, JH], U32, name=f"x_w{h}", align_bytes=64)
+            nc.vector.quantize_mx(out=qw[:].bitcast(FP8X4), scales=qs[:], in_=xb[:].rearrange("p j i -> p (j i)"))
+            x_s.append(qs)
+            x_w.append(qw)
+
+        def fp4_cols(words, c):
+            return words[:, 64 * c : 64 * (c + 1)].bitcast(FP4X4)
+
+        def fp8_cols(words, c):
+            return words[:, P * c : P * (c + 1)].bitcast(FP8X4)
+
+        def scale_cols(slot, c):
+            return w_s[:, slot, 32 * c : 32 * (c + 1)].bitcast(U8)
+
+        for c in range(CHUNKS):
+            o_sb = keep.tile([P, T], F32, name=f"o_sb{c}")
+            nc.gpsimd.memset(o_sb[:], 0.0)
+            for h in range(HALVES):
+                xw, xs, vw, vs = x_w[h][:].bitcast(FP8X4), x_s[h][:], v_w[h][:].bitcast(FP8X4), v_s[h][:]
+                sz = psum.tile([P, JH], F32, name="sz", bufs=2)
+                hn = psum.tile([P, JH], F32, name="hn", bufs=3)
+                xn = psum.tile([P, JH], F32, name="xn", bufs=3)
+                nc.tensor.matmul_mx(out=sz[:], lhsT=fp8_cols(uz_w, c), lhsT_scale=scale_cols(1, c), rhs=vw, rhs_scale=vs, start=True, stop=False)
+                nc.tensor.matmul_mx(out=sz[:], lhsT=fp4_cols(wz_w, c), lhsT_scale=scale_cols(0, c), rhs=xw, rhs_scale=xs, start=False, stop=True)
+                nc.tensor.matmul_mx(out=hn[:], lhsT=fp8_cols(un_w, c), lhsT_scale=scale_cols(3, c), rhs=vw, rhs_scale=vs, start=True, stop=True)
+                nc.tensor.matmul_mx(out=xn[:], lhsT=fp4_cols(wn_w, c), lhsT_scale=scale_cols(2, c), rhs=xw, rhs_scale=xs, start=True, stop=True)
+
+                hg = work.tile([P, JH], F32, name="hg")
+                nc.vector.tensor_copy(hg[:], h_sb[c][:].indirect(part(h)))
+                z = work.tile([P, JH], F32, name="z")
+                nc.scalar.activation(z[:], sz[:], ACT.Sigmoid, bias=bz_sb[:, c : c + 1])
+                zh = work.tile([P, JH], F32, name="zh")
+                nc.vector.tensor_tensor(zh[:], hn[:], z[:], ALU.mult)
+                pre = work.tile([P, JH], F32, name="pre")
+                nc.vector.tensor_tensor(pre[:], xn[:], zh[:], ALU.add)
+                cd = work.tile([P, JH], F32, name="cd")
+                nc.scalar.activation(cd[:], pre[:], ACT.Tanh, bias=bn_sb[:, c : c + 1])
+                d = work.tile([P, JH], F32, name="d")
+                nc.gpsimd.tensor_tensor(d[:], cd[:], hg[:], ALU.subtract)
+                e = work.tile([P, JH], F32, name="e")
+                nc.gpsimd.tensor_tensor(e[:], d[:], z[:], ALU.mult)
+                s = work.tile([P, JH], F32, name="s")
+                nc.gpsimd.tensor_tensor(s[:], e[:], hg[:], ALU.add)
+                r = work.tile([P, JH], F32, name="r")
+                nc.gpsimd.tensor_tensor(r[:], s[:], wgo_sb[:, h * JH : (h + 1) * JH], ALU.mult)
+                nc.vector.tensor_copy(o_sb[:].indirect(part(h)), r[:])
+            nc.sync.dma_start(out[c * P : (c + 1) * P, :], o_sb[:])

@@ -21,6 +21,7 @@ PACK = 4
 JH = 512
 HALVES = J // JH
 CHUNKS = N // P
+ZERO_FROM = (0, 0, 0, 0, 0, 1, 2, 3)
 
 
 def tile_list_tgn_mgu_kernel(
@@ -36,70 +37,68 @@ def tile_list_tgn_mgu_kernel(
         offsets = keep.tile([P, J // 16], U16, name="offsets")
         nc.sync.dma_start(offsets[:], offs)
 
-        def load_scale_rows(plane, rows):
-            for q in range(4):
-                nc.sync.dma_start(plane[32 * q : 32 * q + 4, :], rows[0, 4 * q : 4 * q + 4, :].bitcast(I32))
+        def load_scale_rows(queue, plane, rows, quadrants):
+            for q in quadrants:
+                src = rows[0, 4 * q : 4 * q + 4, :].bitcast(I32)
+                queue.dma_start(plane[32 * q : 32 * (q + 1), :], src.unsqueeze(0).broadcast_to([8, *src.shape]))
 
         tab_s = keep.tile([P, T // 4], I32, name="tab_s", align_bytes=64)
-        w_s = keep.tile([P, 4, N // 4], I32, name="w_s", align_bytes=64)
-        nc.gpsimd.memset(tab_s[:], 0)
-        nc.gpsimd.memset(w_s[:], 0)
-        load_scale_rows(tab_s, tab_scales)
         tab_w = keep.tile([P, T], I32, name="tab_w", align_bytes=64)
-        nc.sync.dma_start(tab_w[:], tab_words[0].rearrange("p t i -> p (t i)").bitcast(I32))
-
-        x_rows = x.rearrange("(p i) j -> p i j", i=PACK)
-        x_raw = [keep.tile([P, PACK, JH], F32, name=f"x_raw{h}") for h in range(HALVES)]
-        h_sb = [keep.tile([P, T], F32, name=f"h_sb{c}") for c in range(CHUNKS)]
-        nc.sync.dma_start(x_raw[0][:], x_rows[:, :, 0:JH])
-
+        w_s = keep.tile([P, 4, N // 4], I32, name="w_s", align_bytes=64)
         wz_w = keep.tile([P, N // 2], I32, name="wz_w", align_bytes=64)
         uz_w = keep.tile([P, N], I32, name="uz_w", align_bytes=64)
         wn_w = keep.tile([P, N // 2], I32, name="wn_w", align_bytes=64)
         un_w = keep.tile([P, N], I32, name="un_w", align_bytes=64)
-        nc.sync.dma_start(wz_w[:], wz_words[0].bitcast(I32))
-        nc.sync.dma_start(uz_w[:], uz_words[0].rearrange("p n i -> p (n i)").bitcast(I32))
-        load_scale_rows(w_s[:, 0, :], wz_scales)
-        load_scale_rows(w_s[:, 1, :], uz_scales)
+        x_rows = x.rearrange("(p i) j -> p i j", i=PACK)
+        x_raw = [keep.tile([P, PACK, JH], F32, name=f"x_raw{h}") for h in range(HALVES)]
+        h_sb = [keep.tile([P, T], F32, name=f"h_sb{c}") for c in range(CHUNKS)]
+        wgo_sb = keep.tile([P, J], F32, name="wgo_sb")
         bz_sb = keep.tile([P, CHUNKS], F32, name="bz_sb")
         bn_sb = keep.tile([P, CHUNKS], F32, name="bn_sb")
-        with nc.allow_non_contiguous_dma(reason="one bias value to a partition"):
-            nc.scalar.dma_start(bz_sb[:], bz.rearrange("(c p) -> p c", p=P))
-            nc.scalar.dma_start(bn_sb[:], bn.rearrange("(c p) -> p c", p=P))
+
+        load_scale_rows(nc.sync, tab_s, tab_scales, range(4))
+        load_scale_rows(nc.sync, w_s[:, 1, :], uz_scales, range(2))
+        nc.sync.dma_start(tab_w[:], tab_words[0].rearrange("p t i -> p (t i)").bitcast(I32))
+        load_scale_rows(nc.sync, w_s[:, 1, :], uz_scales, range(2, 4))
+        load_scale_rows(nc.sync, w_s[:, 0, :], wz_scales, range(4))
+        nc.sync.dma_start(x_raw[0][:], x_rows[:, :, 0:JH])
+        nc.sync.dma_start(uz_w[:], uz_words[0].rearrange("p n i -> p (n i)").bitcast(I32))
+        load_scale_rows(nc.sync, w_s[:, 3, :], un_scales, range(4))
+        nc.sync.dma_start(wz_w[:], wz_words[0].bitcast(I32))
         nc.sync.dma_start(un_w[:], un_words[0].rearrange("p n i -> p (n i)").bitcast(I32))
         nc.sync.dma_start(wn_w[:], wn_words[0].bitcast(I32))
-        load_scale_rows(w_s[:, 3, :], un_scales)
-        load_scale_rows(w_s[:, 2, :], wn_scales)
+        with nc.allow_non_contiguous_dma(reason="one bias value to a partition"):
+            nc.sync.dma_start(bz_sb[:], bz.rearrange("(c p) -> p c", p=P))
+            nc.sync.dma_start(bn_sb[:], bn.rearrange("(c p) -> p c", p=P))
         nc.sync.dma_start(h_sb[0][:], hT[0:P, :])
-        nc.sync.dma_start(x_raw[1][:], x_rows[:, :, JH:J])
         nc.sync.dma_start(h_sb[1][:], hT[P : 2 * P, :])
-        wgo_sb = keep.tile([P, J], F32, name="wgo_sb")
+        nc.sync.dma_start(x_raw[1][:], x_rows[:, :, JH:J])
         nc.sync.dma_start(wgo_sb[:], wgo)
         nc.sync.dma_start(h_sb[2][:], hT[2 * P : 3 * P, :])
         nc.sync.dma_start(h_sb[3][:], hT[3 * P : 4 * P, :])
+        load_scale_rows(nc.gpsimd, w_s[:, 2, :], wn_scales, range(4))
+
 
         def part(h):
             return offsets[:, h * (JH // 16) : (h + 1) * (JH // 16)]
 
-        v_s, v_w, x_s, x_w = [], [], [], []
-        for h in range(HALVES):
+        def gather_table(h):
             gs = keep.tile([P, JH], U8, name=f"v_s{h}", align_bytes=64)
             gw = keep.tile([P, JH], U32, name=f"v_w{h}", align_bytes=64)
             nc.vector.tensor_copy(gs[:], tab_s[:].bitcast(U8).indirect(part(h)))
             nc.vector.tensor_copy(gw[:], tab_w[:].bitcast(U32).indirect(part(h)))
-            v_s.append(gs)
-            v_w.append(gw)
-        for h in range(HALVES):
-            xb = keep.tile([P, JH, PACK], BF16, name=f"xb{h}", align_bytes=64)
-            nc.scalar.copy(
-                out=xb[:].rearrange("p (a b) i -> p a i b", b=4),
+            return gw[:].bitcast(FP8X4), gs[:]
+
+        def quantise_x(h, xb):
+            copy = nc.vector.tensor_copy if h == 0 else nc.scalar.copy
+            copy(
+                out=xb.rearrange("p (a b) i -> p a i b", b=4),
                 in_=x_raw[h][:].rearrange("p i (a b) -> p a i b", b=4),
             )
             qs = keep.tile([P, JH], U8, name=f"x_s{h}", align_bytes=64)
             qw = keep.tile([P, JH], U32, name=f"x_w{h}", align_bytes=64)
-            nc.vector.quantize_mx(out=qw[:].bitcast(FP8X4), scales=qs[:], in_=xb[:].rearrange("p j i -> p (j i)"))
-            x_s.append(qs)
-            x_w.append(qw)
+            nc.vector.quantize_mx(out=qw[:].bitcast(FP8X4), scales=qs[:], in_=xb.rearrange("p j i -> p (j i)"))
+            return qw[:].bitcast(FP8X4), qs[:]
 
         def fp4_cols(words, c):
             return words[:, 64 * c : 64 * (c + 1)].bitcast(FP4X4)
@@ -110,36 +109,101 @@ def tile_list_tgn_mgu_kernel(
         def scale_cols(slot, c):
             return w_s[:, slot, 32 * c : 32 * (c + 1)].bitcast(U8)
 
-        for c in range(CHUNKS):
-            o_sb = keep.tile([P, T], F32, name=f"o_sb{c}")
-            nc.gpsimd.memset(o_sb[:], 0.0)
-            for h in range(HALVES):
-                xw, xs, vw, vs = x_w[h][:].bitcast(FP8X4), x_s[h][:], v_w[h][:].bitcast(FP8X4), v_s[h][:]
-                sz = psum.tile([P, JH], F32, name="sz", bufs=2)
-                hn = psum.tile([P, JH], F32, name="hn", bufs=3)
-                xn = psum.tile([P, JH], F32, name="xn", bufs=3)
-                nc.tensor.matmul_mx(out=sz[:], lhsT=fp8_cols(uz_w, c), lhsT_scale=scale_cols(1, c), rhs=vw, rhs_scale=vs, start=True, stop=False)
-                nc.tensor.matmul_mx(out=sz[:], lhsT=fp4_cols(wz_w, c), lhsT_scale=scale_cols(0, c), rhs=xw, rhs_scale=xs, start=False, stop=True)
-                nc.tensor.matmul_mx(out=hn[:], lhsT=fp8_cols(un_w, c), lhsT_scale=scale_cols(3, c), rhs=vw, rhs_scale=vs, start=True, stop=True)
-                nc.tensor.matmul_mx(out=xn[:], lhsT=fp4_cols(wn_w, c), lhsT_scale=scale_cols(2, c), rhs=xw, rhs_scale=xs, start=True, stop=True)
+        bank = {(role, i): psum.tile([P, JH], F32, name=f"{role}{i}") for role in ("sz", "hn", "xn") for i in range(2)}
 
-                hg = work.tile([P, JH], F32, name="hg")
-                nc.vector.tensor_copy(hg[:], h_sb[c][:].indirect(part(h)))
-                z = work.tile([P, JH], F32, name="z")
-                nc.scalar.activation(z[:], sz[:], ACT.Sigmoid, bias=bz_sb[:, c : c + 1])
-                zh = work.tile([P, JH], F32, name="zh")
-                nc.vector.tensor_tensor(zh[:], hn[:], z[:], ALU.mult)
-                pre = work.tile([P, JH], F32, name="pre")
-                nc.vector.tensor_tensor(pre[:], xn[:], zh[:], ALU.add)
-                cd = work.tile([P, JH], F32, name="cd")
-                nc.scalar.activation(cd[:], pre[:], ACT.Tanh, bias=bn_sb[:, c : c + 1])
-                d = work.tile([P, JH], F32, name="d")
-                nc.gpsimd.tensor_tensor(d[:], cd[:], hg[:], ALU.subtract)
-                e = work.tile([P, JH], F32, name="e")
-                nc.gpsimd.tensor_tensor(e[:], d[:], z[:], ALU.mult)
-                s = work.tile([P, JH], F32, name="s")
-                nc.gpsimd.tensor_tensor(s[:], e[:], hg[:], ALU.add)
-                r = work.tile([P, JH], F32, name="r")
-                nc.gpsimd.tensor_tensor(r[:], s[:], wgo_sb[:, h * JH : (h + 1) * JH], ALU.mult)
-                nc.vector.tensor_copy(o_sb[:].indirect(part(h)), r[:])
-            nc.sync.dma_start(out[c * P : (c + 1) * P, :], o_sb[:])
+        units = [(c, h) for h in range(HALVES) for c in range(CHUNKS)]
+        st = [dict() for u in units]
+        xq, vq = {}, {}
+        pre_all = keep.tile([P, len(units), JH], F32, name="pre_all", align_bytes=64)
+        z_all = keep.tile([P, len(units), JH], F32, name="z_all")
+        cd_all = keep.tile([P, len(units), JH], F32, name="cd_all")
+        s_all = keep.tile([P, len(units), JH], F32, name="s_all")
+        zh_all = keep.tile([P, len(units), JH], F32, name="zh_all")
+
+        def front(u):
+            c, h = units[u]
+            (xw, xs), (vw, vs) = xq[h], vq[h]
+            sz, hn, xn = bank["sz", u % 2], bank["hn", u % 2], bank["xn", u % 2]
+            nc.tensor.matmul_mx(out=sz[:], lhsT=fp8_cols(uz_w, c), lhsT_scale=scale_cols(1, c), rhs=vw, rhs_scale=vs, start=True, stop=False)
+            nc.tensor.matmul_mx(out=sz[:], lhsT=fp4_cols(wz_w, c), lhsT_scale=scale_cols(0, c), rhs=xw, rhs_scale=xs, start=False, stop=True)
+            nc.tensor.matmul_mx(out=hn[:], lhsT=fp8_cols(un_w, c), lhsT_scale=scale_cols(3, c), rhs=vw, rhs_scale=vs, start=True, stop=True)
+            nc.tensor.matmul_mx(out=xn[:], lhsT=fp4_cols(wn_w, c), lhsT_scale=scale_cols(2, c), rhs=xw, rhs_scale=xs, start=True, stop=True)
+            z = z_all[:, u, :]
+            nc.scalar.activation(z[:], sz[:], ACT.Sigmoid, bias=bz_sb[:, c : c + 1])
+            zh = zh_all[:, u, :]
+            nc.vector.tensor_tensor(zh[:], hn[:], z[:], ALU.mult)
+            nc.vector.scalar_tensor_tensor(pre_all[:, u, :], xn[:], bn_sb[:, c : c + 1], zh[:], ALU.add, ALU.add)
+            cd = cd_all[:, u, :]
+            nc.scalar.activation(cd[:], pre_all[:, u, :], ACT.Tanh, bias=o_sb[ZERO_FROM[u]][:, 0:1])
+            st[u].update(z=z, zh=zh, cd=cd)
+
+        def gather_state(u, reuse=None):
+            c, h = units[u]
+            hg = keep.tile([P, JH], F32, name=f"hg{u}")[:] if reuse is None else reuse
+            nc.vector.tensor_copy(hg, h_sb[c][:].indirect(part(h)))
+            st[u].update(hg=hg)
+
+        def blend(u, hg, r=None, d=None):
+            n = hg.shape[1]
+            h = units[u][1]
+            span = slice(u, u + n)
+            if d is None:
+                d = work.tile([P, 2, JH], F32, name="d_new", bufs=2)[:, 0:n, :]
+            nc.gpsimd.tensor_tensor(d, cd_all[:, span, :], hg, ALU.subtract)
+            e = work.tile([P, 2, JH], F32, name="e", bufs=2)[:, 0:n, :]
+            nc.gpsimd.tensor_tensor(e, d, z_all[:, span, :], ALU.mult)
+            nc.gpsimd.tensor_tensor(s_all[:, span, :], e, hg, ALU.add)
+            if r is not None:
+                w = wgo_sb[:, h * JH : (h + 1) * JH].unsqueeze(1).broadcast_to([P, n, JH])
+                nc.gpsimd.tensor_tensor(r, s_all[:, span, :], w, ALU.mult)
+                for i in range(n):
+                    st[u + i].update(r=r[:, i, :])
+
+        o_sb = [keep.tile([P, T], F32, name=f"o_sb{c}") for c in range(CHUNKS)]
+
+        def scatter(u):
+            c, h = units[u]
+            if u == len(units) - 1:
+                nc.vector.tensor_tensor(o_sb[c][:].indirect(part(h)), s_all[:, u, :], wgo_sb[:, h * JH : (h + 1) * JH], ALU.mult)
+            else:
+                nc.vector.tensor_copy(o_sb[c][:].indirect(part(h)), st[u]["r"][:])
+            if h == HALVES - 1:
+                nc.sync.dma_start(out[c * P : (c + 1) * P, :], o_sb[c][:])
+
+        nc.vector.memset(o_sb[0][:], 0.0)
+        for c in range(1, CHUNKS):
+            nc.gpsimd.memset(o_sb[c][:], 0.0)
+        vq[0] = gather_table(0)
+        xb0 = keep.tile([P, JH, PACK], BF16, name="xb0", align_bytes=64)
+        xq[0] = quantise_x(0, xb0[:])
+        vq[1] = gather_table(1)
+        hg_first = keep.tile([P, 1, JH], F32, name="hg_first")
+        front(0)
+        gather_state(0, hg_first[:, 0, :])
+        blend(0, hg_first[:], cd_all[:, 0:1, :])
+        front(1)
+        gather_state(1, zh_all[:, 1, :])
+        blend(1, zh_all[:, 1:2, :], cd_all[:, 1:2, :])
+        front(2)
+        front(3)
+        xb1 = pre_all[:, 0:2, :].rearrange("p a j -> p (a j)").bitcast(BF16).rearrange("p (j i) -> p j i", i=PACK)
+        xq[1] = quantise_x(1, xb1)
+        gather_state(4, zh_all[:, 2, :])
+        gather_state(5, zh_all[:, 3, :])
+        gather_state(2, pre_all[:, 0, :])
+        gather_state(3, pre_all[:, 1, :])
+        blend(2, pre_all[:, 0:2, :], cd_all[:, 2:4, :])
+        front(4)
+        front(5)
+        front(6)
+        gather_state(6, pre_all[:, 5, :])
+        front(7)
+        gather_state(7, pre_all[:, 6, :])
+        for u in range(4):
+            scatter(u)
+        blend(4, zh_all[:, 2:4, :], cd_all[:, 2:4, :], s_all[:, 2:4, :])
+        scatter(4)
+        blend(6, pre_all[:, 5:6, :], cd_all[:, 2:3, :], s_all[:, 4:5, :])
+        blend(7, pre_all[:, 6:7, :], None, s_all[:, 6:7, :])
+        for u in range(5, len(units)):
+            scatter(u)

@@ -21,7 +21,6 @@ PACK = 4
 JH = 512
 HALVES = J // JH
 CHUNKS = N // P
-ZERO_FROM = (0, 0, 0, 0, 0, 1, 2, 3)
 
 
 def tile_list_tgn_mgu_kernel(
@@ -31,20 +30,22 @@ def tile_list_tgn_mgu_kernel(
     nc = tc.nc
     with ExitStack() as ctx:
         keep = ctx.enter_context(tc.tile_pool(name="keep", bufs=1))
-        work = ctx.enter_context(tc.tile_pool(name="work", bufs=4))
         psum = ctx.enter_context(tc.psum_pool(name="psum", bufs=1))
 
         offsets = keep.tile([P, J // 16], U16, name="offsets")
         nc.sync.dma_start(offsets[:], offs)
 
-        def load_scale_rows(queue, plane, rows, quadrants):
-            for q in quadrants:
+        def load_scale_rows(queue, plane, rows):
+            for q in range(4):
                 src = rows[0, 4 * q : 4 * q + 4, :].bitcast(I32)
                 queue.dma_start(plane[32 * q : 32 * (q + 1), :], src.unsqueeze(0).broadcast_to([8, *src.shape]))
 
         tab_s = keep.tile([P, T // 4], I32, name="tab_s", align_bytes=64)
-        tab_w = keep.tile([P, T], I32, name="tab_w", align_bytes=64)
-        w_s = keep.tile([P, 4, N // 4], I32, name="w_s", align_bytes=64)
+        tab_w = keep.tile([P, T], I32, name="tab_w", tag="table_then_out", align_bytes=64)
+        uz_s = keep.tile([P, N // 4], I32, name="uz_s", align_bytes=64)
+        wz_s = keep.tile([P, N // 4], I32, name="wz_s", align_bytes=64)
+        un_s = keep.tile([P, N // 4], I32, name="un_s", align_bytes=64)
+        wn_s = keep.tile([P, N // 4], I32, name="wn_s", align_bytes=64)
         wz_w = keep.tile([P, N // 2], I32, name="wz_w", align_bytes=64)
         uz_w = keep.tile([P, N], I32, name="uz_w", align_bytes=64)
         wn_w = keep.tile([P, N // 2], I32, name="wn_w", align_bytes=64)
@@ -56,28 +57,45 @@ def tile_list_tgn_mgu_kernel(
         bz_sb = keep.tile([P, CHUNKS], F32, name="bz_sb")
         bn_sb = keep.tile([P, CHUNKS], F32, name="bn_sb")
 
-        load_scale_rows(nc.sync, tab_s, tab_scales, range(4))
-        load_scale_rows(nc.sync, w_s[:, 1, :], uz_scales, range(2))
+        def load_state(c):
+            for a in range(2):
+                cols = slice(a * (T // 2), (a + 1) * (T // 2))
+                nc.sync.dma_start(h_sb[c][:, cols], hT[c * P : (c + 1) * P, cols])
+
+        def load_bias(tile, vec):
+            with nc.allow_non_contiguous_dma(reason="one bias value to a partition"):
+                nc.scalar.dma_start(tile[:], vec.rearrange("(c p) -> p c", p=P))
+
         nc.sync.dma_start(tab_w[:], tab_words[0].rearrange("p t i -> p (t i)").bitcast(I32))
-        load_scale_rows(nc.sync, w_s[:, 1, :], uz_scales, range(2, 4))
-        load_scale_rows(nc.sync, w_s[:, 0, :], wz_scales, range(4))
         nc.sync.dma_start(x_raw[0][:], x_rows[:, :, 0:JH])
         nc.sync.dma_start(uz_w[:], uz_words[0].rearrange("p n i -> p (n i)").bitcast(I32))
-        load_scale_rows(nc.sync, w_s[:, 3, :], un_scales, range(4))
         nc.sync.dma_start(wz_w[:], wz_words[0].bitcast(I32))
         nc.sync.dma_start(un_w[:], un_words[0].rearrange("p n i -> p (n i)").bitcast(I32))
         nc.sync.dma_start(wn_w[:], wn_words[0].bitcast(I32))
-        with nc.allow_non_contiguous_dma(reason="one bias value to a partition"):
-            nc.sync.dma_start(bz_sb[:], bz.rearrange("(c p) -> p c", p=P))
-            nc.sync.dma_start(bn_sb[:], bn.rearrange("(c p) -> p c", p=P))
-        nc.sync.dma_start(h_sb[0][:], hT[0:P, :])
-        nc.sync.dma_start(h_sb[1][:], hT[P : 2 * P, :])
-        nc.sync.dma_start(x_raw[1][:], x_rows[:, :, JH:J])
+        load_state(0)
+        for a in range(2):
+            nc.sync.dma_start(x_raw[1][:, 2 * a : 2 * a + 2, :], x_rows[:, 2 * a : 2 * a + 2, JH:J])
+        for c in range(1, CHUNKS):
+            load_state(c)
         nc.sync.dma_start(wgo_sb[:], wgo)
-        nc.sync.dma_start(h_sb[2][:], hT[2 * P : 3 * P, :])
-        nc.sync.dma_start(h_sb[3][:], hT[3 * P : 4 * P, :])
-        load_scale_rows(nc.gpsimd, w_s[:, 2, :], wn_scales, range(4))
 
+        load_scale_rows(nc.gpsimd, tab_s, tab_scales)
+        load_scale_rows(nc.scalar, uz_s, uz_scales)
+        load_scale_rows(nc.scalar, wz_s, wz_scales)
+        load_bias(bz_sb, bz)
+        load_scale_rows(nc.scalar, un_s, un_scales)
+        load_scale_rows(nc.scalar, wn_s, wn_scales)
+        load_bias(bn_sb, bn)
+
+        o_sb = [keep.tile([P, T], F32, name=f"o_sb{c}") for c in range(CHUNKS - 1)]
+        nc.vector.memset(o_sb[0][:, 0 : T - 1], 0.0)
+        nc.vector.memset(o_sb[0][:, T - 1 : T], 0.0)
+        nc.vector.memset(o_sb[1][:, 0 : T // 2 - 1], 0.0)
+        nc.vector.memset(o_sb[1][:, T // 2 - 1 : T // 2], 0.0)
+        nc.gpsimd.memset(o_sb[1][:, T // 2 : T], 0.0)
+        nc.gpsimd.memset(o_sb[2][:], 0.0)
+        warm = keep.tile([P, 1], F32, name="warm")
+        nc.scalar.activation(warm[:], o_sb[0][:, 0:1], ACT.Sigmoid)
 
         def part(h):
             return offsets[:, h * (JH // 16) : (h + 1) * (JH // 16)]
@@ -85,16 +103,23 @@ def tile_list_tgn_mgu_kernel(
         def gather_table(h):
             gs = keep.tile([P, JH], U8, name=f"v_s{h}", align_bytes=64)
             gw = keep.tile([P, JH], U32, name=f"v_w{h}", align_bytes=64)
-            nc.vector.tensor_copy(gs[:], tab_s[:].bitcast(U8).indirect(part(h)))
             nc.vector.tensor_copy(gw[:], tab_w[:].bitcast(U32).indirect(part(h)))
+            nc.vector.tensor_copy(gs[:], tab_s[:].bitcast(U8).indirect(part(h)))
             return gw[:].bitcast(FP8X4), gs[:]
 
+        def as_interleaved(words):
+            return words.rearrange("p a j -> p (a j)").bitcast(BF16).rearrange("p (j i) -> p j i", i=PACK)
+
+        def cast_x(h, xb, copy, pieces):
+            width = JH // pieces
+            for a in range(pieces):
+                cols = slice(a * width, (a + 1) * width)
+                copy(
+                    out=xb[:, cols, :].rearrange("p (a b) i -> p a i b", b=4),
+                    in_=x_raw[h][:, :, cols].rearrange("p i (a b) -> p a i b", b=4),
+                )
+
         def quantise_x(h, xb):
-            copy = nc.vector.tensor_copy if h == 0 else nc.scalar.copy
-            copy(
-                out=xb.rearrange("p (a b) i -> p a i b", b=4),
-                in_=x_raw[h][:].rearrange("p i (a b) -> p a i b", b=4),
-            )
             qs = keep.tile([P, JH], U8, name=f"x_s{h}", align_bytes=64)
             qw = keep.tile([P, JH], U32, name=f"x_w{h}", align_bytes=64)
             nc.vector.quantize_mx(out=qw[:].bitcast(FP8X4), scales=qs[:], in_=xb.rearrange("p j i -> p (j i)"))
@@ -106,104 +131,127 @@ def tile_list_tgn_mgu_kernel(
         def fp8_cols(words, c):
             return words[:, P * c : P * (c + 1)].bitcast(FP8X4)
 
-        def scale_cols(slot, c):
-            return w_s[:, slot, 32 * c : 32 * (c + 1)].bitcast(U8)
+        def scale_cols(plane, c):
+            return plane[:, 32 * c : 32 * (c + 1)].bitcast(U8)
 
-        bank = {(role, i): psum.tile([P, JH], F32, name=f"{role}{i}") for role in ("sz", "hn", "xn") for i in range(2)}
+        sz_bank = [psum.tile([P, JH], F32, name=f"sz{i}") for i in range(2)]
+        hn_bank = [psum.tile([P, JH], F32, name=f"hn{i}") for i in range(3)]
+        xn_bank = [psum.tile([P, JH], F32, name=f"xn{i}") for i in range(3)]
 
         units = [(c, h) for h in range(HALVES) for c in range(CHUNKS)]
-        st = [dict() for u in units]
+        n_units = len(units)
         xq, vq = {}, {}
-        pre_all = keep.tile([P, len(units), JH], F32, name="pre_all", align_bytes=64)
-        z_all = keep.tile([P, len(units), JH], F32, name="z_all")
-        cd_all = keep.tile([P, len(units), JH], F32, name="cd_all")
-        s_all = keep.tile([P, len(units), JH], F32, name="s_all")
-        zh_all = keep.tile([P, len(units), JH], F32, name="zh_all")
+        z_all = keep.tile([P, n_units, JH], F32, name="z_all")
+        zc_all = keep.tile([P, n_units, JH], F32, name="zc_all")
+        zh_all = keep.tile([P, n_units, JH], F32, name="zh_all")
+        cd_all = keep.tile([P, n_units, JH], F32, name="cd_all")
+        pre_first = keep.tile([P, 2, JH], F32, name="pre_first", align_bytes=64)
+        pre_rest = keep.tile([P, n_units - 2, JH], F32, name="pre_rest")
+        zc_first = keep.tile([P, JH], F32, name="zc_first")
 
         def front(u):
             c, h = units[u]
             (xw, xs), (vw, vs) = xq[h], vq[h]
-            sz, hn, xn = bank["sz", u % 2], bank["hn", u % 2], bank["xn", u % 2]
-            nc.tensor.matmul_mx(out=sz[:], lhsT=fp8_cols(uz_w, c), lhsT_scale=scale_cols(1, c), rhs=vw, rhs_scale=vs, start=True, stop=False)
-            nc.tensor.matmul_mx(out=sz[:], lhsT=fp4_cols(wz_w, c), lhsT_scale=scale_cols(0, c), rhs=xw, rhs_scale=xs, start=False, stop=True)
-            nc.tensor.matmul_mx(out=hn[:], lhsT=fp8_cols(un_w, c), lhsT_scale=scale_cols(3, c), rhs=vw, rhs_scale=vs, start=True, stop=True)
-            nc.tensor.matmul_mx(out=xn[:], lhsT=fp4_cols(wn_w, c), lhsT_scale=scale_cols(2, c), rhs=xw, rhs_scale=xs, start=True, stop=True)
-            z = z_all[:, u, :]
-            nc.scalar.activation(z[:], sz[:], ACT.Sigmoid, bias=bz_sb[:, c : c + 1])
-            zh = zh_all[:, u, :]
-            nc.vector.tensor_tensor(zh[:], hn[:], z[:], ALU.mult)
-            nc.vector.scalar_tensor_tensor(pre_all[:, u, :], xn[:], bn_sb[:, c : c + 1], zh[:], ALU.add, ALU.add)
-            cd = cd_all[:, u, :]
-            nc.scalar.activation(cd[:], pre_all[:, u, :], ACT.Tanh, bias=o_sb[ZERO_FROM[u]][:, 0:1])
-            st[u].update(z=z, zh=zh, cd=cd)
+            sz, hn, xn = sz_bank[u % 2], hn_bank[u % 3], xn_bank[u % 3]
+            nc.tensor.matmul_mx(out=sz[:], lhsT=fp8_cols(uz_w, c), lhsT_scale=scale_cols(uz_s, c), rhs=vw, rhs_scale=vs, start=True, stop=False)
+            nc.tensor.matmul_mx(out=sz[:], lhsT=fp4_cols(wz_w, c), lhsT_scale=scale_cols(wz_s, c), rhs=xw, rhs_scale=xs, start=False, stop=True)
+            nc.tensor.matmul_mx(out=hn[:], lhsT=fp8_cols(un_w, c), lhsT_scale=scale_cols(un_s, c), rhs=vw, rhs_scale=vs, start=True, stop=True)
+            nc.tensor.matmul_mx(out=xn[:], lhsT=fp4_cols(wn_w, c), lhsT_scale=scale_cols(wn_s, c), rhs=xw, rhs_scale=xs, start=True, stop=True)
+            pre = pre_first[:, u, :] if u < 2 else pre_rest[:, u - 2, :]
+            nc.scalar.activation(z_all[:, u, :], sz[:], ACT.Sigmoid, bias=bz_sb[:, c : c + 1])
+            nc.vector.tensor_tensor(zh_all[:, u, :], hn[:], z_all[:, u, :], ALU.mult)
+            nc.vector.tensor_tensor(pre, xn[:], zh_all[:, u, :], ALU.add)
+            nc.scalar.activation(cd_all[:, u, :], pre, ACT.Tanh, bias=bn_sb[:, c : c + 1])
 
-        def gather_state(u, reuse=None):
+        def one_minus_z(u, dst):
+            nc.scalar.activation(dst, z_all[:, u, :], ACT.Copy, bias=1.0, scale=-1.0)
+
+        def picked_state(u):
             c, h = units[u]
-            hg = keep.tile([P, JH], F32, name=f"hg{u}")[:] if reuse is None else reuse
-            nc.vector.tensor_copy(hg, h_sb[c][:].indirect(part(h)))
-            st[u].update(hg=hg)
+            return h_sb[c][:].indirect(part(h))
 
-        def blend(u, hg, r=None, d=None):
-            n = hg.shape[1]
-            h = units[u][1]
-            span = slice(u, u + n)
-            if d is None:
-                d = work.tile([P, 2, JH], F32, name="d_new", bufs=2)[:, 0:n, :]
-            nc.gpsimd.tensor_tensor(d, cd_all[:, span, :], hg, ALU.subtract)
-            e = work.tile([P, 2, JH], F32, name="e", bufs=2)[:, 0:n, :]
-            nc.gpsimd.tensor_tensor(e, d, z_all[:, span, :], ALU.mult)
-            nc.gpsimd.tensor_tensor(s_all[:, span, :], e, hg, ALU.add)
-            if r is not None:
-                w = wgo_sb[:, h * JH : (h + 1) * JH].unsqueeze(1).broadcast_to([P, n, JH])
-                nc.gpsimd.tensor_tensor(r, s_all[:, span, :], w, ALU.mult)
-                for i in range(n):
-                    st[u + i].update(r=r[:, i, :])
+        def gather_state(u, dst):
+            nc.vector.tensor_copy(dst, picked_state(u))
 
-        o_sb = [keep.tile([P, T], F32, name=f"o_sb{c}") for c in range(CHUNKS)]
+        def mul(dst, a, b):
+            nc.gpsimd.tensor_tensor(dst, a, b, ALU.mult)
+
+        def add(dst, a, b):
+            nc.gpsimd.tensor_tensor(dst, a, b, ALU.add)
+
+        def weights(h, n):
+            return wgo_sb[:, h * JH : (h + 1) * JH].unsqueeze(1).broadcast_to([P, n, JH])
 
         def scatter(u):
             c, h = units[u]
-            if u == len(units) - 1:
-                nc.vector.tensor_tensor(o_sb[c][:].indirect(part(h)), s_all[:, u, :], wgo_sb[:, h * JH : (h + 1) * JH], ALU.mult)
+            if u == n_units - 1:
+                nc.vector.tensor_tensor(o_sb[c][:].indirect(part(h)), cd_all[:, 0, :], wgo_sb[:, h * JH : (h + 1) * JH], ALU.mult)
             else:
-                nc.vector.tensor_copy(o_sb[c][:].indirect(part(h)), st[u]["r"][:])
+                nc.vector.tensor_copy(o_sb[c][:].indirect(part(h)), z_all[:, u, :])
             if h == HALVES - 1:
                 nc.sync.dma_start(out[c * P : (c + 1) * P, :], o_sb[c][:])
 
-        nc.vector.memset(o_sb[0][:], 0.0)
-        for c in range(1, CHUNKS):
-            nc.gpsimd.memset(o_sb[c][:], 0.0)
+        z, zc, zh, cd = z_all, zc_all, zh_all, cd_all
         vq[0] = gather_table(0)
-        xb0 = keep.tile([P, JH, PACK], BF16, name="xb0", align_bytes=64)
-        xq[0] = quantise_x(0, xb0[:])
+        x_first = keep.tile([P, 2, JH], F32, name="x_first", align_bytes=64)
+        xb0 = as_interleaved(x_first[:])
+        cast_x(0, xb0, nc.vector.tensor_copy, 1)
+        xq[0] = quantise_x(0, xb0)
         vq[1] = gather_table(1)
-        hg_first = keep.tile([P, 1, JH], F32, name="hg_first")
+        o_last = keep.tile([P, T], F32, name="o_last", tag="table_then_out", align_bytes=64)
+        o_sb.append(o_last)
+        nc.gpsimd.memset(o_last[:], 0.0)
+
         front(0)
-        gather_state(0, hg_first[:, 0, :])
-        blend(0, hg_first[:], cd_all[:, 0:1, :])
+        one_minus_z(0, zc_first[:])
+        nc.vector.tensor_tensor(zc[:, 0, :], picked_state(0), zc_first[:], ALU.mult)
         front(1)
-        gather_state(1, zh_all[:, 1, :])
-        blend(1, zh_all[:, 1:2, :], cd_all[:, 1:2, :])
+        gather_state(4, zh[:, 1, :])
         front(2)
+        gather_state(1, zh[:, 2, :])
         front(3)
-        xb1 = pre_all[:, 0:2, :].rearrange("p a j -> p (a j)").bitcast(BF16).rearrange("p (j i) -> p j i", i=PACK)
+        gather_state(5, zh[:, 3, :])
+        one_minus_z(1, zc[:, 1, :])
+        xb1 = as_interleaved(pre_first[:])
+        cast_x(1, xb1, nc.scalar.copy, 2)
         xq[1] = quantise_x(1, xb1)
-        gather_state(4, zh_all[:, 2, :])
-        gather_state(5, zh_all[:, 3, :])
-        gather_state(2, pre_all[:, 0, :])
-        gather_state(3, pre_all[:, 1, :])
-        blend(2, pre_all[:, 0:2, :], cd_all[:, 2:4, :])
+        gather_state(2, pre_first[:, 0, :])
+        gather_state(3, pre_first[:, 1, :])
         front(4)
+        gather_state(6, zh[:, 4, :])
         front(5)
+        gather_state(7, zh[:, 5, :])
         front(6)
-        gather_state(6, pre_all[:, 5, :])
         front(7)
-        gather_state(7, pre_all[:, 6, :])
-        for u in range(4):
-            scatter(u)
-        blend(4, zh_all[:, 2:4, :], cd_all[:, 2:4, :], s_all[:, 2:4, :])
+        for u in range(2, n_units):
+            one_minus_z(u, zc[:, u, :])
+
+        mul(cd[:, 0, :], z[:, 0, :], cd[:, 0, :])
+        mul(cd[:, 1, :], z[:, 1, :], cd[:, 1, :])
+        add(cd[:, 0, :], zc[:, 0, :], cd[:, 0, :])
+        mul(cd[:, 2:4, :], z[:, 2:4, :], cd[:, 2:4, :])
+        mul(zc[:, 1, :], zc[:, 1, :], zh[:, 2, :])
+        add(cd[:, 1, :], zc[:, 1, :], cd[:, 1, :])
+        mul(z[:, 0:2, :], cd[:, 0:2, :], weights(0, 2))
+        scatter(0)
+        scatter(1)
+        mul(cd[:, 0:2, :], zc[:, 2:4, :], pre_first[:])
+        add(cd[:, 2:4, :], cd[:, 0:2, :], cd[:, 2:4, :])
+        mul(z[:, 2:4, :], cd[:, 2:4, :], weights(0, 2))
+        scatter(2)
+        scatter(3)
+        mul(cd[:, 0:2, :], z[:, 4:6, :], cd[:, 4:6, :])
+        mul(cd[:, 2:4, :], zc[:, 4:6, :], zh[:, 1:4:2, :])
+        add(cd[:, 0:2, :], cd[:, 0:2, :], cd[:, 2:4, :])
+        mul(z[:, 4:6, :], cd[:, 0:2, :], weights(1, 2))
         scatter(4)
-        blend(6, pre_all[:, 5:6, :], cd_all[:, 2:3, :], s_all[:, 4:5, :])
-        blend(7, pre_all[:, 6:7, :], None, s_all[:, 6:7, :])
-        for u in range(5, len(units)):
-            scatter(u)
+        scatter(5)
+        mul(cd[:, 0, :], zc[:, 6, :], zh[:, 4, :])
+        mul(cd[:, 1, :], z[:, 6, :], cd[:, 6, :])
+        add(cd[:, 0, :], cd[:, 0, :], cd[:, 1, :])
+        mul(z[:, 6, :], cd[:, 0, :], wgo_sb[:, JH:J])
+        scatter(6)
+        mul(cd[:, 0, :], zc[:, 7, :], zh[:, 5, :])
+        mul(cd[:, 1, :], z[:, 7, :], cd[:, 7, :])
+        add(cd[:, 0, :], cd[:, 0, :], cd[:, 1, :])
+        scatter(7)

@@ -30,22 +30,20 @@ def tile_list_tgn_mgu_kernel(
     nc = tc.nc
     with ExitStack() as ctx:
         keep = ctx.enter_context(tc.tile_pool(name="keep", bufs=1))
+        reuse = ctx.enter_context(tc.tile_pool(name="reuse", bufs=1))
         psum = ctx.enter_context(tc.psum_pool(name="psum", bufs=1))
 
         offsets = keep.tile([P, J // 16], U16, name="offsets")
         nc.sync.dma_start(offsets[:], offs)
 
-        def load_scale_rows(queue, plane, rows):
-            for q in range(4):
-                src = rows[0, 4 * q : 4 * q + 4, :].bitcast(I32)
-                queue.dma_start(plane[32 * q : 32 * (q + 1), :], src.unsqueeze(0).broadcast_to([8, *src.shape]))
+        def load_scale_rows(queue, plane, rows, quadrants):
+            for q in quadrants:
+                queue.dma_start(plane[32 * q : 32 * q + 4, :], rows[0, 4 * q : 4 * q + 4, :].bitcast(I32))
 
-        tab_s = keep.tile([P, T // 4], I32, name="tab_s", align_bytes=64)
-        tab_w = keep.tile([P, T], I32, name="tab_w", tag="table_then_out", align_bytes=64)
-        uz_s = keep.tile([P, N // 4], I32, name="uz_s", align_bytes=64)
-        wz_s = keep.tile([P, N // 4], I32, name="wz_s", align_bytes=64)
-        un_s = keep.tile([P, N // 4], I32, name="un_s", align_bytes=64)
-        wn_s = keep.tile([P, N // 4], I32, name="wn_s", align_bytes=64)
+        tab_s = keep.tile([P, T // 4 + 1], I32, name="tab_s", align_bytes=64)
+        tab_w = keep.tile([P, T], I32, name="tab_w", align_bytes=64)
+        w_s = keep.tile([P, N + 1], I32, name="w_s", align_bytes=64)
+        uz_s, wz_s, un_s, wn_s = [w_s[:, a * (N // 4) : (a + 1) * (N // 4)] for a in range(4)]
         wz_w = keep.tile([P, N // 2], I32, name="wz_w", align_bytes=64)
         uz_w = keep.tile([P, N], I32, name="uz_w", align_bytes=64)
         wn_w = keep.tile([P, N // 2], I32, name="wn_w", align_bytes=64)
@@ -58,53 +56,49 @@ def tile_list_tgn_mgu_kernel(
         bn_sb = keep.tile([P, CHUNKS], F32, name="bn_sb")
 
         def load_state(c):
-            for a in range(2):
-                cols = slice(a * (T // 2), (a + 1) * (T // 2))
-                nc.sync.dma_start(h_sb[c][:, cols], hT[c * P : (c + 1) * P, cols])
+            nc.sync.dma_start(h_sb[c][:], hT[c * P : (c + 1) * P, :])
 
         def load_bias(tile, vec):
             with nc.allow_non_contiguous_dma(reason="one bias value to a partition"):
-                nc.scalar.dma_start(tile[:], vec.rearrange("(c p) -> p c", p=P))
+                nc.sync.dma_start(tile[:], vec.rearrange("(c p) -> p c", p=P))
+
+        o_sb = [keep.tile([P, T], F32, name=f"o_sb{c}") for c in range(2)]
+        nc.vector.memset(tab_s[:], 0)
+        nc.vector.memset(w_s[:], 0)
+        nc.vector.memset(o_sb[0][:, 0 : T - 1], 0.0)
+        nc.vector.memset(o_sb[0][:, T - 1 : T], 0.0)
+        nc.gpsimd.memset(o_sb[1][:], 0.0)
 
         nc.sync.dma_start(tab_w[:], tab_words[0].rearrange("p t i -> p (t i)").bitcast(I32))
+        load_scale_rows(nc.sync, tab_s[:, 0 : T // 4], tab_scales, range(4))
+        load_scale_rows(nc.sync, uz_s, uz_scales, range(2))
         nc.sync.dma_start(x_raw[0][:], x_rows[:, :, 0:JH])
+        load_scale_rows(nc.sync, uz_s, uz_scales, range(2, 4))
+        load_scale_rows(nc.sync, wz_s, wz_scales, range(2))
         nc.sync.dma_start(uz_w[:], uz_words[0].rearrange("p n i -> p (n i)").bitcast(I32))
         nc.sync.dma_start(wz_w[:], wz_words[0].bitcast(I32))
         nc.sync.dma_start(un_w[:], un_words[0].rearrange("p n i -> p (n i)").bitcast(I32))
+        load_scale_rows(nc.sync, wz_s, wz_scales, range(2, 4))
+        load_bias(bz_sb, bz)
+        load_scale_rows(nc.sync, un_s, un_scales, range(4))
         nc.sync.dma_start(wn_w[:], wn_words[0].bitcast(I32))
-        load_state(0)
-        for a in range(2):
-            nc.sync.dma_start(x_raw[1][:, 2 * a : 2 * a + 2, :], x_rows[:, 2 * a : 2 * a + 2, JH:J])
-        for c in range(1, CHUNKS):
+        load_bias(bn_sb, bn)
+        for c in range(CHUNKS - 1):
             load_state(c)
         nc.sync.dma_start(wgo_sb[:], wgo)
+        nc.sync.dma_start(x_raw[1][:], x_rows[:, :, JH:J])
+        load_state(CHUNKS - 1)
+        load_scale_rows(nc.gpsimd, wn_s, wn_scales, range(4))
 
-        load_scale_rows(nc.gpsimd, tab_s, tab_scales)
-        load_scale_rows(nc.scalar, uz_s, uz_scales)
-        load_scale_rows(nc.scalar, wz_s, wz_scales)
-        load_bias(bz_sb, bz)
-        load_scale_rows(nc.scalar, un_s, un_scales)
-        load_scale_rows(nc.scalar, wn_s, wn_scales)
-        load_bias(bn_sb, bn)
-
-        o_sb = [keep.tile([P, T], F32, name=f"o_sb{c}") for c in range(CHUNKS - 1)]
-        nc.vector.memset(o_sb[0][:, 0 : T - 1], 0.0)
-        nc.vector.memset(o_sb[0][:, T - 1 : T], 0.0)
-        nc.vector.memset(o_sb[1][:, 0 : T // 2 - 1], 0.0)
-        nc.vector.memset(o_sb[1][:, T // 2 - 1 : T // 2], 0.0)
-        nc.gpsimd.memset(o_sb[1][:, T // 2 : T], 0.0)
-        nc.gpsimd.memset(o_sb[2][:], 0.0)
         warm = keep.tile([P, 1], F32, name="warm")
         nc.scalar.activation(warm[:], o_sb[0][:, 0:1], ACT.Sigmoid)
 
         def part(h):
             return offsets[:, h * (JH // 16) : (h + 1) * (JH // 16)]
 
-        def gather_table(h):
-            gs = keep.tile([P, JH], U8, name=f"v_s{h}", align_bytes=64)
-            gw = keep.tile([P, JH], U32, name=f"v_w{h}", align_bytes=64)
+        def gather_table(h, gw, gs):
             nc.vector.tensor_copy(gw[:], tab_w[:].bitcast(U32).indirect(part(h)))
-            nc.vector.tensor_copy(gs[:], tab_s[:].bitcast(U8).indirect(part(h)))
+            nc.vector.tensor_copy(gs[:], tab_s[:, 0 : T // 4].bitcast(U8).indirect(part(h)))
             return gw[:].bitcast(FP8X4), gs[:]
 
         def as_interleaved(words):
@@ -119,9 +113,8 @@ def tile_list_tgn_mgu_kernel(
                     in_=x_raw[h][:, :, cols].rearrange("p i (a b) -> p a i b", b=4),
                 )
 
-        def quantise_x(h, xb):
+        def quantise_x(h, xb, qw):
             qs = keep.tile([P, JH], U8, name=f"x_s{h}", align_bytes=64)
-            qw = keep.tile([P, JH], U32, name=f"x_w{h}", align_bytes=64)
             nc.vector.quantize_mx(out=qw[:].bitcast(FP8X4), scales=qs[:], in_=xb.rearrange("p j i -> p (j i)"))
             return qw[:].bitcast(FP8X4), qs[:]
 
@@ -138,40 +131,37 @@ def tile_list_tgn_mgu_kernel(
         hn_bank = [psum.tile([P, JH], F32, name=f"hn{i}") for i in range(3)]
         xn_bank = [psum.tile([P, JH], F32, name=f"xn{i}") for i in range(3)]
 
-        units = [(c, h) for h in range(HALVES) for c in range(CHUNKS)]
+        units = [(0, 0), (1, 0), (2, 0), (0, 1), (1, 1), (2, 1), (3, 0), (3, 1)]
         n_units = len(units)
         xq, vq = {}, {}
         z_all = keep.tile([P, n_units, JH], F32, name="z_all")
         zc_all = keep.tile([P, n_units, JH], F32, name="zc_all")
-        zh_all = keep.tile([P, n_units, JH], F32, name="zh_all")
         cd_all = keep.tile([P, n_units, JH], F32, name="cd_all")
-        pre_first = keep.tile([P, 2, JH], F32, name="pre_first", align_bytes=64)
-        pre_rest = keep.tile([P, n_units - 2, JH], F32, name="pre_rest")
-        zc_first = keep.tile([P, JH], F32, name="zc_first")
+        scratch = keep.tile([P, 2 * n_units, JH], F32, name="scratch")
+        zh_all, pre_all = scratch[:, 0:n_units, :], scratch[:, n_units:, :]
+        pre_pair = keep.tile([P, 2, JH], F32, name="pre_pair", align_bytes=64)
+        front_order = [0, 1, 2, 6, 3, 4, 5, 7]
+        zero_from = {4: 2, 7: 1}
 
         def front(u):
             c, h = units[u]
+            turn = front_order.index(u)
             (xw, xs), (vw, vs) = xq[h], vq[h]
-            sz, hn, xn = sz_bank[u % 2], hn_bank[u % 3], xn_bank[u % 3]
+            sz, hn, xn = sz_bank[turn % 2], hn_bank[turn % 3], xn_bank[turn % 3]
             nc.tensor.matmul_mx(out=sz[:], lhsT=fp8_cols(uz_w, c), lhsT_scale=scale_cols(uz_s, c), rhs=vw, rhs_scale=vs, start=True, stop=False)
             nc.tensor.matmul_mx(out=sz[:], lhsT=fp4_cols(wz_w, c), lhsT_scale=scale_cols(wz_s, c), rhs=xw, rhs_scale=xs, start=False, stop=True)
             nc.tensor.matmul_mx(out=hn[:], lhsT=fp8_cols(un_w, c), lhsT_scale=scale_cols(un_s, c), rhs=vw, rhs_scale=vs, start=True, stop=True)
             nc.tensor.matmul_mx(out=xn[:], lhsT=fp4_cols(wn_w, c), lhsT_scale=scale_cols(wn_s, c), rhs=xw, rhs_scale=xs, start=True, stop=True)
-            pre = pre_first[:, u, :] if u < 2 else pre_rest[:, u - 2, :]
+            pre = pre_pair[:, u - 1, :] if u in (1, 2) else pre_all[:, u, :]
             nc.scalar.activation(z_all[:, u, :], sz[:], ACT.Sigmoid, bias=bz_sb[:, c : c + 1])
             nc.vector.tensor_tensor(zh_all[:, u, :], hn[:], z_all[:, u, :], ALU.mult)
-            nc.vector.tensor_tensor(pre, xn[:], zh_all[:, u, :], ALU.add)
-            nc.scalar.activation(cd_all[:, u, :], pre, ACT.Tanh, bias=bn_sb[:, c : c + 1])
-
-        def one_minus_z(u, dst):
-            nc.scalar.activation(dst, z_all[:, u, :], ACT.Copy, bias=1.0, scale=-1.0)
-
-        def picked_state(u):
-            c, h = units[u]
-            return h_sb[c][:].indirect(part(h))
+            nc.vector.scalar_tensor_tensor(pre, xn[:], bn_sb[:, c : c + 1], zh_all[:, u, :], ALU.add, ALU.add)
+            nc.scalar.activation(cd_all[:, u, :], pre, ACT.Tanh, bias=o_sb[zero_from.get(u, 0)][:, 0:1])
+            nc.scalar.activation(zc_all[:, u, :], z_all[:, u, :], ACT.Copy, bias=1.0, scale=-1.0)
 
         def gather_state(u, dst):
-            nc.vector.tensor_copy(dst, picked_state(u))
+            c, h = units[u]
+            nc.vector.tensor_copy(dst, h_sb[c][:].indirect(part(h)))
 
         def mul(dst, a, b):
             nc.gpsimd.tensor_tensor(dst, a, b, ALU.mult)
@@ -185,73 +175,73 @@ def tile_list_tgn_mgu_kernel(
         def scatter(u):
             c, h = units[u]
             if u == n_units - 1:
-                nc.vector.tensor_tensor(o_sb[c][:].indirect(part(h)), cd_all[:, 0, :], wgo_sb[:, h * JH : (h + 1) * JH], ALU.mult)
+                nc.vector.tensor_tensor(o_sb[c][:].indirect(part(h)), cd_all[:, 1, :], wgo_sb[:, h * JH : (h + 1) * JH], ALU.mult)
             else:
                 nc.vector.tensor_copy(o_sb[c][:].indirect(part(h)), z_all[:, u, :])
             if h == HALVES - 1:
                 nc.sync.dma_start(out[c * P : (c + 1) * P, :], o_sb[c][:])
 
         z, zc, zh, cd = z_all, zc_all, zh_all, cd_all
-        vq[0] = gather_table(0)
-        x_first = keep.tile([P, 2, JH], F32, name="x_first", align_bytes=64)
+        v_w0 = keep.tile([P, JH], U32, name="v_w0", align_bytes=64)
+        v_s0 = keep.tile([P, JH], U8, name="v_s0", align_bytes=64)
+        vq[0] = gather_table(0, v_w0, v_s0)
+        x_first = reuse.tile([P, 2, JH], F32, name="x_first", align_bytes=64, offset=0)
         xb0 = as_interleaved(x_first[:])
         cast_x(0, xb0, nc.vector.tensor_copy, 1)
-        xq[0] = quantise_x(0, xb0)
-        vq[1] = gather_table(1)
-        o_last = keep.tile([P, T], F32, name="o_last", tag="table_then_out", align_bytes=64)
-        o_sb.append(o_last)
-        nc.gpsimd.memset(o_last[:], 0.0)
+        x_w0 = keep.tile([P, JH], U32, name="x_w0", align_bytes=64)
+        xq[0] = quantise_x(0, xb0, x_w0)
+        v_w1 = reuse.tile([P, JH], U32, name="v_w1", align_bytes=64, offset=0)
+        v_s1 = reuse.tile([P, JH], U8, name="v_s1", align_bytes=64, offset=4 * JH)
+        vq[1] = gather_table(1, v_w1, v_s1)
+        o_third = reuse.tile([P, T], F32, name="o_third", align_bytes=64, offset=5 * JH)
+        nc.gpsimd.memset(o_third[:], 0.0)
+        o_sb.extend([o_third, o_sb[0]])
 
         front(0)
-        one_minus_z(0, zc_first[:])
-        nc.vector.tensor_tensor(zc[:, 0, :], picked_state(0), zc_first[:], ALU.mult)
+        gather_state(0, zh[:, 0, :])
         front(1)
-        gather_state(4, zh[:, 1, :])
         front(2)
         gather_state(1, zh[:, 2, :])
-        front(3)
-        gather_state(5, zh[:, 3, :])
-        one_minus_z(1, zc[:, 1, :])
-        xb1 = as_interleaved(pre_first[:])
-        cast_x(1, xb1, nc.scalar.copy, 2)
-        xq[1] = quantise_x(1, xb1)
-        gather_state(2, pre_first[:, 0, :])
-        gather_state(3, pre_first[:, 1, :])
-        front(4)
-        gather_state(6, zh[:, 4, :])
-        front(5)
-        gather_state(7, zh[:, 5, :])
         front(6)
+        gather_state(2, zh[:, 6, :])
+        gather_state(3, zh[:, 1, :])
+        gather_state(4, pre_all[:, 6, :])
+        xb1 = as_interleaved(pre_pair[:])
+        cast_x(1, xb1, nc.scalar.copy, 2)
+        x_w1 = keep.tile([P, JH], U32, name="x_w1", align_bytes=64)
+        xq[1] = quantise_x(1, xb1, x_w1)
+        front(3)
+        front(4)
+        front(5)
         front(7)
-        for u in range(2, n_units):
-            one_minus_z(u, zc[:, u, :])
+        gather_state(5, pre_pair[:, 0, :])
+        gather_state(6, pre_pair[:, 1, :])
+        gather_state(7, zh[:, 3, :])
 
-        mul(cd[:, 0, :], z[:, 0, :], cd[:, 0, :])
-        mul(cd[:, 1, :], z[:, 1, :], cd[:, 1, :])
-        add(cd[:, 0, :], zc[:, 0, :], cd[:, 0, :])
-        mul(cd[:, 2:4, :], z[:, 2:4, :], cd[:, 2:4, :])
-        mul(zc[:, 1, :], zc[:, 1, :], zh[:, 2, :])
-        add(cd[:, 1, :], zc[:, 1, :], cd[:, 1, :])
+        def blend_in_place(u, state):
+            mul(cd[:, u, :], z[:, u, :], cd[:, u, :])
+            mul(zc[:, u, :], zc[:, u, :], state)
+            add(cd[:, u, :], zc[:, u, :], cd[:, u, :])
+
+        blend_in_place(0, zh[:, 0, :])
+        blend_in_place(1, zh[:, 2, :])
         mul(z[:, 0:2, :], cd[:, 0:2, :], weights(0, 2))
         scatter(0)
         scatter(1)
-        mul(cd[:, 0:2, :], zc[:, 2:4, :], pre_first[:])
-        add(cd[:, 2:4, :], cd[:, 0:2, :], cd[:, 2:4, :])
-        mul(z[:, 2:4, :], cd[:, 2:4, :], weights(0, 2))
+        blend_in_place(2, zh[:, 6, :])
+        mul(z[:, 2, :], cd[:, 2, :], wgo_sb[:, 0:JH])
         scatter(2)
+        mul(cd[:, 1:3, :], z[:, 3:5, :], cd[:, 3:5, :])
+        mul(cd[:, 3:5, :], zc[:, 3:5, :], scratch[:, 1 : n_units + 7 : n_units + 5, :])
+        add(cd[:, 1:3, :], cd[:, 1:3, :], cd[:, 3:5, :])
+        mul(z[:, 3:5, :], cd[:, 1:3, :], weights(1, 2))
         scatter(3)
-        mul(cd[:, 0:2, :], z[:, 4:6, :], cd[:, 4:6, :])
-        mul(cd[:, 2:4, :], zc[:, 4:6, :], zh[:, 1:4:2, :])
-        add(cd[:, 0:2, :], cd[:, 0:2, :], cd[:, 2:4, :])
-        mul(z[:, 4:6, :], cd[:, 0:2, :], weights(1, 2))
         scatter(4)
-        scatter(5)
-        mul(cd[:, 0, :], zc[:, 6, :], zh[:, 4, :])
-        mul(cd[:, 1, :], z[:, 6, :], cd[:, 6, :])
-        add(cd[:, 0, :], cd[:, 0, :], cd[:, 1, :])
-        mul(z[:, 6, :], cd[:, 0, :], wgo_sb[:, JH:J])
-        scatter(6)
-        mul(cd[:, 0, :], zc[:, 7, :], zh[:, 5, :])
-        mul(cd[:, 1, :], z[:, 7, :], cd[:, 7, :])
-        add(cd[:, 0, :], cd[:, 0, :], cd[:, 1, :])
-        scatter(7)
+        for u, state in ((5, pre_pair[:, 0, :]), (6, pre_pair[:, 1, :]), (7, zh[:, 3, :])):
+            h = units[u][1]
+            mul(cd[:, 2, :], z[:, u, :], cd[:, u, :])
+            mul(cd[:, 1, :], zc[:, u, :], state)
+            add(cd[:, 1, :], cd[:, 1, :], cd[:, 2, :])
+            if u < n_units - 1:
+                mul(z[:, u, :], cd[:, 1, :], wgo_sb[:, h * JH : (h + 1) * JH])
+            scatter(u)

@@ -1,6 +1,7 @@
 from contextlib import ExitStack
 
 import concourse.mybir as mybir
+from concourse.masks import make_identity
 
 K, M, N, T, J = 512, 512, 512, 2048, 1024
 FLOPS = 2 * (2 * K + 2 * M) * N * J
@@ -21,6 +22,9 @@ PACK = 4
 JH = 512
 HALVES = J // JH
 CHUNKS = N // P
+CAST_SPLIT = 336
+PRODUCT_ON_GPSIMD = (7,)
+SUM_ON_GPSIMD = (5, 6, 7)
 
 
 def tile_list_tgn_mgu_kernel(
@@ -52,6 +56,7 @@ def tile_list_tgn_mgu_kernel(
         x_raw = [keep.tile([P, PACK, JH], F32, name=f"x_raw{h}") for h in range(HALVES)]
         h_sb = [keep.tile([P, T], F32, name=f"h_sb{c}") for c in range(CHUNKS)]
         wgo_sb = keep.tile([P, J], F32, name="wgo_sb")
+        wgo_rows = keep.tile([P, P], F32, name="wgo_rows")
         bz_sb = keep.tile([P, CHUNKS], F32, name="bz_sb")
         bn_sb = keep.tile([P, CHUNKS], F32, name="bn_sb")
 
@@ -83,13 +88,17 @@ def tile_list_tgn_mgu_kernel(
         load_scale_rows(nc.sync, un_s, un_scales, range(4))
         nc.sync.dma_start(wn_w[:], wn_words[0].bitcast(I32))
         load_bias(bn_sb, bn)
-        for c in range(CHUNKS - 1):
-            load_state(c)
-        nc.sync.dma_start(wgo_sb[:], wgo)
+        load_state(0)
+        load_state(1)
+        load_state(2)
         nc.sync.dma_start(x_raw[1][:], x_rows[:, :, JH:J])
+        nc.sync.dma_start(wgo_sb[:], wgo)
         load_state(CHUNKS - 1)
+        nc.sync.dma_start(wgo_rows[:], wgo[0 : P * P // J, :].rearrange("a (b j) -> (a b) j", j=P))
         load_scale_rows(nc.gpsimd, wn_s, wn_scales, range(4))
 
+        ident = keep.tile([P, P], F32, name="ident")
+        make_identity(nc, ident[:])
         warm = keep.tile([P, 1], F32, name="warm")
         nc.scalar.activation(warm[:], o_sb[0][:, 0:1], ACT.Sigmoid)
 
@@ -104,14 +113,11 @@ def tile_list_tgn_mgu_kernel(
         def as_interleaved(words):
             return words.rearrange("p a j -> p (a j)").bitcast(BF16).rearrange("p (j i) -> p j i", i=PACK)
 
-        def cast_x(h, xb, copy, pieces):
-            width = JH // pieces
-            for a in range(pieces):
-                cols = slice(a * width, (a + 1) * width)
-                copy(
-                    out=xb[:, cols, :].rearrange("p (a b) i -> p a i b", b=4),
-                    in_=x_raw[h][:, :, cols].rearrange("p i (a b) -> p a i b", b=4),
-                )
+        def cast_x(h, xb, copy, cols):
+            copy(
+                out=xb[:, cols, :].rearrange("p (a b) i -> p a i b", b=4),
+                in_=x_raw[h][:, :, cols].rearrange("p i (a b) -> p a i b", b=4),
+            )
 
         def quantise_x(h, xb, qw):
             qs = keep.tile([P, JH], U8, name=f"x_s{h}", align_bytes=64)
@@ -141,7 +147,8 @@ def tile_list_tgn_mgu_kernel(
         zh_all, pre_all = scratch[:, 0:n_units, :], scratch[:, n_units:, :]
         pre_pair = keep.tile([P, 2, JH], F32, name="pre_pair", align_bytes=64)
         front_order = [0, 1, 2, 6, 3, 4, 5, 7]
-        zero_from = {4: 2, 7: 1}
+        leave_zero_from = {7: 1}
+        zero_from = {7: 2}
 
         def front(u):
             c, h = units[u]
@@ -154,9 +161,17 @@ def tile_list_tgn_mgu_kernel(
             nc.tensor.matmul_mx(out=xn[:], lhsT=fp4_cols(wn_w, c), lhsT_scale=scale_cols(wn_s, c), rhs=xw, rhs_scale=xs, start=True, stop=True)
             pre = pre_pair[:, u - 1, :] if u in (1, 2) else pre_all[:, u, :]
             nc.scalar.activation(z_all[:, u, :], sz[:], ACT.Sigmoid, bias=bz_sb[:, c : c + 1])
-            nc.vector.tensor_tensor(zh_all[:, u, :], hn[:], z_all[:, u, :], ALU.mult)
-            nc.vector.scalar_tensor_tensor(pre, xn[:], bn_sb[:, c : c + 1], zh_all[:, u, :], ALU.add, ALU.add)
-            nc.scalar.activation(cd_all[:, u, :], pre, ACT.Tanh, bias=o_sb[zero_from.get(u, 0)][:, 0:1])
+            if u in PRODUCT_ON_GPSIMD:
+                nc.scalar.activation(zh_all[:, u, :], hn[:], ACT.Identity, bias=o_sb[zero_from.get(u, 0)][:, 0:1])
+            elif u in zero_from:
+                nc.vector.scalar_tensor_tensor(zh_all[:, u, :], hn[:], o_sb[zero_from[u]][:, 0:1], z_all[:, u, :], ALU.add, ALU.mult)
+            else:
+                nc.vector.tensor_tensor(zh_all[:, u, :], hn[:], z_all[:, u, :], ALU.mult)
+            if u in SUM_ON_GPSIMD:
+                nc.scalar.activation(pre, xn[:], ACT.Identity, bias=o_sb[leave_zero_from.get(u, 0)][:, 0:1])
+            else:
+                nc.vector.scalar_tensor_tensor(pre, xn[:], bn_sb[:, c : c + 1], zh_all[:, u, :], ALU.add, ALU.add)
+                nc.scalar.activation(cd_all[:, u, :], pre, ACT.Tanh)
             nc.scalar.activation(zc_all[:, u, :], z_all[:, u, :], ACT.Copy, bias=1.0, scale=-1.0)
 
         def gather_state(u, dst):
@@ -182,13 +197,14 @@ def tile_list_tgn_mgu_kernel(
                 nc.sync.dma_start(out[c * P : (c + 1) * P, :], o_sb[c][:])
 
         z, zc, zh, cd = z_all, zc_all, zh_all, cd_all
-        v_w0 = keep.tile([P, JH], U32, name="v_w0", align_bytes=64)
+        v_w0 = keep.tile([P, JH], U32, name="v_w0", tag="v_w0", align_bytes=64)
         v_s0 = keep.tile([P, JH], U8, name="v_s0", align_bytes=64)
         vq[0] = gather_table(0, v_w0, v_s0)
         x_first = reuse.tile([P, 2, JH], F32, name="x_first", align_bytes=64, offset=0)
         xb0 = as_interleaved(x_first[:])
-        cast_x(0, xb0, nc.vector.tensor_copy, 1)
-        x_w0 = keep.tile([P, JH], U32, name="x_w0", align_bytes=64)
+        cast_x(0, xb0, nc.vector.tensor_copy, slice(0, CAST_SPLIT))
+        cast_x(0, xb0, nc.scalar.copy, slice(CAST_SPLIT, JH))
+        x_w0 = keep.tile([P, JH], U32, name="x_w0", tag="x_w0", align_bytes=64)
         xq[0] = quantise_x(0, xb0, x_w0)
         v_w1 = reuse.tile([P, JH], U32, name="v_w1", align_bytes=64, offset=0)
         v_s1 = reuse.tile([P, JH], U8, name="v_s1", align_bytes=64, offset=4 * JH)
@@ -201,14 +217,16 @@ def tile_list_tgn_mgu_kernel(
         gather_state(0, zh[:, 0, :])
         front(1)
         front(2)
-        gather_state(1, zh[:, 2, :])
         front(6)
-        gather_state(2, zh[:, 6, :])
-        gather_state(3, zh[:, 1, :])
-        gather_state(4, pre_all[:, 6, :])
+        picked = {u: keep.tile([P, JH], F32, name=f"picked{u}", tag=tag, align_bytes=64) for u, tag in ((1, "v_w0"), (4, "x_w0"))}
+        gather_state(1, picked[1][:])
+        gather_state(2, zh[:, 2, :])
+        gather_state(3, pre_all[:, 0, :])
+        gather_state(4, picked[4][:])
         xb1 = as_interleaved(pre_pair[:])
-        cast_x(1, xb1, nc.scalar.copy, 2)
-        x_w1 = keep.tile([P, JH], U32, name="x_w1", align_bytes=64)
+        for a in range(2):
+            cast_x(1, xb1, nc.scalar.copy, slice(a * JH // 2, (a + 1) * JH // 2))
+        x_w1 = keep.tile([P, JH], U32, name="x_w1", tag="x_w1", align_bytes=64)
         xq[1] = quantise_x(1, xb1, x_w1)
         front(3)
         front(4)
@@ -216,7 +234,8 @@ def tile_list_tgn_mgu_kernel(
         front(7)
         gather_state(5, pre_pair[:, 0, :])
         gather_state(6, pre_pair[:, 1, :])
-        gather_state(7, zh[:, 3, :])
+        picked_last = keep.tile([P, JH], F32, name="picked_last", tag="x_w1", align_bytes=64)
+        gather_state(7, picked_last[:])
 
         def blend_in_place(u, state):
             mul(cd[:, u, :], z[:, u, :], cd[:, u, :])
@@ -224,24 +243,71 @@ def tile_list_tgn_mgu_kernel(
             add(cd[:, u, :], zc[:, u, :], cd[:, u, :])
 
         blend_in_place(0, zh[:, 0, :])
-        blend_in_place(1, zh[:, 2, :])
+        blend_in_place(1, picked[1][:])
         mul(z[:, 0:2, :], cd[:, 0:2, :], weights(0, 2))
         scatter(0)
         scatter(1)
-        blend_in_place(2, zh[:, 6, :])
+        blend_in_place(2, zh[:, 2, :])
+
+        sums = {}
+        cand = [pre_all[:, u - 2, :] if u in SUM_ON_GPSIMD else cd[:, u, :] for u in range(n_units)]
+
+        def candidate(u, dst):
+            if u in PRODUCT_ON_GPSIMD:
+                mul(dst, zh[:, u, :], z[:, u, :])
+                add(dst, pre_all[:, u, :], dst)
+            elif u in SUM_ON_GPSIMD:
+                add(dst, pre_all[:, u, :], zh[:, u, :])
+            sums[u] = dst
+
+        def late_tanh(u):
+            c = units[u][0]
+            nc.scalar.activation(cand[u], sums[u], ACT.Tanh, bias=bn_sb[:, c : c + 1])
+
+        kept = {}
+
+        def products(u, state, dst):
+            kept[u] = dst
+            mul(dst, zc[:, u, :], state)
+            mul(cd[:, u, :], z[:, u, :], cand[u])
+
+        w_cols = keep.tile([P, J // P], F32, name="w_cols")
+        blocks = range(JH // P)
+
+        def turned_sum(u):
+            h = units[u][1]
+            turned, back = [bank[:].rearrange("p (b n) -> p b n", n=P) for bank in (sz_bank[1], xn_bank[u % 2])]
+            weighted = pre_all[:, u, :].rearrange("p (b n) -> p b n", n=P)
+            for b in blocks:
+                cols = slice(b * P, (b + 1) * P)
+                nc.tensor.matmul(turned[:, b, :], cd[:, u, cols], ident[:], start=True, stop=False, is_transpose=True)
+                nc.tensor.matmul(turned[:, b, :], kept[u][:, cols], ident[:], start=False, stop=True, is_transpose=True)
+            for b in blocks:
+                col = h * (JH // P) + b
+                nc.scalar.activation(weighted[:, b, :], turned[:, b, :], ACT.Copy, scale=w_cols[:, col : col + 1])
+            for b in blocks:
+                nc.tensor.transpose(back[:, b, :], weighted[:, b, :], ident[:])
+            nc.scalar.copy(z[:, u, :], back.rearrange("p b n -> p (b n)"))
+            scatter(u)
+
         mul(z[:, 2, :], cd[:, 2, :], wgo_sb[:, 0:JH])
         scatter(2)
-        mul(cd[:, 1:3, :], z[:, 3:5, :], cd[:, 3:5, :])
-        mul(cd[:, 3:5, :], zc[:, 3:5, :], scratch[:, 1 : n_units + 7 : n_units + 5, :])
-        add(cd[:, 1:3, :], cd[:, 1:3, :], cd[:, 3:5, :])
-        mul(z[:, 3:5, :], cd[:, 1:3, :], weights(1, 2))
-        scatter(3)
-        scatter(4)
-        for u, state in ((5, pre_pair[:, 0, :]), (6, pre_pair[:, 1, :]), (7, zh[:, 3, :])):
-            h = units[u][1]
-            mul(cd[:, 2, :], z[:, u, :], cd[:, u, :])
-            mul(cd[:, 1, :], zc[:, u, :], state)
-            add(cd[:, 1, :], cd[:, 1, :], cd[:, 2, :])
-            if u < n_units - 1:
-                mul(z[:, u, :], cd[:, 1, :], wgo_sb[:, h * JH : (h + 1) * JH])
-            scatter(u)
+        nc.tensor.transpose(xn_bank[2][:, 0:P], wgo_rows[:], ident[:])
+        nc.scalar.copy(w_cols[:], xn_bank[2][:, 0 : J // P])
+        products(3, pre_all[:, 0, :], zc[:, 3, :])
+        products(4, picked[4][:], zc[:, 4, :])
+        candidate(5, cd[:, 2, :])
+        turned_sum(3)
+        late_tanh(5)
+        candidate(6, zh[:, 5, :])
+        products(5, pre_pair[:, 0, :], picked[4][:])
+        turned_sum(4)
+        late_tanh(6)
+        products(6, pre_pair[:, 1, :], cand[5])
+        candidate(7, zh[:, 5, :])
+        turned_sum(5)
+        late_tanh(7)
+        products(7, picked_last[:], cand[6])
+        turned_sum(6)
+        add(cd[:, 1, :], kept[7], cd[:, 7, :])
+        scatter(7)

@@ -23,7 +23,7 @@ JH = 512
 HALVES = J // JH
 CHUNKS = N // P
 CAST_SPLIT = 336
-PRODUCT_ON_GPSIMD = (7,)
+PRODUCT_ON_GPSIMD = (6, 7)
 SUM_ON_GPSIMD = (5, 6, 7)
 
 
@@ -53,7 +53,7 @@ def tile_list_tgn_mgu_kernel(
         wn_w = keep.tile([P, N // 2], I32, name="wn_w", align_bytes=64)
         un_w = keep.tile([P, N], I32, name="un_w", align_bytes=64)
         x_rows = x.rearrange("(p i) j -> p i j", i=PACK)
-        x_raw = [keep.tile([P, PACK, JH], F32, name=f"x_raw{h}") for h in range(HALVES)]
+        x_raw = [keep.tile([P, PACK, JH], F32, name=f"x_raw{h}", tag=f"x_raw{h}") for h in range(HALVES)]
         h_sb = [keep.tile([P, T], F32, name=f"h_sb{c}") for c in range(CHUNKS)]
         wgo_sb = keep.tile([P, J], F32, name="wgo_sb")
         wgo_rows = keep.tile([P, P], F32, name="wgo_rows")
@@ -90,8 +90,8 @@ def tile_list_tgn_mgu_kernel(
         load_bias(bn_sb, bn)
         load_state(0)
         load_state(1)
-        load_state(2)
         nc.sync.dma_start(x_raw[1][:], x_rows[:, :, JH:J])
+        load_state(2)
         nc.sync.dma_start(wgo_sb[:], wgo)
         load_state(CHUNKS - 1)
         nc.sync.dma_start(wgo_rows[:], wgo[0 : P * P // J, :].rearrange("a (b j) -> (a b) j", j=P))
@@ -159,20 +159,31 @@ def tile_list_tgn_mgu_kernel(
             nc.tensor.matmul_mx(out=sz[:], lhsT=fp4_cols(wz_w, c), lhsT_scale=scale_cols(wz_s, c), rhs=xw, rhs_scale=xs, start=False, stop=True)
             nc.tensor.matmul_mx(out=hn[:], lhsT=fp8_cols(un_w, c), lhsT_scale=scale_cols(un_s, c), rhs=vw, rhs_scale=vs, start=True, stop=True)
             nc.tensor.matmul_mx(out=xn[:], lhsT=fp4_cols(wn_w, c), lhsT_scale=scale_cols(wn_s, c), rhs=xw, rhs_scale=xs, start=True, stop=True)
-            pre = pre_pair[:, u - 1, :] if u in (1, 2) else pre_all[:, u, :]
             nc.scalar.activation(z_all[:, u, :], sz[:], ACT.Sigmoid, bias=bz_sb[:, c : c + 1])
+
+        zh_row = [zh_all[:, u, :] for u in range(n_units)]
+        pre_row = [pre_pair[:, u, :] if u < 2 else pre_all[:, u, :] for u in range(n_units)]
+        zc_row = [zc_all[:, u, :] for u in range(n_units)]
+
+        def gate_product(u):
+            turn = front_order.index(u)
+            hn = hn_bank[turn % 3]
             if u in PRODUCT_ON_GPSIMD:
-                nc.scalar.activation(zh_all[:, u, :], hn[:], ACT.Identity, bias=o_sb[zero_from.get(u, 0)][:, 0:1])
+                nc.scalar.activation(zh_row[u], hn[:], ACT.Identity, bias=o_sb[zero_from.get(u, 0)][:, 0:1])
             elif u in zero_from:
-                nc.vector.scalar_tensor_tensor(zh_all[:, u, :], hn[:], o_sb[zero_from[u]][:, 0:1], z_all[:, u, :], ALU.add, ALU.mult)
+                nc.vector.scalar_tensor_tensor(zh_row[u], hn[:], o_sb[zero_from[u]][:, 0:1], z_all[:, u, :], ALU.add, ALU.mult)
             else:
-                nc.vector.tensor_tensor(zh_all[:, u, :], hn[:], z_all[:, u, :], ALU.mult)
+                nc.vector.tensor_tensor(zh_row[u], hn[:], z_all[:, u, :], ALU.mult)
+
+        def leave(u):
+            c = units[u][0]
+            xn, pre = xn_bank[front_order.index(u) % 3], pre_row[u]
             if u in SUM_ON_GPSIMD:
                 nc.scalar.activation(pre, xn[:], ACT.Identity, bias=o_sb[leave_zero_from.get(u, 0)][:, 0:1])
             else:
-                nc.vector.scalar_tensor_tensor(pre, xn[:], bn_sb[:, c : c + 1], zh_all[:, u, :], ALU.add, ALU.add)
+                nc.vector.scalar_tensor_tensor(pre, xn[:], bn_sb[:, c : c + 1], zh_row[u], ALU.add, ALU.add)
                 nc.scalar.activation(cd_all[:, u, :], pre, ACT.Tanh)
-            nc.scalar.activation(zc_all[:, u, :], z_all[:, u, :], ACT.Copy, bias=1.0, scale=-1.0)
+            nc.scalar.activation(zc_row[u], z_all[:, u, :], ACT.Copy, bias=1.0, scale=-1.0)
 
         def gather_state(u, dst):
             c, h = units[u]
@@ -214,24 +225,43 @@ def tile_list_tgn_mgu_kernel(
         o_sb.extend([o_third, o_sb[0]])
 
         front(0)
+        gate_product(0)
+        leave(0)
         gather_state(0, zh[:, 0, :])
         front(1)
+        gate_product(1)
+        leave(1)
         front(2)
+        gate_product(2)
+        leave(2)
         front(6)
         picked = {u: keep.tile([P, JH], F32, name=f"picked{u}", tag=tag, align_bytes=64) for u, tag in ((1, "v_w0"), (4, "x_w0"))}
         gather_state(1, picked[1][:])
-        gather_state(2, zh[:, 2, :])
-        gather_state(3, pre_all[:, 0, :])
+        gather_state(2, zh[:, 1, :])
+        gather_state(3, zh[:, 2, :])
         gather_state(4, picked[4][:])
         xb1 = as_interleaved(pre_pair[:])
         for a in range(2):
             cast_x(1, xb1, nc.scalar.copy, slice(a * JH // 2, (a + 1) * JH // 2))
+        late_rows = keep.tile([P, 3, JH], F32, name="late_rows", tag="x_raw1")
+        pre_row[6], zc_row[6] = late_rows[:, 0, :], late_rows[:, 1, :]
+        zh_row[6] = late_rows[:, 2, :]
+        gate_product(6)
+        leave(6)
         x_w1 = keep.tile([P, JH], U32, name="x_w1", tag="x_w1", align_bytes=64)
         xq[1] = quantise_x(1, xb1, x_w1)
         front(3)
+        gate_product(3)
+        leave(3)
         front(4)
+        gate_product(4)
+        leave(4)
         front(5)
+        gate_product(5)
+        leave(5)
         front(7)
+        gate_product(7)
+        leave(7)
         gather_state(5, pre_pair[:, 0, :])
         gather_state(6, pre_pair[:, 1, :])
         picked_last = keep.tile([P, JH], F32, name="picked_last", tag="x_w1", align_bytes=64)
@@ -242,22 +272,16 @@ def tile_list_tgn_mgu_kernel(
             mul(zc[:, u, :], zc[:, u, :], state)
             add(cd[:, u, :], zc[:, u, :], cd[:, u, :])
 
-        blend_in_place(0, zh[:, 0, :])
-        blend_in_place(1, picked[1][:])
-        mul(z[:, 0:2, :], cd[:, 0:2, :], weights(0, 2))
-        scatter(0)
-        scatter(1)
-        blend_in_place(2, zh[:, 2, :])
 
         sums = {}
-        cand = [pre_all[:, u - 2, :] if u in SUM_ON_GPSIMD else cd[:, u, :] for u in range(n_units)]
+        cand = [cd[:, u, :] for u in range(5)] + [pre_all[:, u, :] for u in (3, 4, 6)]
 
         def candidate(u, dst):
             if u in PRODUCT_ON_GPSIMD:
-                mul(dst, zh[:, u, :], z[:, u, :])
-                add(dst, pre_all[:, u, :], dst)
+                mul(dst, zh_row[u], z[:, u, :])
+                add(dst, pre_row[u], dst)
             elif u in SUM_ON_GPSIMD:
-                add(dst, pre_all[:, u, :], zh[:, u, :])
+                add(dst, pre_row[u], zh_row[u])
             sums[u] = dst
 
         def late_tanh(u):
@@ -268,7 +292,7 @@ def tile_list_tgn_mgu_kernel(
 
         def products(u, state, dst):
             kept[u] = dst
-            mul(dst, zc[:, u, :], state)
+            mul(dst, zc_row[u], state)
             mul(cd[:, u, :], z[:, u, :], cand[u])
 
         w_cols = keep.tile([P, J // P], F32, name="w_cols")
@@ -290,11 +314,17 @@ def tile_list_tgn_mgu_kernel(
             nc.scalar.copy(z[:, u, :], back.rearrange("p b n -> p (b n)"))
             scatter(u)
 
+        blend_in_place(0, zh[:, 0, :])
+        mul(z[:, 0, :], cd[:, 0, :], wgo_sb[:, 0:JH])
+        scatter(0)
+        products(1, picked[1][:], zc[:, 1, :])
+        blend_in_place(2, zh[:, 1, :])
         mul(z[:, 2, :], cd[:, 2, :], wgo_sb[:, 0:JH])
         scatter(2)
         nc.tensor.transpose(xn_bank[2][:, 0:P], wgo_rows[:], ident[:])
         nc.scalar.copy(w_cols[:], xn_bank[2][:, 0 : J // P])
-        products(3, pre_all[:, 0, :], zc[:, 3, :])
+        turned_sum(1)
+        products(3, zh[:, 2, :], zc[:, 3, :])
         products(4, picked[4][:], zc[:, 4, :])
         candidate(5, cd[:, 2, :])
         turned_sum(3)
@@ -306,8 +336,8 @@ def tile_list_tgn_mgu_kernel(
         products(6, pre_pair[:, 1, :], cand[5])
         candidate(7, zh[:, 5, :])
         turned_sum(5)
+        turned_sum(6)
         late_tanh(7)
         products(7, picked_last[:], cand[6])
-        turned_sum(6)
         add(cd[:, 1, :], kept[7], cd[:, 7, :])
         scatter(7)

@@ -23,7 +23,7 @@ JH = 512
 HALVES = J // JH
 CHUNKS = N // P
 CAST_SPLIT = 336
-PRODUCT_ON_GPSIMD = (6, 7)
+PRODUCT_ON_GPSIMD = (5, 6, 7)
 SUM_ON_GPSIMD = (5, 6, 7)
 
 
@@ -91,10 +91,11 @@ def tile_list_tgn_mgu_kernel(
         load_state(0)
         load_state(1)
         nc.sync.dma_start(x_raw[1][:], x_rows[:, :, JH:J])
+        nc.sync.dma_start(wgo_sb[:, 0:JH], wgo[:, 0:JH])
         load_state(2)
-        nc.sync.dma_start(wgo_sb[:], wgo)
         load_state(CHUNKS - 1)
         nc.sync.dma_start(wgo_rows[:], wgo[0 : P * P // J, :].rearrange("a (b j) -> (a b) j", j=P))
+        nc.sync.dma_start(wgo_sb[:, JH:J], wgo[:, JH:J])
         load_scale_rows(nc.gpsimd, wn_s, wn_scales, range(4))
 
         ident = keep.tile([P, P], F32, name="ident")
@@ -139,16 +140,19 @@ def tile_list_tgn_mgu_kernel(
 
         units = [(0, 0), (1, 0), (2, 0), (0, 1), (1, 1), (2, 1), (3, 0), (3, 1)]
         n_units = len(units)
-        xq, vq = {}, {}
-        z_all = keep.tile([P, n_units, JH], F32, name="z_all")
-        zc_all = keep.tile([P, n_units, JH], F32, name="zc_all")
-        cd_all = keep.tile([P, n_units, JH], F32, name="cd_all")
-        scratch = keep.tile([P, 2 * n_units, JH], F32, name="scratch")
-        zh_all, pre_all = scratch[:, 0:n_units, :], scratch[:, n_units:, :]
-        pre_pair = keep.tile([P, 2, JH], F32, name="pre_pair", align_bytes=64)
         front_order = [0, 1, 2, 6, 3, 4, 5, 7]
-        leave_zero_from = {7: 1}
-        zero_from = {7: 2}
+        xq, vq = {}, {}
+        z = keep.tile([P, n_units, JH], F32, name="z")
+        cd = keep.tile([P, n_units, JH], F32, name="cd")
+        zh = keep.tile([P, n_units, JH], F32, name="zh")
+        pre = keep.tile([P, n_units, JH], F32, name="pre")
+        diff = keep.tile([P, n_units, JH], F32, name="diff")
+        pre_pair = keep.tile([P, 2, JH], F32, name="pre_pair", align_bytes=64)
+        state = keep.tile([P, CHUNKS, J], F32, name="state")
+        zh_row = [zh[:, u, :] for u in range(n_units)]
+        pre_row = [pre_pair[:, u, :] if u < 2 else pre[:, u, :] for u in range(n_units)]
+        state_row = [state[:, c, h * JH : (h + 1) * JH] for c, h in units]
+        state_row[0], state_row[3] = zh[:, 0, :], zh[:, 2, :]
 
         def front(u):
             c, h = units[u]
@@ -159,63 +163,49 @@ def tile_list_tgn_mgu_kernel(
             nc.tensor.matmul_mx(out=sz[:], lhsT=fp4_cols(wz_w, c), lhsT_scale=scale_cols(wz_s, c), rhs=xw, rhs_scale=xs, start=False, stop=True)
             nc.tensor.matmul_mx(out=hn[:], lhsT=fp8_cols(un_w, c), lhsT_scale=scale_cols(un_s, c), rhs=vw, rhs_scale=vs, start=True, stop=True)
             nc.tensor.matmul_mx(out=xn[:], lhsT=fp4_cols(wn_w, c), lhsT_scale=scale_cols(wn_s, c), rhs=xw, rhs_scale=xs, start=True, stop=True)
-            nc.scalar.activation(z_all[:, u, :], sz[:], ACT.Sigmoid, bias=bz_sb[:, c : c + 1])
-
-        zh_row = [zh_all[:, u, :] for u in range(n_units)]
-        pre_row = [pre_pair[:, u, :] if u < 2 else pre_all[:, u, :] for u in range(n_units)]
-        zc_row = [zc_all[:, u, :] for u in range(n_units)]
-
-        def gate_product(u):
-            turn = front_order.index(u)
-            hn = hn_bank[turn % 3]
-            if u in PRODUCT_ON_GPSIMD:
-                nc.scalar.activation(zh_row[u], hn[:], ACT.Identity, bias=o_sb[zero_from.get(u, 0)][:, 0:1])
-            elif u in zero_from:
-                nc.vector.scalar_tensor_tensor(zh_row[u], hn[:], o_sb[zero_from[u]][:, 0:1], z_all[:, u, :], ALU.add, ALU.mult)
-            else:
-                nc.vector.tensor_tensor(zh_row[u], hn[:], z_all[:, u, :], ALU.mult)
+            nc.scalar.activation(z[:, u, :], sz[:], ACT.Sigmoid, bias=bz_sb[:, c : c + 1])
 
         def leave(u):
             c = units[u][0]
-            xn, pre = xn_bank[front_order.index(u) % 3], pre_row[u]
-            if u in SUM_ON_GPSIMD:
-                nc.scalar.activation(pre, xn[:], ACT.Identity, bias=o_sb[leave_zero_from.get(u, 0)][:, 0:1])
+            turn = front_order.index(u)
+            hn, xn = hn_bank[turn % 3], xn_bank[turn % 3]
+            if u in PRODUCT_ON_GPSIMD:
+                nc.scalar.copy(zh_row[u], hn[:])
             else:
-                nc.vector.scalar_tensor_tensor(pre, xn[:], bn_sb[:, c : c + 1], zh_row[u], ALU.add, ALU.add)
-                nc.scalar.activation(cd_all[:, u, :], pre, ACT.Tanh)
-            nc.scalar.activation(zc_row[u], z_all[:, u, :], ACT.Copy, bias=1.0, scale=-1.0)
+                nc.vector.tensor_tensor(zh_row[u], hn[:], z[:, u, :], ALU.mult)
+            if u in SUM_ON_GPSIMD:
+                nc.scalar.activation(pre_row[u], xn[:], ACT.Identity, bias=o_sb[0][:, 0:1] if u == 5 else 0.0)
+            else:
+                nc.vector.scalar_tensor_tensor(pre_row[u], xn[:], bn_sb[:, c : c + 1], zh_row[u], ALU.add, ALU.add)
+                nc.scalar.activation(cd[:, u, :], pre_row[u], ACT.Tanh)
 
-        def gather_state(u, dst):
+        def gather_unit(u):
             c, h = units[u]
-            nc.vector.tensor_copy(dst, h_sb[c][:].indirect(part(h)))
+            nc.vector.tensor_copy(state_row[u], h_sb[c][:].indirect(part(h)))
 
-        def mul(dst, a, b):
-            nc.gpsimd.tensor_tensor(dst, a, b, ALU.mult)
+        def gather_block(c):
+            nc.vector.tensor_copy(state[:, c, :], h_sb[c][:].indirect(offsets[:]))
 
-        def add(dst, a, b):
-            nc.gpsimd.tensor_tensor(dst, a, b, ALU.add)
-
-        def weights(h, n):
-            return wgo_sb[:, h * JH : (h + 1) * JH].unsqueeze(1).broadcast_to([P, n, JH])
+        def on_gpsimd(dst, a, b, op):
+            nc.gpsimd.tensor_tensor(dst, a, b, op)
 
         def scatter(u):
             c, h = units[u]
             if u == n_units - 1:
-                nc.vector.tensor_tensor(o_sb[c][:].indirect(part(h)), cd_all[:, 1, :], wgo_sb[:, h * JH : (h + 1) * JH], ALU.mult)
+                nc.vector.tensor_tensor(o_sb[c][:].indirect(part(h)), cd[:, u, :], wgo_sb[:, h * JH : (h + 1) * JH], ALU.mult)
             else:
-                nc.vector.tensor_copy(o_sb[c][:].indirect(part(h)), z_all[:, u, :])
+                nc.vector.tensor_copy(o_sb[c][:].indirect(part(h)), z[:, u, :])
             if h == HALVES - 1:
                 nc.sync.dma_start(out[c * P : (c + 1) * P, :], o_sb[c][:])
 
-        z, zc, zh, cd = z_all, zc_all, zh_all, cd_all
-        v_w0 = keep.tile([P, JH], U32, name="v_w0", tag="v_w0", align_bytes=64)
+        v_w0 = keep.tile([P, JH], U32, name="v_w0", align_bytes=64)
         v_s0 = keep.tile([P, JH], U8, name="v_s0", align_bytes=64)
         vq[0] = gather_table(0, v_w0, v_s0)
         x_first = reuse.tile([P, 2, JH], F32, name="x_first", align_bytes=64, offset=0)
         xb0 = as_interleaved(x_first[:])
         cast_x(0, xb0, nc.vector.tensor_copy, slice(0, CAST_SPLIT))
         cast_x(0, xb0, nc.scalar.copy, slice(CAST_SPLIT, JH))
-        x_w0 = keep.tile([P, JH], U32, name="x_w0", tag="x_w0", align_bytes=64)
+        x_w0 = keep.tile([P, JH], U32, name="x_w0", align_bytes=64)
         xq[0] = quantise_x(0, xb0, x_w0)
         v_w1 = reuse.tile([P, JH], U32, name="v_w1", align_bytes=64, offset=0)
         v_s1 = reuse.tile([P, JH], U8, name="v_s1", align_bytes=64, offset=4 * JH)
@@ -224,120 +214,112 @@ def tile_list_tgn_mgu_kernel(
         nc.gpsimd.memset(o_third[:], 0.0)
         o_sb.extend([o_third, o_sb[0]])
 
-        front(0)
-        gate_product(0)
-        leave(0)
-        gather_state(0, zh[:, 0, :])
-        front(1)
-        gate_product(1)
-        leave(1)
-        front(2)
-        gate_product(2)
-        leave(2)
+        for u in range(3):
+            front(u)
+            leave(u)
+            if u != 1:
+                gather_unit(0 if u == 0 else 3)
         front(6)
-        picked = {u: keep.tile([P, JH], F32, name=f"picked{u}", tag=tag, align_bytes=64) for u, tag in ((1, "v_w0"), (4, "x_w0"))}
-        gather_state(1, picked[1][:])
-        gather_state(2, zh[:, 1, :])
-        gather_state(3, zh[:, 2, :])
-        gather_state(4, picked[4][:])
+        gather_block(1)
         xb1 = as_interleaved(pre_pair[:])
         for a in range(2):
             cast_x(1, xb1, nc.scalar.copy, slice(a * JH // 2, (a + 1) * JH // 2))
         late_rows = keep.tile([P, 3, JH], F32, name="late_rows", tag="x_raw1")
-        pre_row[6], zc_row[6] = late_rows[:, 0, :], late_rows[:, 1, :]
-        zh_row[6] = late_rows[:, 2, :]
-        gate_product(6)
+        zh_row[6], pre_row[6] = late_rows[:, 0, :], late_rows[:, 1, :]
         leave(6)
-        x_w1 = keep.tile([P, JH], U32, name="x_w1", tag="x_w1", align_bytes=64)
+        x_w1 = keep.tile([P, JH], U32, name="x_w1", align_bytes=64)
         xq[1] = quantise_x(1, xb1, x_w1)
-        front(3)
-        gate_product(3)
-        leave(3)
-        front(4)
-        gate_product(4)
-        leave(4)
-        front(5)
-        gate_product(5)
-        leave(5)
+        for u in (3, 4, 5):
+            front(u)
+            leave(u)
         front(7)
-        gate_product(7)
-        leave(7)
-        gather_state(5, pre_pair[:, 0, :])
-        gather_state(6, pre_pair[:, 1, :])
-        picked_last = keep.tile([P, JH], F32, name="picked_last", tag="x_w1", align_bytes=64)
-        gather_state(7, picked_last[:])
-
-        def blend_in_place(u, state):
-            mul(cd[:, u, :], z[:, u, :], cd[:, u, :])
-            mul(zc[:, u, :], zc[:, u, :], state)
-            add(cd[:, u, :], zc[:, u, :], cd[:, u, :])
-
+        gather_block(2)
+        gather_block(3)
 
         sums = {}
-        cand = [cd[:, u, :] for u in range(5)] + [pre_all[:, u, :] for u in (3, 4, 6)]
+        cand = [cd[:, u, :] for u in range(n_units)]
 
         def candidate(u, dst):
             if u in PRODUCT_ON_GPSIMD:
-                mul(dst, zh_row[u], z[:, u, :])
-                add(dst, pre_row[u], dst)
-            elif u in SUM_ON_GPSIMD:
-                add(dst, pre_row[u], zh_row[u])
+                on_gpsimd(dst, zh_row[u], z[:, u, :], ALU.mult)
+                on_gpsimd(dst, pre_row[u], dst, ALU.add)
+            else:
+                on_gpsimd(dst, pre_row[u], zh_row[u], ALU.add)
             sums[u] = dst
 
-        def late_tanh(u):
+        def late_tanh(u, dst):
             c = units[u][0]
-            nc.scalar.activation(cand[u], sums[u], ACT.Tanh, bias=bn_sb[:, c : c + 1])
+            cand[u] = dst
+            nc.scalar.activation(dst, sums[u], ACT.Tanh, bias=bn_sb[:, c : c + 1])
 
-        kept = {}
+        def step(u, dst):
+            on_gpsimd(dst, cand[u], state_row[u], ALU.subtract)
+            on_gpsimd(cd[:, u, :], dst, z[:, u, :], ALU.mult)
 
-        def products(u, state, dst):
+        kept = list(state_row)
+
+        def kept_share(u, dst):
+            rest = {5: weighted_all[:, 2, :], 6: late_rows[:, 2, :], 7: cd[:, 3, :]}.get(u, dst)
+            nc.scalar.activation(rest, z[:, u, :], ACT.Copy, bias=1.0, scale=-1.0)
+            on_gpsimd(dst, rest, state_row[u], ALU.mult)
             kept[u] = dst
-            mul(dst, zc_row[u], state)
-            mul(cd[:, u, :], z[:, u, :], cand[u])
+
+        def new_share(u):
+            on_gpsimd(cd[:, u, :], cand[u], z[:, u, :], ALU.mult)
 
         w_cols = keep.tile([P, J // P], F32, name="w_cols")
+        weighted_all = keep.tile([P, n_units, JH], F32, name="weighted_all")
         blocks = range(JH // P)
 
         def turned_sum(u):
             h = units[u][1]
-            turned, back = [bank[:].rearrange("p (b n) -> p b n", n=P) for bank in (sz_bank[1], xn_bank[u % 2])]
-            weighted = pre_all[:, u, :].rearrange("p (b n) -> p b n", n=P)
+            back = xn_bank[2 * (u % 2)][:].rearrange("p (b n) -> p b n", n=P)
+            first = sz_bank[0] if u < 5 else hn_bank[0]
+            turned = [(first if b < 2 else hn_bank[0])[:, b * P : (b + 1) * P] for b in blocks]
+            weighted = weighted_all[:, u, :].rearrange("p (b n) -> p b n", n=P)
             for b in blocks:
                 cols = slice(b * P, (b + 1) * P)
-                nc.tensor.matmul(turned[:, b, :], cd[:, u, cols], ident[:], start=True, stop=False, is_transpose=True)
-                nc.tensor.matmul(turned[:, b, :], kept[u][:, cols], ident[:], start=False, stop=True, is_transpose=True)
+                nc.tensor.matmul(turned[b], cd[:, u, cols], ident[:], start=True, stop=False, is_transpose=True)
+                nc.tensor.matmul(turned[b], kept[u][:, cols], ident[:], start=False, stop=True, is_transpose=True)
             for b in blocks:
                 col = h * (JH // P) + b
-                nc.scalar.activation(weighted[:, b, :], turned[:, b, :], ACT.Copy, scale=w_cols[:, col : col + 1])
+                nc.scalar.activation(weighted[:, b, :], turned[b], ACT.Copy, scale=w_cols[:, col : col + 1])
             for b in blocks:
                 nc.tensor.transpose(back[:, b, :], weighted[:, b, :], ident[:])
             nc.scalar.copy(z[:, u, :], back.rearrange("p b n -> p (b n)"))
             scatter(u)
 
-        blend_in_place(0, zh[:, 0, :])
-        mul(z[:, 0, :], cd[:, 0, :], wgo_sb[:, 0:JH])
+        nc.tensor.transpose(hn_bank[2][:, 0:P], wgo_rows[:], ident[:])
+        nc.scalar.copy(w_cols[:], hn_bank[2][:, 0 : J // P])
+        new_share(0)
+        kept_share(0, diff[:, 0, :])
+        on_gpsimd(cd[:, 0, :], cd[:, 0, :], kept[0], ALU.add)
+        on_gpsimd(z[:, 0, :], cd[:, 0, :], wgo_sb[:, 0:JH], ALU.mult)
         scatter(0)
-        products(1, picked[1][:], zc[:, 1, :])
-        blend_in_place(2, zh[:, 1, :])
-        mul(z[:, 2, :], cd[:, 2, :], wgo_sb[:, 0:JH])
-        scatter(2)
-        nc.tensor.transpose(xn_bank[2][:, 0:P], wgo_rows[:], ident[:])
-        nc.scalar.copy(w_cols[:], xn_bank[2][:, 0 : J // P])
+        for u in (1, 2):
+            new_share(u)
+            kept_share(u, diff[:, u, :])
         turned_sum(1)
-        products(3, zh[:, 2, :], zc[:, 3, :])
-        products(4, picked[4][:], zc[:, 4, :])
-        candidate(5, cd[:, 2, :])
+        turned_sum(2)
+        zh_row[7], pre_row[7] = weighted_all[:, 1, :], cd[:, 2, :]
+        leave(7)
+        step(3, diff[:, 3, :])
+        step(4, diff[:, 4, :])
+        candidate(5, diff[:, 3, :])
+        candidate(6, diff[:, 4, :])
+        kept_share(5, zh[:, 5, :])
         turned_sum(3)
-        late_tanh(5)
-        candidate(6, zh[:, 5, :])
-        products(5, pre_pair[:, 0, :], picked[4][:])
+        late_tanh(5, weighted_all[:, 3, :])
+        new_share(5)
+        kept_share(6, cand[5])
         turned_sum(4)
-        late_tanh(6)
-        products(6, pre_pair[:, 1, :], cand[5])
-        candidate(7, zh[:, 5, :])
+        late_tanh(6, weighted_all[:, 4, :])
+        new_share(6)
+        candidate(7, diff[:, 4, :])
+        kept_share(7, cand[6])
         turned_sum(5)
         turned_sum(6)
-        late_tanh(7)
-        products(7, picked_last[:], cand[6])
-        add(cd[:, 1, :], kept[7], cd[:, 7, :])
+        late_tanh(7, weighted_all[:, 6, :])
+        new_share(7)
+        on_gpsimd(cd[:, 7, :], cd[:, 7, :], kept[7], ALU.add)
         scatter(7)

@@ -19,12 +19,16 @@ ALU = mybir.AluOpType
 
 P = 128
 PACK = 4
+QUADRANTS = 4
 JH = 512
 HALVES = J // JH
 CHUNKS = N // P
+LIST_GROUP = 16
 CAST_SPLIT = 336
-PRODUCT_ON_GPSIMD = (5, 6, 7)
-SUM_ON_GPSIMD = (5, 6, 7)
+UNITS = [(0, 0), (1, 0), (2, 0), (0, 1), (1, 1), (2, 1), (3, 0), (3, 1)]
+MATMUL_ORDER = sorted(range(len(UNITS)), key=lambda u: UNITS[u][1])
+LATE_FROM = 5
+LAST = len(UNITS) - 1
 
 
 def tile_list_tgn_mgu_kernel(
@@ -37,17 +41,13 @@ def tile_list_tgn_mgu_kernel(
         reuse = ctx.enter_context(tc.tile_pool(name="reuse", bufs=1))
         psum = ctx.enter_context(tc.psum_pool(name="psum", bufs=1))
 
-        offsets = keep.tile([P, J // 16], U16, name="offsets")
+        offsets = keep.tile([P, J // LIST_GROUP], U16, name="offsets")
         nc.sync.dma_start(offsets[:], offs)
 
-        def load_scale_rows(queue, plane, rows, quadrants):
-            for q in quadrants:
-                queue.dma_start(plane[32 * q : 32 * q + 4, :], rows[0, 4 * q : 4 * q + 4, :].bitcast(I32))
-
-        tab_s = keep.tile([P, T // 4 + 1], I32, name="tab_s", align_bytes=64)
+        tab_s = keep.tile([P, T // 4], I32, name="tab_s", align_bytes=64)
         tab_w = keep.tile([P, T], I32, name="tab_w", align_bytes=64)
-        w_s = keep.tile([P, N + 1], I32, name="w_s", align_bytes=64)
-        uz_s, wz_s, un_s, wn_s = [w_s[:, a * (N // 4) : (a + 1) * (N // 4)] for a in range(4)]
+        weight_s = keep.tile([P, N], I32, name="weight_s", align_bytes=64)
+        uz_s, wz_s, un_s, wn_s = [weight_s[:, a * (N // 4) : (a + 1) * (N // 4)] for a in range(4)]
         wz_w = keep.tile([P, N // 2], I32, name="wz_w", align_bytes=64)
         uz_w = keep.tile([P, N], I32, name="uz_w", align_bytes=64)
         wn_w = keep.tile([P, N // 2], I32, name="wn_w", align_bytes=64)
@@ -60,32 +60,43 @@ def tile_list_tgn_mgu_kernel(
         bz_sb = keep.tile([P, CHUNKS], F32, name="bz_sb")
         bn_sb = keep.tile([P, CHUNKS], F32, name="bn_sb")
 
-        def load_state(c):
-            nc.sync.dma_start(h_sb[c][:], hT[c * P : (c + 1) * P, :])
+        def zero_on_vector(tile, zero):
+            width = tile.shape[1]
+            nc.vector.memset(tile[:, 0 : width - 1], zero)
+            nc.vector.memset(tile[:, width - 1 : width], zero)
+
+        def load_scale_rows(queue, scales, rows, quadrants):
+            for q in quadrants:
+                queue.dma_start(scales[32 * q : 32 * q + 4, :], rows[0, 4 * q : 4 * q + 4, :].bitcast(I32))
+
+        def load_words(tile, words):
+            nc.sync.dma_start(tile[:], words[0].rearrange("p n i -> p (n i)").bitcast(I32))
 
         def load_bias(tile, vec):
             with nc.allow_non_contiguous_dma(reason="one bias value to a partition"):
                 nc.sync.dma_start(tile[:], vec.rearrange("(c p) -> p c", p=P))
 
+        def load_state(c):
+            nc.sync.dma_start(h_sb[c][:], hT[c * P : (c + 1) * P, :])
+
         o_sb = [keep.tile([P, T], F32, name=f"o_sb{c}") for c in range(2)]
-        nc.vector.memset(tab_s[:], 0)
-        nc.vector.memset(w_s[:], 0)
-        nc.vector.memset(o_sb[0][:, 0 : T - 1], 0.0)
-        nc.vector.memset(o_sb[0][:, T - 1 : T], 0.0)
+        zero_on_vector(tab_s, 0)
+        zero_on_vector(weight_s, 0)
+        zero_on_vector(o_sb[0], 0.0)
         nc.gpsimd.memset(o_sb[1][:], 0.0)
 
-        nc.sync.dma_start(tab_w[:], tab_words[0].rearrange("p t i -> p (t i)").bitcast(I32))
-        load_scale_rows(nc.sync, tab_s[:, 0 : T // 4], tab_scales, range(4))
-        load_scale_rows(nc.sync, uz_s, uz_scales, range(2))
+        load_words(tab_w, tab_words)
+        load_scale_rows(nc.sync, tab_s, tab_scales, range(QUADRANTS))
+        load_scale_rows(nc.sync, uz_s, uz_scales, range(QUADRANTS // 2))
         nc.sync.dma_start(x_raw[0][:], x_rows[:, :, 0:JH])
-        load_scale_rows(nc.sync, uz_s, uz_scales, range(2, 4))
-        load_scale_rows(nc.sync, wz_s, wz_scales, range(2))
-        nc.sync.dma_start(uz_w[:], uz_words[0].rearrange("p n i -> p (n i)").bitcast(I32))
+        load_scale_rows(nc.sync, uz_s, uz_scales, range(QUADRANTS // 2, QUADRANTS))
+        load_scale_rows(nc.sync, wz_s, wz_scales, range(QUADRANTS // 2))
+        load_words(uz_w, uz_words)
         nc.sync.dma_start(wz_w[:], wz_words[0].bitcast(I32))
-        nc.sync.dma_start(un_w[:], un_words[0].rearrange("p n i -> p (n i)").bitcast(I32))
-        load_scale_rows(nc.sync, wz_s, wz_scales, range(2, 4))
+        load_words(un_w, un_words)
+        load_scale_rows(nc.sync, wz_s, wz_scales, range(QUADRANTS // 2, QUADRANTS))
         load_bias(bz_sb, bz)
-        load_scale_rows(nc.sync, un_s, un_scales, range(4))
+        load_scale_rows(nc.sync, un_s, un_scales, range(QUADRANTS))
         nc.sync.dma_start(wn_w[:], wn_words[0].bitcast(I32))
         load_bias(bn_sb, bn)
         load_state(0)
@@ -93,26 +104,25 @@ def tile_list_tgn_mgu_kernel(
         nc.sync.dma_start(x_raw[1][:], x_rows[:, :, JH:J])
         nc.sync.dma_start(wgo_sb[:, 0:JH], wgo[:, 0:JH])
         load_state(2)
-        load_state(CHUNKS - 1)
+        load_state(3)
         nc.sync.dma_start(wgo_rows[:], wgo[0 : P * P // J, :].rearrange("a (b j) -> (a b) j", j=P))
         nc.sync.dma_start(wgo_sb[:, JH:J], wgo[:, JH:J])
-        load_scale_rows(nc.gpsimd, wn_s, wn_scales, range(4))
+        load_scale_rows(nc.gpsimd, wn_s, wn_scales, range(QUADRANTS))
 
         ident = keep.tile([P, P], F32, name="ident")
         make_identity(nc, ident[:])
-        warm = keep.tile([P, 1], F32, name="warm")
-        nc.scalar.activation(warm[:], o_sb[0][:, 0:1], ACT.Sigmoid)
 
-        def part(h):
-            return offsets[:, h * (JH // 16) : (h + 1) * (JH // 16)]
+        def entries(h):
+            width = JH // LIST_GROUP
+            return offsets[:, h * width : (h + 1) * width]
 
-        def gather_table(h, gw, gs):
-            nc.vector.tensor_copy(gw[:], tab_w[:].bitcast(U32).indirect(part(h)))
-            nc.vector.tensor_copy(gs[:], tab_s[:, 0 : T // 4].bitcast(U8).indirect(part(h)))
-            return gw[:].bitcast(FP8X4), gs[:]
+        def gather_table(h, words, scales):
+            nc.vector.tensor_copy(words[:], tab_w[:].bitcast(U32).indirect(entries(h)))
+            nc.vector.tensor_copy(scales[:], tab_s[:].bitcast(U8).indirect(entries(h)))
+            return words[:].bitcast(FP8X4), scales[:]
 
-        def as_interleaved(words):
-            return words.rearrange("p a j -> p (a j)").bitcast(BF16).rearrange("p (j i) -> p j i", i=PACK)
+        def as_quantise_input(rows):
+            return rows.rearrange("p a j -> p (a j)").bitcast(BF16).rearrange("p (j i) -> p j i", i=PACK)
 
         def cast_x(h, xb, copy, cols):
             copy(
@@ -120,206 +130,202 @@ def tile_list_tgn_mgu_kernel(
                 in_=x_raw[h][:, :, cols].rearrange("p i (a b) -> p a i b", b=4),
             )
 
-        def quantise_x(h, xb, qw):
-            qs = keep.tile([P, JH], U8, name=f"x_s{h}", align_bytes=64)
-            nc.vector.quantize_mx(out=qw[:].bitcast(FP8X4), scales=qs[:], in_=xb.rearrange("p j i -> p (j i)"))
-            return qw[:].bitcast(FP8X4), qs[:]
+        def quantise_x(h, xb):
+            words = keep.tile([P, JH], U32, name=f"x_w{h}", align_bytes=64)
+            scales = keep.tile([P, JH], U8, name=f"x_s{h}", align_bytes=64)
+            nc.vector.quantize_mx(out=words[:].bitcast(FP8X4), scales=scales[:], in_=xb.rearrange("p j i -> p (j i)"))
+            return words[:].bitcast(FP8X4), scales[:]
 
         def fp4_cols(words, c):
-            return words[:, 64 * c : 64 * (c + 1)].bitcast(FP4X4)
+            return words[:, (P // 2) * c : (P // 2) * (c + 1)].bitcast(FP4X4)
 
         def fp8_cols(words, c):
             return words[:, P * c : P * (c + 1)].bitcast(FP8X4)
 
-        def scale_cols(plane, c):
-            return plane[:, 32 * c : 32 * (c + 1)].bitcast(U8)
+        def scale_cols(scales, c):
+            return scales[:, (P // 4) * c : (P // 4) * (c + 1)].bitcast(U8)
 
         sz_bank = [psum.tile([P, JH], F32, name=f"sz{i}") for i in range(2)]
         hn_bank = [psum.tile([P, JH], F32, name=f"hn{i}") for i in range(3)]
         xn_bank = [psum.tile([P, JH], F32, name=f"xn{i}") for i in range(3)]
 
-        units = [(0, 0), (1, 0), (2, 0), (0, 1), (1, 1), (2, 1), (3, 0), (3, 1)]
-        n_units = len(units)
-        front_order = [0, 1, 2, 6, 3, 4, 5, 7]
-        xq, vq = {}, {}
-        z = keep.tile([P, n_units, JH], F32, name="z")
-        cd = keep.tile([P, n_units, JH], F32, name="cd")
-        zh = keep.tile([P, n_units, JH], F32, name="zh")
-        pre = keep.tile([P, n_units, JH], F32, name="pre")
-        diff = keep.tile([P, n_units, JH], F32, name="diff")
-        pre_pair = keep.tile([P, 2, JH], F32, name="pre_pair", align_bytes=64)
-        state = keep.tile([P, CHUNKS, J], F32, name="state")
-        zh_row = [zh[:, u, :] for u in range(n_units)]
-        pre_row = [pre_pair[:, u, :] if u < 2 else pre[:, u, :] for u in range(n_units)]
-        state_row = [state[:, c, h * JH : (h + 1) * JH] for c, h in units]
-        state_row[0], state_row[3] = zh[:, 0, :], zh[:, 2, :]
+        def banks(u):
+            turn = MATMUL_ORDER.index(u)
+            return [group[turn % len(group)] for group in (sz_bank, hn_bank, xn_bank)]
 
-        def front(u):
-            c, h = units[u]
-            turn = front_order.index(u)
+        def unit_rows(name):
+            tile = keep.tile([P, len(UNITS), JH], F32, name=name)
+            return [tile[:, u, :] for u in range(len(UNITS))]
+
+        xq, vq = {}, {}
+        z = unit_rows("z")
+        cd = unit_rows("cd")
+        zh = unit_rows("zh")
+        pre = unit_rows("pre")
+        spare = unit_rows("spare")
+        pre_then_x = keep.tile([P, 2, JH], F32, name="pre_then_x", align_bytes=64)
+        pre[0], pre[1] = pre_then_x[:, 0, :], pre_then_x[:, 1, :]
+        picked = keep.tile([P, CHUNKS - 1, J], F32, name="picked")
+        state = [picked[:, c - 1, h * JH : (h + 1) * JH] if c else zh[2 * h] for c, h in UNITS]
+        hn_part, xn_part = list(zh), list(pre)
+
+        def matmuls_and_gate(u):
+            c, h = UNITS[u]
             (xw, xs), (vw, vs) = xq[h], vq[h]
-            sz, hn, xn = sz_bank[turn % 2], hn_bank[turn % 3], xn_bank[turn % 3]
+            sz, hn, xn = banks(u)
             nc.tensor.matmul_mx(out=sz[:], lhsT=fp8_cols(uz_w, c), lhsT_scale=scale_cols(uz_s, c), rhs=vw, rhs_scale=vs, start=True, stop=False)
             nc.tensor.matmul_mx(out=sz[:], lhsT=fp4_cols(wz_w, c), lhsT_scale=scale_cols(wz_s, c), rhs=xw, rhs_scale=xs, start=False, stop=True)
             nc.tensor.matmul_mx(out=hn[:], lhsT=fp8_cols(un_w, c), lhsT_scale=scale_cols(un_s, c), rhs=vw, rhs_scale=vs, start=True, stop=True)
             nc.tensor.matmul_mx(out=xn[:], lhsT=fp4_cols(wn_w, c), lhsT_scale=scale_cols(wn_s, c), rhs=xw, rhs_scale=xs, start=True, stop=True)
-            nc.scalar.activation(z[:, u, :], sz[:], ACT.Sigmoid, bias=bz_sb[:, c : c + 1])
+            nc.scalar.activation(z[u], sz[:], ACT.Sigmoid, bias=bz_sb[:, c : c + 1])
 
-        def leave(u):
-            c = units[u][0]
-            turn = front_order.index(u)
-            hn, xn = hn_bank[turn % 3], xn_bank[turn % 3]
-            if u in PRODUCT_ON_GPSIMD:
-                nc.scalar.copy(zh_row[u], hn[:])
-            else:
-                nc.vector.tensor_tensor(zh_row[u], hn[:], z[:, u, :], ALU.mult)
-            if u in SUM_ON_GPSIMD:
-                nc.scalar.activation(pre_row[u], xn[:], ACT.Identity, bias=o_sb[0][:, 0:1] if u == 5 else 0.0)
-            else:
-                nc.vector.scalar_tensor_tensor(pre_row[u], xn[:], bn_sb[:, c : c + 1], zh_row[u], ALU.add, ALU.add)
-                nc.scalar.activation(cd[:, u, :], pre_row[u], ACT.Tanh)
+        def early_candidate(u):
+            c = UNITS[u][0]
+            hn, xn = banks(u)[1:]
+            nc.vector.tensor_tensor(zh[u], hn[:], z[u], ALU.mult)
+            nc.vector.scalar_tensor_tensor(pre[u], xn[:], bn_sb[:, c : c + 1], zh[u], ALU.add, ALU.add)
+            nc.scalar.activation(cd[u], pre[u], ACT.Tanh)
+
+        def empty_banks(u, hn_row, xn_row, zero):
+            hn, xn = banks(u)[1:]
+            nc.scalar.copy(hn_row, hn[:])
+            nc.scalar.activation(xn_row, xn[:], ACT.Identity, bias=zero)
+            hn_part[u], xn_part[u] = hn_row, xn_row
 
         def gather_unit(u):
-            c, h = units[u]
-            nc.vector.tensor_copy(state_row[u], h_sb[c][:].indirect(part(h)))
+            c, h = UNITS[u]
+            nc.vector.tensor_copy(state[u], h_sb[c][:].indirect(entries(h)))
 
         def gather_block(c):
-            nc.vector.tensor_copy(state[:, c, :], h_sb[c][:].indirect(offsets[:]))
+            nc.vector.tensor_copy(picked[:, c - 1, :], h_sb[c][:].indirect(offsets[:]))
 
-        def on_gpsimd(dst, a, b, op):
-            nc.gpsimd.tensor_tensor(dst, a, b, op)
-
-        def scatter(u):
-            c, h = units[u]
-            if u == n_units - 1:
-                nc.vector.tensor_tensor(o_sb[c][:].indirect(part(h)), cd[:, u, :], wgo_sb[:, h * JH : (h + 1) * JH], ALU.mult)
-            else:
-                nc.vector.tensor_copy(o_sb[c][:].indirect(part(h)), z[:, u, :])
+        def store_if_complete(u):
+            c, h = UNITS[u]
             if h == HALVES - 1:
                 nc.sync.dma_start(out[c * P : (c + 1) * P, :], o_sb[c][:])
+
+        def scatter(u):
+            c, h = UNITS[u]
+            nc.vector.tensor_copy(o_sb[c][:].indirect(entries(h)), z[u])
+            store_if_complete(u)
 
         v_w0 = keep.tile([P, JH], U32, name="v_w0", align_bytes=64)
         v_s0 = keep.tile([P, JH], U8, name="v_s0", align_bytes=64)
         vq[0] = gather_table(0, v_w0, v_s0)
         x_first = reuse.tile([P, 2, JH], F32, name="x_first", align_bytes=64, offset=0)
-        xb0 = as_interleaved(x_first[:])
+        xb0 = as_quantise_input(x_first[:])
         cast_x(0, xb0, nc.vector.tensor_copy, slice(0, CAST_SPLIT))
         cast_x(0, xb0, nc.scalar.copy, slice(CAST_SPLIT, JH))
-        x_w0 = keep.tile([P, JH], U32, name="x_w0", align_bytes=64)
-        xq[0] = quantise_x(0, xb0, x_w0)
+        xq[0] = quantise_x(0, xb0)
         v_w1 = reuse.tile([P, JH], U32, name="v_w1", align_bytes=64, offset=0)
         v_s1 = reuse.tile([P, JH], U8, name="v_s1", align_bytes=64, offset=4 * JH)
         vq[1] = gather_table(1, v_w1, v_s1)
-        o_third = reuse.tile([P, T], F32, name="o_third", align_bytes=64, offset=5 * JH)
+        o_third = reuse.tile([P, T], F32, name="o_third", align_bytes=64, offset=4 * JH + JH)
         nc.gpsimd.memset(o_third[:], 0.0)
         o_sb.extend([o_third, o_sb[0]])
 
-        for u in range(3):
-            front(u)
-            leave(u)
-            if u != 1:
-                gather_unit(0 if u == 0 else 3)
-        front(6)
+        matmuls_and_gate(0)
+        early_candidate(0)
+        gather_unit(0)
+        for u in (1, 2):
+            matmuls_and_gate(u)
+            early_candidate(u)
+        gather_unit(3)
+        matmuls_and_gate(6)
         gather_block(1)
-        xb1 = as_interleaved(pre_pair[:])
+        xb1 = as_quantise_input(pre_then_x[:])
         for a in range(2):
             cast_x(1, xb1, nc.scalar.copy, slice(a * JH // 2, (a + 1) * JH // 2))
-        late_rows = keep.tile([P, 3, JH], F32, name="late_rows", tag="x_raw1")
-        zh_row[6], pre_row[6] = late_rows[:, 0, :], late_rows[:, 1, :]
-        leave(6)
-        x_w1 = keep.tile([P, JH], U32, name="x_w1", align_bytes=64)
-        xq[1] = quantise_x(1, xb1, x_w1)
-        for u in (3, 4, 5):
-            front(u)
-            leave(u)
-        front(7)
+        after_cast = keep.tile([P, 3, JH], F32, name="after_cast", tag="x_raw1")
+        empty_banks(6, after_cast[:, 0, :], after_cast[:, 1, :], 0.0)
+        xq[1] = quantise_x(1, xb1)
+        for u in range(3, LATE_FROM):
+            matmuls_and_gate(u)
+            early_candidate(u)
+        matmuls_and_gate(LATE_FROM)
+        empty_banks(LATE_FROM, zh[LATE_FROM], pre[LATE_FROM], o_sb[0][:, 0:1])
+        matmuls_and_gate(LAST)
         gather_block(2)
         gather_block(3)
 
-        sums = {}
-        cand = [cd[:, u, :] for u in range(n_units)]
+        candidate, tanh_argument = list(cd), {}
+        kept = list(state)
 
-        def candidate(u, dst):
-            if u in PRODUCT_ON_GPSIMD:
-                on_gpsimd(dst, zh_row[u], z[:, u, :], ALU.mult)
-                on_gpsimd(dst, pre_row[u], dst, ALU.add)
-            else:
-                on_gpsimd(dst, pre_row[u], zh_row[u], ALU.add)
-            sums[u] = dst
+        def late_argument(u, dst):
+            nc.gpsimd.tensor_tensor(dst, hn_part[u], z[u], ALU.mult)
+            nc.gpsimd.tensor_tensor(dst, xn_part[u], dst, ALU.add)
+            tanh_argument[u] = dst
 
-        def late_tanh(u, dst):
-            c = units[u][0]
-            cand[u] = dst
-            nc.scalar.activation(dst, sums[u], ACT.Tanh, bias=bn_sb[:, c : c + 1])
+        def late_candidate(u, dst):
+            c = UNITS[u][0]
+            nc.scalar.activation(dst, tanh_argument[u], ACT.Tanh, bias=bn_sb[:, c : c + 1])
+            candidate[u] = dst
 
-        def step(u, dst):
-            on_gpsimd(dst, cand[u], state_row[u], ALU.subtract)
-            on_gpsimd(cd[:, u, :], dst, z[:, u, :], ALU.mult)
+        def step_term(u):
+            nc.gpsimd.tensor_tensor(spare[u], candidate[u], state[u], ALU.subtract)
+            nc.gpsimd.tensor_tensor(cd[u], spare[u], z[u], ALU.mult)
 
-        kept = list(state_row)
-
-        def kept_share(u, dst):
-            rest = {5: weighted_all[:, 2, :], 6: late_rows[:, 2, :], 7: cd[:, 3, :]}.get(u, dst)
-            nc.scalar.activation(rest, z[:, u, :], ACT.Copy, bias=1.0, scale=-1.0)
-            on_gpsimd(dst, rest, state_row[u], ALU.mult)
+        def kept_term(u, one_minus_z, dst):
+            nc.scalar.activation(one_minus_z, z[u], ACT.Copy, bias=1.0, scale=-1.0)
+            nc.gpsimd.tensor_tensor(dst, one_minus_z, state[u], ALU.mult)
             kept[u] = dst
 
-        def new_share(u):
-            on_gpsimd(cd[:, u, :], cand[u], z[:, u, :], ALU.mult)
+        def new_term(u):
+            nc.gpsimd.tensor_tensor(cd[u], candidate[u], z[u], ALU.mult)
 
         w_cols = keep.tile([P, J // P], F32, name="w_cols")
-        weighted_all = keep.tile([P, n_units, JH], F32, name="weighted_all")
-        blocks = range(JH // P)
+        weighted = unit_rows("weighted")
+        blocks = [slice(b * P, (b + 1) * P) for b in range(JH // P)]
+        turn_banks = [sz_bank[0], xn_bank[2], xn_bank[0]]
 
         def turned_sum(u):
-            h = units[u][1]
-            back = xn_bank[2 * (u % 2)][:].rearrange("p (b n) -> p b n", n=P)
-            first = sz_bank[0] if u < 5 else hn_bank[0]
-            turned = [(first if b < 2 else hn_bank[0])[:, b * P : (b + 1) * P] for b in blocks]
-            weighted = weighted_all[:, u, :].rearrange("p (b n) -> p b n", n=P)
-            for b in blocks:
-                cols = slice(b * P, (b + 1) * P)
-                nc.tensor.matmul(turned[b], cd[:, u, cols], ident[:], start=True, stop=False, is_transpose=True)
+            h = UNITS[u][1]
+            first, second, way_back = [turn_banks[(u - 1 + a) % 3] for a in range(3)]
+            turned = [(first, second)[b // 2][:, cols] for b, cols in enumerate(blocks)]
+            for b, cols in enumerate(blocks):
+                nc.tensor.matmul(turned[b], cd[u][:, cols], ident[:], start=True, stop=False, is_transpose=True)
                 nc.tensor.matmul(turned[b], kept[u][:, cols], ident[:], start=False, stop=True, is_transpose=True)
-            for b in blocks:
-                col = h * (JH // P) + b
-                nc.scalar.activation(weighted[:, b, :], turned[b], ACT.Copy, scale=w_cols[:, col : col + 1])
-            for b in blocks:
-                nc.tensor.transpose(back[:, b, :], weighted[:, b, :], ident[:])
-            nc.scalar.copy(z[:, u, :], back.rearrange("p b n -> p (b n)"))
+            for b, cols in enumerate(blocks):
+                col = h * len(blocks) + b
+                nc.scalar.activation(weighted[u][:, cols], turned[b], ACT.Copy, scale=w_cols[:, col : col + 1])
+            for cols in blocks:
+                nc.tensor.transpose(way_back[:, cols], weighted[u][:, cols], ident[:])
+            nc.scalar.copy(z[u], way_back[:])
             scatter(u)
 
         nc.tensor.transpose(hn_bank[2][:, 0:P], wgo_rows[:], ident[:])
         nc.scalar.copy(w_cols[:], hn_bank[2][:, 0 : J // P])
-        new_share(0)
-        kept_share(0, diff[:, 0, :])
-        on_gpsimd(cd[:, 0, :], cd[:, 0, :], kept[0], ALU.add)
-        on_gpsimd(z[:, 0, :], cd[:, 0, :], wgo_sb[:, 0:JH], ALU.mult)
+
+        new_term(0)
+        kept_term(0, spare[0], spare[0])
+        nc.gpsimd.tensor_tensor(cd[0], cd[0], kept[0], ALU.add)
+        nc.gpsimd.tensor_tensor(z[0], cd[0], wgo_sb[:, 0:JH], ALU.mult)
         scatter(0)
         for u in (1, 2):
-            new_share(u)
-            kept_share(u, diff[:, u, :])
+            new_term(u)
+            kept_term(u, spare[u], spare[u])
         turned_sum(1)
         turned_sum(2)
-        zh_row[7], pre_row[7] = weighted_all[:, 1, :], cd[:, 2, :]
-        leave(7)
-        step(3, diff[:, 3, :])
-        step(4, diff[:, 4, :])
-        candidate(5, diff[:, 3, :])
-        candidate(6, diff[:, 4, :])
-        kept_share(5, zh[:, 5, :])
+        empty_banks(LAST, weighted[1], cd[2], 0.0)
+        step_term(3)
+        step_term(4)
+        late_argument(5, spare[3])
+        late_argument(6, spare[4])
+        kept_term(5, weighted[2], zh[5])
         turned_sum(3)
-        late_tanh(5, weighted_all[:, 3, :])
-        new_share(5)
-        kept_share(6, cand[5])
+        late_candidate(5, weighted[3])
+        new_term(5)
+        kept_term(6, after_cast[:, 2, :], candidate[5])
         turned_sum(4)
-        late_tanh(6, weighted_all[:, 4, :])
-        new_share(6)
-        candidate(7, diff[:, 4, :])
-        kept_share(7, cand[6])
+        late_candidate(6, weighted[4])
+        new_term(6)
+        late_argument(LAST, spare[4])
+        kept_term(LAST, cd[3], candidate[6])
         turned_sum(5)
         turned_sum(6)
-        late_tanh(7, weighted_all[:, 6, :])
-        new_share(7)
-        on_gpsimd(cd[:, 7, :], cd[:, 7, :], kept[7], ALU.add)
-        scatter(7)
+        late_candidate(LAST, weighted[6])
+        new_term(LAST)
+        nc.gpsimd.tensor_tensor(cd[LAST], cd[LAST], kept[LAST], ALU.add)
+        c, h = UNITS[LAST]
+        nc.vector.tensor_tensor(o_sb[c][:].indirect(entries(h)), cd[LAST], wgo_sb[:, h * JH : (h + 1) * JH], ALU.mult)
+        store_if_complete(LAST)

@@ -111,6 +111,8 @@ def tile_list_tgn_mgu_kernel(
 
         ident = keep.tile([P, P], F32, name="ident")
         make_identity(nc, ident[:])
+        warm = keep.tile([P, 1], F32, name="warm")
+        nc.scalar.activation(warm[:], o_sb[0][:, 0:1], ACT.Sigmoid)
 
         def entries(h):
             width = JH // LIST_GROUP

@@ -90,13 +90,13 @@ def tile_list_tgn_mgu_kernel(
         load_scale_rows(nc.sync, uz_s, uz_scales, range(QUADRANTS // 2))
         nc.sync.dma_start(x_raw[0][:], x_rows[:, :, 0:JH])
         load_scale_rows(nc.sync, uz_s, uz_scales, range(QUADRANTS // 2, QUADRANTS))
-        load_scale_rows(nc.sync, wz_s, wz_scales, range(QUADRANTS // 2))
+        load_scale_rows(nc.sync, un_s, un_scales, range(QUADRANTS // 2))
         load_words(uz_w, uz_words)
-        nc.sync.dma_start(wz_w[:], wz_words[0].bitcast(I32))
         load_words(un_w, un_words)
-        load_scale_rows(nc.sync, wz_s, wz_scales, range(QUADRANTS // 2, QUADRANTS))
+        nc.sync.dma_start(wz_w[:], wz_words[0].bitcast(I32))
+        load_scale_rows(nc.sync, un_s, un_scales, range(QUADRANTS // 2, QUADRANTS))
         load_bias(bz_sb, bz)
-        load_scale_rows(nc.sync, un_s, un_scales, range(QUADRANTS))
+        load_scale_rows(nc.sync, wz_s, wz_scales, range(QUADRANTS))
         nc.sync.dma_start(wn_w[:], wn_words[0].bitcast(I32))
         load_bias(bn_sb, bn)
         load_state(0)
@@ -236,8 +236,7 @@ def tile_list_tgn_mgu_kernel(
         matmuls_and_gate(6)
         gather_block(1)
         xb1 = as_quantise_input(pre_then_x[:])
-        for a in range(2):
-            cast_x(1, xb1, nc.scalar.copy, slice(a * JH // 2, (a + 1) * JH // 2))
+        cast_x(1, xb1, nc.scalar.copy, slice(0, JH))
         after_cast = keep.tile([P, 3, JH], F32, name="after_cast", tag="x_raw1")
         empty_banks(6, after_cast[:, 0, :], after_cast[:, 1, :], 0.0)
         xq[1] = quantise_x(1, xb1)

@@ -24,10 +24,8 @@ JH = 512
 HALVES = J // JH
 CHUNKS = N // P
 LIST_GROUP = 16
-CAST_SPLIT = 336
-UNITS = [(0, 0), (1, 0), (2, 0), (0, 1), (1, 1), (2, 1), (3, 0), (3, 1)]
-MATMUL_ORDER = sorted(range(len(UNITS)), key=lambda u: UNITS[u][1])
-LATE_FROM = 5
+XP = 256
+UNITS = [(2 * b + c, h) for b in range(CHUNKS // 2) for h in range(HALVES) for c in range(2)]
 LAST = len(UNITS) - 1
 
 
@@ -38,7 +36,6 @@ def tile_list_tgn_mgu_kernel(
     nc = tc.nc
     with ExitStack() as ctx:
         keep = ctx.enter_context(tc.tile_pool(name="keep", bufs=1))
-        reuse = ctx.enter_context(tc.tile_pool(name="reuse", bufs=1))
         psum = ctx.enter_context(tc.psum_pool(name="psum", bufs=1))
 
         offsets = keep.tile([P, J // LIST_GROUP], U16, name="offsets")
@@ -53,9 +50,9 @@ def tile_list_tgn_mgu_kernel(
         wn_w = keep.tile([P, N // 2], I32, name="wn_w", align_bytes=64)
         un_w = keep.tile([P, N], I32, name="un_w", align_bytes=64)
         x_rows = x.rearrange("(p i) j -> p i j", i=PACK)
-        x_raw = [keep.tile([P, PACK, JH], F32, name=f"x_raw{h}", tag=f"x_raw{h}") for h in range(HALVES)]
-        h_sb = [keep.tile([P, T], F32, name=f"h_sb{c}") for c in range(CHUNKS)]
-        wgo_sb = keep.tile([P, J], F32, name="wgo_sb")
+        x_raw = [keep.tile([P, PACK, XP], F32, name=f"x_raw{a}", tag=f"x_raw{a}") for a in range(J // XP)]
+        h_sb = [keep.tile([P, T], F32, name=f"h_sb{c}", tag=f"h_sb{c}") for c in range(CHUNKS)]
+        wgo_last = keep.tile([P, JH], F32, name="wgo_last")
         wgo_rows = keep.tile([P, P], F32, name="wgo_rows")
         bz_sb = keep.tile([P, CHUNKS], F32, name="bz_sb")
         bn_sb = keep.tile([P, CHUNKS], F32, name="bn_sb")
@@ -79,35 +76,38 @@ def tile_list_tgn_mgu_kernel(
         def load_state(c):
             nc.sync.dma_start(h_sb[c][:], hT[c * P : (c + 1) * P, :])
 
-        o_sb = [keep.tile([P, T], F32, name=f"o_sb{c}") for c in range(2)]
+        def load_x(a):
+            nc.sync.dma_start(x_raw[a][:], x_rows[:, :, a * XP : (a + 1) * XP])
+
+        o_sb = [keep.tile([P, T], F32, name=f"o_sb{c}") for c in range(3)]
         zero_on_vector(tab_s, 0)
         zero_on_vector(weight_s, 0)
         zero_on_vector(o_sb[0], 0.0)
         nc.gpsimd.memset(o_sb[1][:], 0.0)
 
         load_words(tab_w, tab_words)
-        load_scale_rows(nc.sync, tab_s, tab_scales, range(QUADRANTS))
-        load_scale_rows(nc.sync, uz_s, uz_scales, range(QUADRANTS // 2))
-        nc.sync.dma_start(x_raw[0][:], x_rows[:, :, 0:JH])
-        load_scale_rows(nc.sync, uz_s, uz_scales, range(QUADRANTS // 2, QUADRANTS))
-        load_scale_rows(nc.sync, un_s, un_scales, range(QUADRANTS // 2))
+        load_scale_rows(nc.sync, tab_s, tab_scales, range(0, 4))
+        load_x(0)
+        load_x(1)
         load_words(uz_w, uz_words)
-        load_words(un_w, un_words)
         nc.sync.dma_start(wz_w[:], wz_words[0].bitcast(I32))
-        load_scale_rows(nc.sync, un_s, un_scales, range(QUADRANTS // 2, QUADRANTS))
-        load_bias(bz_sb, bz)
-        load_scale_rows(nc.sync, wz_s, wz_scales, range(QUADRANTS))
-        nc.sync.dma_start(wn_w[:], wn_words[0].bitcast(I32))
-        load_bias(bn_sb, bn)
+        load_scale_rows(nc.sync, uz_s, uz_scales, range(0, 4))
         load_state(0)
+        load_scale_rows(nc.sync, wz_s, wz_scales, range(0, 4))
+        load_words(un_w, un_words)
+        load_bias(bz_sb, bz)
+        nc.sync.dma_start(wn_w[:], wn_words[0].bitcast(I32))
+        load_scale_rows(nc.sync, wn_s, wn_scales, range(0, 4))
+        load_bias(bn_sb, bn)
         load_state(1)
-        nc.sync.dma_start(x_raw[1][:], x_rows[:, :, JH:J])
-        nc.sync.dma_start(wgo_sb[:, 0:JH], wgo[:, 0:JH])
+        load_x(2)
+        load_x(3)
+        nc.sync.dma_start(wgo_rows[:], wgo[0 : P * P // J, :].rearrange("a (b j) -> (a b) j", j=P))
         load_state(2)
         load_state(3)
-        nc.sync.dma_start(wgo_rows[:], wgo[0 : P * P // J, :].rearrange("a (b j) -> (a b) j", j=P))
-        nc.sync.dma_start(wgo_sb[:, JH:J], wgo[:, JH:J])
-        load_scale_rows(nc.gpsimd, wn_s, wn_scales, range(QUADRANTS))
+        nc.sync.dma_start(wgo_last[:], wgo[:, JH:J])
+        load_scale_rows(nc.gpsimd, un_s, un_scales, range(0, 4))
+        nc.gpsimd.memset(o_sb[2][:], 0.0)
 
         ident = keep.tile([P, P], F32, name="ident")
         make_identity(nc, ident[:])
@@ -118,24 +118,26 @@ def tile_list_tgn_mgu_kernel(
             width = JH // LIST_GROUP
             return offsets[:, h * width : (h + 1) * width]
 
-        def gather_table(h, words, scales):
+        def gather_words(h):
+            words = keep.tile([P, JH], U32, name=f"v_w{h}", align_bytes=64)
             nc.vector.tensor_copy(words[:], tab_w[:].bitcast(U32).indirect(entries(h)))
+            return words[:].bitcast(FP8X4)
+
+        def gather_scales(h, scales):
             nc.vector.tensor_copy(scales[:], tab_s[:].bitcast(U8).indirect(entries(h)))
-            return words[:].bitcast(FP8X4), scales[:]
+            return scales[:]
 
-        def as_quantise_input(rows):
-            return rows.rearrange("p a j -> p (a j)").bitcast(BF16).rearrange("p (j i) -> p j i", i=PACK)
-
-        def cast_x(h, xb, copy, cols):
+        def cast_x(a, xb, copy):
+            cols = slice((a * XP) % JH, (a * XP) % JH + XP)
             copy(
                 out=xb[:, cols, :].rearrange("p (a b) i -> p a i b", b=4),
-                in_=x_raw[h][:, :, cols].rearrange("p i (a b) -> p a i b", b=4),
+                in_=x_raw[a][:].rearrange("p i (a b) -> p a i b", b=4),
             )
 
         def quantise_x(h, xb):
             words = keep.tile([P, JH], U32, name=f"x_w{h}", align_bytes=64)
             scales = keep.tile([P, JH], U8, name=f"x_s{h}", align_bytes=64)
-            nc.vector.quantize_mx(out=words[:].bitcast(FP8X4), scales=scales[:], in_=xb.rearrange("p j i -> p (j i)"))
+            nc.vector.quantize_mx(out=words[:].bitcast(FP8X4), scales=scales[:], in_=xb[:].rearrange("p j i -> p (j i)"))
             return words[:].bitcast(FP8X4), scales[:]
 
         def fp4_cols(words, c):
@@ -147,186 +149,167 @@ def tile_list_tgn_mgu_kernel(
         def scale_cols(scales, c):
             return scales[:, (P // 4) * c : (P // 4) * (c + 1)].bitcast(U8)
 
-        sz_bank = [psum.tile([P, JH], F32, name=f"sz{i}") for i in range(2)]
-        hn_bank = [psum.tile([P, JH], F32, name=f"hn{i}") for i in range(3)]
-        xn_bank = [psum.tile([P, JH], F32, name=f"xn{i}") for i in range(3)]
+        bank = [psum.tile([P, JH], F32, name=f"bank{i}") for i in range(8)]
+        turns = [CHUNKS * h + c for c, h in UNITS]
+        sz_bank = [bank[m % 2] for m in turns]
+        hn_bank = [bank[2 + m % 3] for m in turns]
+        xn_bank = [bank[5 + m % 3] for m in turns[:6]] + [bank[6], bank[6]]
 
-        def banks(u):
-            turn = MATMUL_ORDER.index(u)
-            return [group[turn % len(group)] for group in (sz_bank, hn_bank, xn_bank)]
-
-        def unit_rows(name):
-            tile = keep.tile([P, len(UNITS), JH], F32, name=name)
-            return [tile[:, u, :] for u in range(len(UNITS))]
+        def rows(name, count, tag=None):
+            return keep.tile([P, count, JH], F32, name=name, tag=tag or name)
 
         xq, vq = {}, {}
-        z = unit_rows("z")
-        cd = unit_rows("cd")
-        zh = unit_rows("zh")
-        pre = unit_rows("pre")
-        spare = unit_rows("spare")
-        pre_then_x = keep.tile([P, 2, JH], F32, name="pre_then_x", align_bytes=64)
-        pre[0], pre[1] = pre_then_x[:, 0, :], pre_then_x[:, 1, :]
-        picked = keep.tile([P, CHUNKS - 1, J], F32, name="picked")
-        state = [picked[:, c - 1, h * JH : (h + 1) * JH] if c else zh[2 * h] for c, h in UNITS]
-        hn_part, xn_part = list(zh), list(pre)
+        z = rows("z", 8)
+        pre = rows("pre", 4)
+        picked = keep.tile([P, CHUNKS, J], F32, name="picked")
 
-        def matmuls_and_gate(u):
+        def state(u, count=1):
             c, h = UNITS[u]
-            (xw, xs), (vw, vs) = xq[h], vq[h]
-            sz, hn, xn = banks(u)
-            nc.tensor.matmul_mx(out=sz[:], lhsT=fp8_cols(uz_w, c), lhsT_scale=scale_cols(uz_s, c), rhs=vw, rhs_scale=vs, start=True, stop=False)
-            nc.tensor.matmul_mx(out=sz[:], lhsT=fp4_cols(wz_w, c), lhsT_scale=scale_cols(wz_s, c), rhs=xw, rhs_scale=xs, start=False, stop=True)
-            nc.tensor.matmul_mx(out=hn[:], lhsT=fp8_cols(un_w, c), lhsT_scale=scale_cols(un_s, c), rhs=vw, rhs_scale=vs, start=True, stop=True)
-            nc.tensor.matmul_mx(out=xn[:], lhsT=fp4_cols(wn_w, c), lhsT_scale=scale_cols(wn_s, c), rhs=xw, rhs_scale=xs, start=True, stop=True)
-            nc.scalar.activation(z[u], sz[:], ACT.Sigmoid, bias=bz_sb[:, c : c + 1])
+            return picked[:, c : c + count, h * JH : (h + 1) * JH]
 
-        def early_candidate(u):
+        def mx(dst, lw, ls, operand, start, stop):
+            nc.tensor.matmul_mx(out=dst[:], lhsT=lw, lhsT_scale=ls, rhs=operand[0], rhs_scale=operand[1], start=start, stop=stop)
+
+        def gate(u):
+            c, h = UNITS[u]
+            mx(sz_bank[u], fp8_cols(uz_w, c), scale_cols(uz_s, c), vq[h], True, False)
+            mx(sz_bank[u], fp4_cols(wz_w, c), scale_cols(wz_s, c), xq[h], False, True)
+            mx(hn_bank[u], fp8_cols(un_w, c), scale_cols(un_s, c), vq[h], True, True)
+            nc.scalar.activation(z[:, u, :], sz_bank[u][:], ACT.Sigmoid, bias=bz_sb[:, c : c + 1])
+
+        def message(u):
+            c, h = UNITS[u]
+            mx(xn_bank[u], fp4_cols(wn_w, c), scale_cols(wn_s, c), xq[h], True, True)
+
+        def empty_message(u, dst):
             c = UNITS[u][0]
-            hn, xn = banks(u)[1:]
-            nc.vector.tensor_tensor(zh[u], hn[:], z[u], ALU.mult)
-            nc.vector.scalar_tensor_tensor(pre[u], xn[:], bn_sb[:, c : c + 1], zh[u], ALU.add, ALU.add)
-            nc.scalar.activation(cd[u], pre[u], ACT.Tanh)
+            message(u)
+            nc.scalar.activation(dst, xn_bank[u][:], ACT.Identity, bias=bn_sb[:, c : c + 1])
 
-        def empty_banks(u, hn_row, xn_row, zero):
-            hn, xn = banks(u)[1:]
-            nc.scalar.copy(hn_row, hn[:])
-            nc.scalar.activation(xn_row, xn[:], ACT.Identity, bias=zero)
-            hn_part[u], xn_part[u] = hn_row, xn_row
-
-        def gather_unit(u):
-            c, h = UNITS[u]
-            nc.vector.tensor_copy(state[u], h_sb[c][:].indirect(entries(h)))
+        def gated(u, dst):
+            nc.vector.tensor_tensor(dst, hn_bank[u][:], z[:, u, :], ALU.mult)
 
         def gather_block(c):
-            nc.vector.tensor_copy(picked[:, c - 1, :], h_sb[c][:].indirect(offsets[:]))
+            nc.vector.tensor_copy(picked[:, c, :], h_sb[c][:].indirect(offsets[:]))
 
         def store_if_complete(u):
             c, h = UNITS[u]
             if h == HALVES - 1:
-                nc.sync.dma_start(out[c * P : (c + 1) * P, :], o_sb[c][:])
+                nc.sync.dma_start(out[c * P : (c + 1) * P, :], o_sb[c % 3][:])
 
-        def scatter(u):
-            c, h = UNITS[u]
-            nc.vector.tensor_copy(o_sb[c][:].indirect(entries(h)), z[u])
-            store_if_complete(u)
+        for h in range(HALVES):
+            words = gather_words(h)
+            vq[h] = (words, gather_scales(h, keep.tile([P, JH], U8, name=f"v_s{h}", align_bytes=64)))
+        xb = [keep.tile([P, JH, PACK], BF16, name=f"xb{h}", tag=f"xb{h}", align_bytes=64) for h in range(HALVES)]
+        cast_x(0, xb[0], nc.scalar.copy)
+        cast_x(1, xb[0], nc.scalar.copy)
+        xq[0] = quantise_x(0, xb[0])
 
-        v_w0 = keep.tile([P, JH], U32, name="v_w0", align_bytes=64)
-        v_s0 = keep.tile([P, JH], U8, name="v_s0", align_bytes=64)
-        vq[0] = gather_table(0, v_w0, v_s0)
-        x_first = reuse.tile([P, 2, JH], F32, name="x_first", align_bytes=64, offset=0)
-        xb0 = as_quantise_input(x_first[:])
-        cast_x(0, xb0, nc.vector.tensor_copy, slice(0, CAST_SPLIT))
-        cast_x(0, xb0, nc.scalar.copy, slice(CAST_SPLIT, JH))
-        xq[0] = quantise_x(0, xb0)
-        v_w1 = reuse.tile([P, JH], U32, name="v_w1", align_bytes=64, offset=0)
-        v_s1 = reuse.tile([P, JH], U8, name="v_s1", align_bytes=64, offset=4 * JH)
-        vq[1] = gather_table(1, v_w1, v_s1)
-        o_third = reuse.tile([P, T], F32, name="o_third", align_bytes=64, offset=4 * JH + JH)
-        nc.gpsimd.memset(o_third[:], 0.0)
-        o_sb.extend([o_third, o_sb[0]])
+        def pair(tile, u):
+            return tile[:, u : u + 2, :]
 
-        matmuls_and_gate(0)
-        early_candidate(0)
-        gather_unit(0)
-        for u in (1, 2):
-            matmuls_and_gate(u)
-            early_candidate(u)
-        gather_unit(3)
-        matmuls_and_gate(6)
-        gather_block(1)
-        xb1 = as_quantise_input(pre_then_x[:])
-        cast_x(1, xb1, nc.scalar.copy, slice(0, JH))
-        after_cast = keep.tile([P, 3, JH], F32, name="after_cast", tag="x_raw1")
-        empty_banks(6, after_cast[:, 0, :], after_cast[:, 1, :], 0.0)
-        xq[1] = quantise_x(1, xb1)
-        for u in range(3, LATE_FROM):
-            matmuls_and_gate(u)
-            early_candidate(u)
-        matmuls_and_gate(LATE_FROM)
-        empty_banks(LATE_FROM, zh[LATE_FROM], pre[LATE_FROM], o_sb[0][:, 0:1])
-        matmuls_and_gate(LAST)
-        gather_block(2)
-        gather_block(3)
-
-        candidate, tanh_argument = list(cd), {}
-        kept = list(state)
-
-        def late_argument(u, dst):
-            nc.gpsimd.tensor_tensor(dst, hn_part[u], z[u], ALU.mult)
-            nc.gpsimd.tensor_tensor(dst, xn_part[u], dst, ALU.add)
-            tanh_argument[u] = dst
-
-        def late_candidate(u, dst):
+        def candidate(u, t_row):
             c = UNITS[u][0]
-            nc.scalar.activation(dst, tanh_argument[u], ACT.Tanh, bias=bn_sb[:, c : c + 1])
-            candidate[u] = dst
+            gate(u)
+            message(u)
+            gated(u, t_row)
+            nc.vector.tensor_tensor(pre[:, u, :], xn_bank[u][:], t_row, ALU.add)
+            nc.scalar.activation(t_row, pre[:, u, :], ACT.Tanh, bias=bn_sb[:, c : c + 1])
 
-        def step_term(u):
-            nc.gpsimd.tensor_tensor(spare[u], candidate[u], state[u], ALU.subtract)
-            nc.gpsimd.tensor_tensor(cd[u], spare[u], z[u], ALU.mult)
+        def step(dst, cand, h_rows, z_rows):
+            nc.gpsimd.tensor_tensor(dst, cand, h_rows, ALU.subtract)
+            nc.gpsimd.tensor_tensor(dst, dst, z_rows, ALU.mult)
 
-        def kept_term(u, one_minus_z, dst):
-            nc.scalar.activation(one_minus_z, z[u], ACT.Copy, bias=1.0, scale=-1.0)
-            nc.gpsimd.tensor_tensor(dst, one_minus_z, state[u], ALU.mult)
-            kept[u] = dst
-
-        def new_term(u):
-            nc.gpsimd.tensor_tensor(cd[u], candidate[u], z[u], ALU.mult)
+        gather_block(0)
+        t0 = rows("t0", 2)
+        candidate(0, t0[:, 0, :])
+        candidate(1, t0[:, 1, :])
+        step(t0[:, 0, :], t0[:, 0, :], state(0)[:, 0, :], z[:, 0, :])
+        gather_block(1)
+        t1 = rows("t1", 2, tag="h_sb1")
+        for u in (4, 5):
+            gate(u)
+            gated(u, t1[:, u - 4, :])
+        cast_x(2, xb[1], nc.scalar.copy)
+        cast_x(3, xb[1], nc.scalar.copy)
+        xq[1] = quantise_x(1, xb[1])
+        xn45 = rows("xn45", 2, tag="x_raw3")
+        for u in (4, 5):
+            empty_message(u, xn45[:, u - 4, :])
+        after_x = keep.tile([P, 1, JH], F32, name="after_x", tag="xb1", align_bytes=64)
+        e1 = after_x[:, 0, :]
+        step(e1, t0[:, 1, :], state(1)[:, 0, :], z[:, 1, :])
+        pre45 = pair(z, 0)
+        nc.gpsimd.tensor_tensor(pre45, xn45[:], t1[:], ALU.add)
+        gather_block(2)
+        e23 = rows("e23", 2, tag="h_sb2")
+        candidate(2, e23[:, 0, :])
+        candidate(3, e23[:, 1, :])
+        step(e23[:], e23[:], state(2, 2), pair(z, 2))
+        gather_block(3)
+        late = rows("late", 2, tag="h_sb3")
+        for u in (6, 7):
+            gate(u)
+            nc.vector.scalar_tensor_tensor(
+                late[:, u - 6, :], hn_bank[u][:], o_sb[u - 6][:, 0:1], z[:, u, :], ALU.add, ALU.mult
+            )
 
         w_cols = keep.tile([P, J // P], F32, name="w_cols")
-        weighted = unit_rows("weighted")
+        nc.tensor.transpose(bank[5][:, 0:P], wgo_rows[:], ident[:])
+        nc.scalar.copy(w_cols[:], bank[5][:, 0 : J // P])
+        weighted = rows("weighted", LAST + 1)
+        w_row = [0, 1, 2, 7, 4, 5, 6]
+        result = rows("result", LAST)
         blocks = [slice(b * P, (b + 1) * P) for b in range(JH // P)]
-        turn_banks = [sz_bank[0], xn_bank[2], xn_bank[0]]
+        turn_banks = [[bank[0], bank[1], bank[5]]]
+        for u in range(1, LAST):
+            first, second, way_back = turn_banks[-1]
+            if u % 2:
+                turn_banks.append([second, second, first])
+            else:
+                turn_banks.append([second, way_back, bank[5]])
 
-        def turned_sum(u):
-            h = UNITS[u][1]
-            first, second, way_back = [turn_banks[(u - 1 + a) % 3] for a in range(3)]
+        def turned_sum(u, step):
+            c, h = UNITS[u]
+            kept = picked[:, c, h * JH : (h + 1) * JH]
+            first, second, way_back = turn_banks[u]
             turned = [(first, second)[b // 2][:, cols] for b, cols in enumerate(blocks)]
             for b, cols in enumerate(blocks):
-                nc.tensor.matmul(turned[b], cd[u][:, cols], ident[:], start=True, stop=False, is_transpose=True)
-                nc.tensor.matmul(turned[b], kept[u][:, cols], ident[:], start=False, stop=True, is_transpose=True)
+                nc.tensor.matmul(turned[b], step[:, cols], ident[:], start=True, stop=False, is_transpose=True)
+                nc.tensor.matmul(turned[b], kept[:, cols], ident[:], start=False, stop=True, is_transpose=True)
             for b, cols in enumerate(blocks):
                 col = h * len(blocks) + b
-                nc.scalar.activation(weighted[u][:, cols], turned[b], ACT.Copy, scale=w_cols[:, col : col + 1])
+                nc.scalar.activation(weighted[:, w_row[u], cols], turned[b], ACT.Copy, scale=w_cols[:, col : col + 1])
             for cols in blocks:
-                nc.tensor.transpose(way_back[:, cols], weighted[u][:, cols], ident[:])
-            nc.scalar.copy(z[u], way_back[:])
-            scatter(u)
+                nc.tensor.transpose(way_back[:, cols], weighted[:, w_row[u], cols], ident[:])
+            nc.scalar.copy(result[:, u, :], way_back[:])
+            nc.vector.tensor_copy(o_sb[c % 3][:].indirect(entries(h)), result[:, u, :])
+            store_if_complete(u)
 
-        nc.tensor.transpose(hn_bank[2][:, 0:P], wgo_rows[:], ident[:])
-        nc.scalar.copy(w_cols[:], hn_bank[2][:, 0 : J // P])
-
-        new_term(0)
-        kept_term(0, spare[0], spare[0])
-        nc.gpsimd.tensor_tensor(cd[0], cd[0], kept[0], ALU.add)
-        nc.gpsimd.tensor_tensor(z[0], cd[0], wgo_sb[:, 0:JH], ALU.mult)
-        scatter(0)
-        for u in (1, 2):
-            new_term(u)
-            kept_term(u, spare[u], spare[u])
-        turned_sum(1)
-        turned_sum(2)
-        empty_banks(LAST, weighted[1], cd[2], 0.0)
-        step_term(3)
-        step_term(4)
-        late_argument(5, spare[3])
-        late_argument(6, spare[4])
-        kept_term(5, weighted[2], zh[5])
-        turned_sum(3)
-        late_candidate(5, weighted[3])
-        new_term(5)
-        kept_term(6, after_cast[:, 2, :], candidate[5])
-        turned_sum(4)
-        late_candidate(6, weighted[4])
-        new_term(6)
-        late_argument(LAST, spare[4])
-        kept_term(LAST, cd[3], candidate[6])
-        turned_sum(5)
-        turned_sum(6)
-        late_candidate(LAST, weighted[6])
-        new_term(LAST)
-        nc.gpsimd.tensor_tensor(cd[LAST], cd[LAST], kept[LAST], ALU.add)
+        turned_sum(0, t0[:, 0, :])
+        turned_sum(1, e1)
+        e45 = pair(weighted, 0)
+        nc.scalar.activation(e45, pre45, ACT.Tanh)
+        step(e45, e45, state(4, 2), pair(z, 4))
+        turned_sum(2, e23[:, 0, :])
+        xn67 = pair(weighted, 2)
+        for u in (6, 7):
+            empty_message(u, xn67[:, u - 6, :])
+        turned_sum(3, e23[:, 1, :])
+        pre67 = pair(z, 4)
+        nc.gpsimd.tensor_tensor(pre67, xn67, late[:], ALU.add)
+        turned_sum(4, e45[:, 0, :])
+        e6 = weighted[:, 4, :]
+        nc.scalar.activation(e6, pre67[:, 0, :], ACT.Tanh)
+        nc.scalar.activation(pre67[:, 0, :], pre67[:, 1, :], ACT.Tanh)
+        step(e6, e6, state(6)[:, 0, :], z[:, 6, :])
+        turned_sum(5, e45[:, 1, :])
+        h7 = state(LAST)[:, 0, :]
+        nc.gpsimd.tensor_tensor(z[:, 6, :], pre67[:, 0, :], h7, ALU.subtract)
+        turned_sum(6, e6)
+        s7 = weighted[:, 6, :]
+        nc.gpsimd.tensor_tensor(s7, z[:, 6, :], z[:, LAST, :], ALU.mult)
+        nc.gpsimd.tensor_tensor(s7, s7, h7, ALU.add)
         c, h = UNITS[LAST]
-        nc.vector.tensor_tensor(o_sb[c][:].indirect(entries(h)), cd[LAST], wgo_sb[:, h * JH : (h + 1) * JH], ALU.mult)
+        nc.vector.tensor_tensor(o_sb[c % 3][:].indirect(entries(h)), s7, wgo_last[:], ALU.mult)
         store_if_complete(LAST)

@@ -36,6 +36,7 @@ def tile_list_tgn_mgu_kernel(
     nc = tc.nc
     with ExitStack() as ctx:
         keep = ctx.enter_context(tc.tile_pool(name="keep", bufs=1))
+        reuse = ctx.enter_context(tc.tile_pool(name="reuse", bufs=1))
         psum = ctx.enter_context(tc.psum_pool(name="psum", bufs=1))
 
         offsets = keep.tile([P, J // LIST_GROUP], U16, name="offsets")
@@ -79,11 +80,10 @@ def tile_list_tgn_mgu_kernel(
         def load_x(a):
             nc.sync.dma_start(x_raw[a][:], x_rows[:, :, a * XP : (a + 1) * XP])
 
-        o_sb = [keep.tile([P, T], F32, name=f"o_sb{c}") for c in range(3)]
-        zero_on_vector(tab_s, 0)
+        o_sb = [keep.tile([P, T], F32, name="o_sb0")]
         zero_on_vector(weight_s, 0)
+        zero_on_vector(tab_s, 0)
         zero_on_vector(o_sb[0], 0.0)
-        nc.gpsimd.memset(o_sb[1][:], 0.0)
 
         load_words(tab_w, tab_words)
         load_scale_rows(nc.sync, tab_s, tab_scales, range(0, 4))
@@ -107,7 +107,6 @@ def tile_list_tgn_mgu_kernel(
         load_state(3)
         nc.sync.dma_start(wgo_last[:], wgo[:, JH:J])
         load_scale_rows(nc.gpsimd, un_s, un_scales, range(0, 4))
-        nc.gpsimd.memset(o_sb[2][:], 0.0)
 
         ident = keep.tile([P, P], F32, name="ident")
         make_identity(nc, ident[:])
@@ -153,7 +152,7 @@ def tile_list_tgn_mgu_kernel(
         turns = [CHUNKS * h + c for c, h in UNITS]
         sz_bank = [bank[m % 2] for m in turns]
         hn_bank = [bank[2 + m % 3] for m in turns]
-        xn_bank = [bank[5 + m % 3] for m in turns[:6]] + [bank[6], bank[6]]
+        xn_bank = [bank[5 + m % 3] for m in turns[:6]] + bank[6:8]
 
         def rows(name, count, tag=None):
             return keep.tile([P, count, JH], F32, name=name, tag=tag or name)
@@ -200,10 +199,16 @@ def tile_list_tgn_mgu_kernel(
         for h in range(HALVES):
             words = gather_words(h)
             vq[h] = (words, gather_scales(h, keep.tile([P, JH], U8, name=f"v_s{h}", align_bytes=64)))
-        xb = [keep.tile([P, JH, PACK], BF16, name=f"xb{h}", tag=f"xb{h}", align_bytes=64) for h in range(HALVES)]
+        xb = [
+            reuse.tile([P, JH, PACK], BF16, name="xb0", align_bytes=64, offset=4 * T - 4 * JH),
+            keep.tile([P, JH, PACK], BF16, name="xb1", tag="xb1", align_bytes=64),
+        ]
         cast_x(0, xb[0], nc.scalar.copy)
         cast_x(1, xb[0], nc.scalar.copy)
         xq[0] = quantise_x(0, xb[0])
+        for a in range(2):
+            o_sb.append(reuse.tile([P, T], F32, name=f"o_late{a}", align_bytes=64, offset=4 * T * a))
+            nc.gpsimd.memset(o_sb[-1][:], 0.0)
 
         def pair(tile, u):
             return tile[:, u : u + 2, :]
@@ -245,7 +250,9 @@ def tile_list_tgn_mgu_kernel(
         e23 = rows("e23", 2, tag="h_sb2")
         candidate(2, e23[:, 0, :])
         candidate(3, e23[:, 1, :])
-        step(e23[:], e23[:], state(2, 2), pair(z, 2))
+        nc.gpsimd.tensor_tensor(e23[:], e23[:], state(2, 2), ALU.subtract)
+        for u in (2, 3):
+            nc.gpsimd.tensor_tensor(e23[:, u - 2, :], e23[:, u - 2, :], z[:, u, :], ALU.mult)
         gather_block(3)
         late = rows("late", 2, tag="h_sb3")
         for u in (6, 7):
@@ -258,58 +265,56 @@ def tile_list_tgn_mgu_kernel(
         nc.tensor.transpose(bank[5][:, 0:P], wgo_rows[:], ident[:])
         nc.scalar.copy(w_cols[:], bank[5][:, 0 : J // P])
         weighted = rows("weighted", LAST + 1)
-        w_row = [0, 1, 2, 7, 4, 5, 6]
         result = rows("result", LAST)
         blocks = [slice(b * P, (b + 1) * P) for b in range(JH // P)]
-        turn_banks = [[bank[0], bank[1], bank[5]]]
-        for u in range(1, LAST):
-            first, second, way_back = turn_banks[-1]
-            if u % 2:
-                turn_banks.append([second, second, first])
-            else:
-                turn_banks.append([second, way_back, bank[5]])
+        turned, way_back = bank[0], bank[5]
 
-        def turned_sum(u, step):
+        def turned_sum(u, step, kept):
             c, h = UNITS[u]
-            kept = picked[:, c, h * JH : (h + 1) * JH]
-            first, second, way_back = turn_banks[u]
-            turned = [(first, second)[b // 2][:, cols] for b, cols in enumerate(blocks)]
-            for b, cols in enumerate(blocks):
-                nc.tensor.matmul(turned[b], step[:, cols], ident[:], start=True, stop=False, is_transpose=True)
-                nc.tensor.matmul(turned[b], kept[:, cols], ident[:], start=False, stop=True, is_transpose=True)
+            for cols in blocks:
+                nc.tensor.matmul(turned[:, cols], step[:, cols], ident[:], start=True, stop=False, is_transpose=True)
+                nc.tensor.matmul(turned[:, cols], kept[:, cols], ident[:], start=False, stop=True, is_transpose=True)
             for b, cols in enumerate(blocks):
                 col = h * len(blocks) + b
-                nc.scalar.activation(weighted[:, w_row[u], cols], turned[b], ACT.Copy, scale=w_cols[:, col : col + 1])
+                nc.scalar.activation(weighted[:, u, cols], turned[:, cols], ACT.Copy, scale=w_cols[:, col : col + 1])
             for cols in blocks:
-                nc.tensor.transpose(way_back[:, cols], weighted[:, w_row[u], cols], ident[:])
+                nc.tensor.transpose(way_back[:, cols], weighted[:, u, cols], ident[:])
             nc.scalar.copy(result[:, u, :], way_back[:])
             nc.vector.tensor_copy(o_sb[c % 3][:].indirect(entries(h)), result[:, u, :])
             store_if_complete(u)
 
-        turned_sum(0, t0[:, 0, :])
-        turned_sum(1, e1)
-        e45 = pair(weighted, 0)
-        nc.scalar.activation(e45, pre45, ACT.Tanh)
-        step(e45, e45, state(4, 2), pair(z, 4))
-        turned_sum(2, e23[:, 0, :])
-        xn67 = pair(weighted, 2)
-        for u in (6, 7):
-            empty_message(u, xn67[:, u - 6, :])
-        turned_sum(3, e23[:, 1, :])
+        def held(u):
+            return state(u)[:, 0, :]
+
+        turned_sum(0, t0[:, 0, :], held(0))
+        cd45 = weighted[:, 0 : LAST + 1 : LAST, :]
+        nc.scalar.activation(cd45, pre45, ACT.Tanh)
+        turned_sum(1, e1, held(1))
+        empty_message(6, weighted[:, 1, :])
+        d45 = pair(z, 2)
+        nc.gpsimd.tensor_tensor(d45, cd45, state(4, 2), ALU.subtract)
+        for u in (4, 5):
+            nc.gpsimd.tensor_tensor(d45[:, u - 4, :], d45[:, u - 4, :], z[:, u, :], ALU.mult)
+        turned_sum(2, e23[:, 0, :], held(2))
+        empty_message(7, weighted[:, 2, :])
+        turned_sum(3, e23[:, 1, :], held(3))
+        kept6 = weighted[:, 3, :]
+        nc.scalar.activation(kept6, z[:, 6, :], ACT.Copy, bias=1.0, scale=-1.0)
         pre67 = pair(z, 4)
-        nc.gpsimd.tensor_tensor(pre67, xn67, late[:], ALU.add)
-        turned_sum(4, e45[:, 0, :])
-        e6 = weighted[:, 4, :]
-        nc.scalar.activation(e6, pre67[:, 0, :], ACT.Tanh)
-        nc.scalar.activation(pre67[:, 0, :], pre67[:, 1, :], ACT.Tanh)
-        step(e6, e6, state(6)[:, 0, :], z[:, 6, :])
-        turned_sum(5, e45[:, 1, :])
-        h7 = state(LAST)[:, 0, :]
-        nc.gpsimd.tensor_tensor(z[:, 6, :], pre67[:, 0, :], h7, ALU.subtract)
-        turned_sum(6, e6)
+        nc.gpsimd.tensor_tensor(pre67, pair(weighted, 1), late[:], ALU.add)
+        nc.gpsimd.tensor_tensor(late[:, 0, :], kept6, held(6), ALU.mult)
+        turned_sum(4, d45[:, 0, :], held(4))
+        new6 = weighted[:, 4, :]
+        nc.scalar.activation(new6, pre67[:, 0, :], ACT.Tanh)
+        nc.gpsimd.tensor_tensor(new6, new6, z[:, 6, :], ALU.mult)
+        turned_sum(5, d45[:, 1, :], held(5))
+        e7 = weighted[:, 5, :]
+        nc.scalar.activation(e7, pre67[:, 1, :], ACT.Tanh)
+        nc.gpsimd.tensor_tensor(e7, e7, held(LAST), ALU.subtract)
+        turned_sum(6, new6, late[:, 0, :])
         s7 = weighted[:, 6, :]
-        nc.gpsimd.tensor_tensor(s7, z[:, 6, :], z[:, LAST, :], ALU.mult)
-        nc.gpsimd.tensor_tensor(s7, s7, h7, ALU.add)
+        nc.gpsimd.tensor_tensor(s7, e7, z[:, LAST, :], ALU.mult)
+        nc.gpsimd.tensor_tensor(s7, s7, held(LAST), ALU.add)
         c, h = UNITS[LAST]
         nc.vector.tensor_tensor(o_sb[c % 3][:].indirect(entries(h)), s7, wgo_last[:], ALU.mult)
         store_if_complete(LAST)

@@ -25,7 +25,7 @@ HALVES = J // JH
 CHUNKS = N // P
 LIST_GROUP = 16
 XP = 256
-UNITS = [(2 * b + c, h) for b in range(CHUNKS // 2) for h in range(HALVES) for c in range(2)]
+UNITS = [(c, h) for h in range(HALVES) for c in range(CHUNKS)]
 LAST = len(UNITS) - 1
 
 
@@ -80,8 +80,8 @@ def tile_list_tgn_mgu_kernel(
         def load_x(a):
             nc.sync.dma_start(x_raw[a][:], x_rows[:, :, a * XP : (a + 1) * XP])
 
-        o_sb = [keep.tile([P, T], F32, name="o_sb0")]
-        zero_on_vector(weight_s, 0)
+        o_sb = [keep.tile([P, T], F32, name=f"o_sb{c}") for c in range(2)]
+        nc.gpsimd.memset(weight_s[:], 0)
         zero_on_vector(tab_s, 0)
         zero_on_vector(o_sb[0], 0.0)
 
@@ -90,23 +90,24 @@ def tile_list_tgn_mgu_kernel(
         load_x(0)
         load_x(1)
         load_words(uz_w, uz_words)
-        nc.sync.dma_start(wz_w[:], wz_words[0].bitcast(I32))
         load_scale_rows(nc.sync, uz_s, uz_scales, range(0, 4))
         load_state(0)
         load_scale_rows(nc.sync, wz_s, wz_scales, range(0, 4))
-        load_words(un_w, un_words)
+        nc.sync.dma_start(wz_w[:], wz_words[0].bitcast(I32))
         load_bias(bz_sb, bz)
+        load_words(un_w, un_words)
         nc.sync.dma_start(wn_w[:], wn_words[0].bitcast(I32))
         load_scale_rows(nc.sync, wn_s, wn_scales, range(0, 4))
         load_bias(bn_sb, bn)
+        nc.sync.dma_start(wgo_rows[:], wgo[0 : P * P // J, :].rearrange("a (b j) -> (a b) j", j=P))
         load_state(1)
         load_x(2)
         load_x(3)
-        nc.sync.dma_start(wgo_rows[:], wgo[0 : P * P // J, :].rearrange("a (b j) -> (a b) j", j=P))
         load_state(2)
         load_state(3)
         nc.sync.dma_start(wgo_last[:], wgo[:, JH:J])
         load_scale_rows(nc.gpsimd, un_s, un_scales, range(0, 4))
+        nc.gpsimd.memset(o_sb[1][:], 0.0)
 
         ident = keep.tile([P, P], F32, name="ident")
         make_identity(nc, ident[:])
@@ -116,15 +117,6 @@ def tile_list_tgn_mgu_kernel(
         def entries(h):
             width = JH // LIST_GROUP
             return offsets[:, h * width : (h + 1) * width]
-
-        def gather_words(h):
-            words = keep.tile([P, JH], U32, name=f"v_w{h}", align_bytes=64)
-            nc.vector.tensor_copy(words[:], tab_w[:].bitcast(U32).indirect(entries(h)))
-            return words[:].bitcast(FP8X4)
-
-        def gather_scales(h, scales):
-            nc.vector.tensor_copy(scales[:], tab_s[:].bitcast(U8).indirect(entries(h)))
-            return scales[:]
 
         def cast_x(a, xb, copy):
             cols = slice((a * XP) % JH, (a * XP) % JH + XP)
@@ -149,17 +141,17 @@ def tile_list_tgn_mgu_kernel(
             return scales[:, (P // 4) * c : (P // 4) * (c + 1)].bitcast(U8)
 
         bank = [psum.tile([P, JH], F32, name=f"bank{i}") for i in range(8)]
-        turns = [CHUNKS * h + c for c, h in UNITS]
-        sz_bank = [bank[m % 2] for m in turns]
-        hn_bank = [bank[2 + m % 3] for m in turns]
-        xn_bank = [bank[5 + m % 3] for m in turns[:6]] + bank[6:8]
+        sz_bank = [bank[u % 2] for u in range(8)]
+        hn_bank = [bank[2 + u % 3] for u in range(6)] + bank[3:5]
+        xn_bank = [bank[5 + u % 3] for u in range(6)] + bank[6:8]
+        turned, way_back = bank[2], bank[5]
 
         def rows(name, count, tag=None):
             return keep.tile([P, count, JH], F32, name=name, tag=tag or name)
 
         xq, vq = {}, {}
         z = rows("z", 8)
-        pre = rows("pre", 4)
+        pre = rows("pre", 2)
         picked = keep.tile([P, CHUNKS, J], F32, name="picked")
 
         def state(u, count=1):
@@ -173,8 +165,11 @@ def tile_list_tgn_mgu_kernel(
             c, h = UNITS[u]
             mx(sz_bank[u], fp8_cols(uz_w, c), scale_cols(uz_s, c), vq[h], True, False)
             mx(sz_bank[u], fp4_cols(wz_w, c), scale_cols(wz_s, c), xq[h], False, True)
-            mx(hn_bank[u], fp8_cols(un_w, c), scale_cols(un_s, c), vq[h], True, True)
             nc.scalar.activation(z[:, u, :], sz_bank[u][:], ACT.Sigmoid, bias=bz_sb[:, c : c + 1])
+
+        def memory(u):
+            c, h = UNITS[u]
+            mx(hn_bank[u], fp8_cols(un_w, c), scale_cols(un_s, c), vq[h], True, True)
 
         def message(u):
             c, h = UNITS[u]
@@ -194,11 +189,14 @@ def tile_list_tgn_mgu_kernel(
         def store_if_complete(u):
             c, h = UNITS[u]
             if h == HALVES - 1:
-                nc.sync.dma_start(out[c * P : (c + 1) * P, :], o_sb[c % 3][:])
+                nc.sync.dma_start(out[c * P : (c + 1) * P, :], o_sb[c][:])
 
         for h in range(HALVES):
-            words = gather_words(h)
-            vq[h] = (words, gather_scales(h, keep.tile([P, JH], U8, name=f"v_s{h}", align_bytes=64)))
+            words = keep.tile([P, JH], U32, name=f"v_w{h}", align_bytes=64)
+            scales = keep.tile([P, JH], U8, name=f"v_s{h}", align_bytes=64)
+            nc.vector.tensor_copy(words[:], tab_w[:].bitcast(U32).indirect(entries(h)))
+            nc.vector.tensor_copy(scales[:], tab_s[:].bitcast(U8).indirect(entries(h)))
+            vq[h] = (words[:].bitcast(FP8X4), scales[:])
         xb = [
             reuse.tile([P, JH, PACK], BF16, name="xb0", align_bytes=64, offset=4 * T - 4 * JH),
             keep.tile([P, JH, PACK], BF16, name="xb1", tag="xb1", align_bytes=64),
@@ -213,108 +211,148 @@ def tile_list_tgn_mgu_kernel(
         def pair(tile, u):
             return tile[:, u : u + 2, :]
 
+        def held(u):
+            return state(u)[:, 0, :]
+
         def candidate(u, t_row):
             c = UNITS[u][0]
             gate(u)
+            memory(u)
             message(u)
             gated(u, t_row)
             nc.vector.tensor_tensor(pre[:, u, :], xn_bank[u][:], t_row, ALU.add)
             nc.scalar.activation(t_row, pre[:, u, :], ACT.Tanh, bias=bn_sb[:, c : c + 1])
 
-        def step(dst, cand, h_rows, z_rows):
+        def difference(dst, cand, h_rows):
             nc.gpsimd.tensor_tensor(dst, cand, h_rows, ALU.subtract)
-            nc.gpsimd.tensor_tensor(dst, dst, z_rows, ALU.mult)
 
-        gather_block(0)
-        t0 = rows("t0", 2)
-        candidate(0, t0[:, 0, :])
-        candidate(1, t0[:, 1, :])
-        step(t0[:, 0, :], t0[:, 0, :], state(0)[:, 0, :], z[:, 0, :])
-        gather_block(1)
-        t1 = rows("t1", 2, tag="h_sb1")
-        for u in (4, 5):
-            gate(u)
-            gated(u, t1[:, u - 4, :])
-        cast_x(2, xb[1], nc.scalar.copy)
-        cast_x(3, xb[1], nc.scalar.copy)
-        xq[1] = quantise_x(1, xb[1])
-        xn45 = rows("xn45", 2, tag="x_raw3")
-        for u in (4, 5):
-            empty_message(u, xn45[:, u - 4, :])
-        after_x = keep.tile([P, 1, JH], F32, name="after_x", tag="xb1", align_bytes=64)
-        e1 = after_x[:, 0, :]
-        step(e1, t0[:, 1, :], state(1)[:, 0, :], z[:, 1, :])
-        pre45 = pair(z, 0)
-        nc.gpsimd.tensor_tensor(pre45, xn45[:], t1[:], ALU.add)
-        gather_block(2)
-        e23 = rows("e23", 2, tag="h_sb2")
-        candidate(2, e23[:, 0, :])
-        candidate(3, e23[:, 1, :])
-        nc.gpsimd.tensor_tensor(e23[:], e23[:], state(2, 2), ALU.subtract)
-        for u in (2, 3):
-            nc.gpsimd.tensor_tensor(e23[:, u - 2, :], e23[:, u - 2, :], z[:, u, :], ALU.mult)
-        gather_block(3)
-        late = rows("late", 2, tag="h_sb3")
-        for u in (6, 7):
-            gate(u)
-            nc.vector.scalar_tensor_tensor(
-                late[:, u - 6, :], hn_bank[u][:], o_sb[u - 6][:, 0:1], z[:, u, :], ALU.add, ALU.mult
-            )
+        def product(dst, a, b):
+            nc.gpsimd.tensor_tensor(dst, a, b, ALU.mult)
 
         w_cols = keep.tile([P, J // P], F32, name="w_cols")
-        nc.tensor.transpose(bank[5][:, 0:P], wgo_rows[:], ident[:])
-        nc.scalar.copy(w_cols[:], bank[5][:, 0 : J // P])
-        weighted = rows("weighted", LAST + 1)
+        weighted = rows("weighted", LAST)
         result = rows("result", LAST)
         blocks = [slice(b * P, (b + 1) * P) for b in range(JH // P)]
-        turned, way_back = bank[0], bank[5]
 
-        def turned_sum(u, step, kept):
-            c, h = UNITS[u]
+        def turn(u, step, kept, scaled):
+            h = UNITS[u][1]
             for cols in blocks:
                 nc.tensor.matmul(turned[:, cols], step[:, cols], ident[:], start=True, stop=False, is_transpose=True)
                 nc.tensor.matmul(turned[:, cols], kept[:, cols], ident[:], start=False, stop=True, is_transpose=True)
             for b, cols in enumerate(blocks):
                 col = h * len(blocks) + b
-                nc.scalar.activation(weighted[:, u, cols], turned[:, cols], ACT.Copy, scale=w_cols[:, col : col + 1])
+                nc.scalar.activation(scaled[:, cols], turned[:, cols], ACT.Copy, scale=w_cols[:, col : col + 1])
+
+        def turn_back(u, scaled):
             for cols in blocks:
-                nc.tensor.transpose(way_back[:, cols], weighted[:, u, cols], ident[:])
+                nc.tensor.transpose(way_back[:, cols], scaled[:, cols], ident[:])
             nc.scalar.copy(result[:, u, :], way_back[:])
-            nc.vector.tensor_copy(o_sb[c % 3][:].indirect(entries(h)), result[:, u, :])
+
+        def turned_sum(u, step, kept):
+            turn(u, step, kept, weighted[:, u, :])
+            turn_back(u, weighted[:, u, :])
+
+        def scatter(u):
+            c, h = UNITS[u]
+            nc.vector.tensor_copy(o_sb[c][:].indirect(entries(h)), result[:, u, :])
             store_if_complete(u)
 
-        def held(u):
-            return state(u)[:, 0, :]
+        def add(dst, a, b):
+            nc.gpsimd.tensor_tensor(dst, a, b, ALU.add)
 
-        turned_sum(0, t0[:, 0, :], held(0))
-        cd45 = weighted[:, 0 : LAST + 1 : LAST, :]
-        nc.scalar.activation(cd45, pre45, ACT.Tanh)
-        turned_sum(1, e1, held(1))
-        empty_message(6, weighted[:, 1, :])
-        d45 = pair(z, 2)
-        nc.gpsimd.tensor_tensor(d45, cd45, state(4, 2), ALU.subtract)
+        early = rows("early", 2)
+        gather_block(0)
+        for u in (0, 1):
+            candidate(u, early[:, u, :])
+        nc.tensor.transpose(bank[6][:, 0:P], wgo_rows[:], ident[:])
+        nc.scalar.copy(w_cols[:], bank[6][:, 0 : J // P])
+        difference(early[:, 0, :], early[:, 0, :], held(0))
+        product(early[:, 0, :], early[:, 0, :], z[:, 0, :])
+        gather_block(1)
+        difference(early[:, 1, :], early[:, 1, :], held(1))
+        t23 = rows("t23", 2, tag="h_sb1")
+        for u in (2, 3):
+            gate(u)
+            memory(u)
+            gated(u, t23[:, u - 2, :])
+        cast_x(2, xb[1], nc.scalar.copy)
+        cast_x(3, xb[1], nc.scalar.copy)
+        xq[1] = quantise_x(1, xb[1])
+        after_cast = rows("after_cast", 3, tag="x_raw3")
+        xn23 = after_cast[:, 0:2, :]
+        for u in (2, 3):
+            empty_message(u, xn23[:, u - 2, :])
+        pre23 = keep.tile([P, 2, JH], F32, name="pre23", tag="xb1", align_bytes=64)
+        add(pre23[:], xn23, t23[:])
+        e1 = t23[:, 0, :]
+        product(e1, early[:, 1, :], z[:, 1, :])
+        turn(0, early[:, 0, :], held(0), after_cast[:, 2, :])
         for u in (4, 5):
-            nc.gpsimd.tensor_tensor(d45[:, u - 4, :], d45[:, u - 4, :], z[:, u, :], ALU.mult)
-        turned_sum(2, e23[:, 0, :], held(2))
-        empty_message(7, weighted[:, 2, :])
-        turned_sum(3, e23[:, 1, :], held(3))
-        kept6 = weighted[:, 3, :]
+            gate(u)
+        turn_back(0, after_cast[:, 2, :])
+        nc.scalar.activation(xn23, pre23[:], ACT.Tanh)
+        for u in (4, 5):
+            memory(u)
+            message(u)
+        for u in (6, 7):
+            gate(u)
+        gather_block(2)
+        gather_block(3)
+        difference(xn23, xn23, state(2, 2))
+        for u in (2, 3):
+            product(xn23[:, u - 2, :], xn23[:, u - 2, :], z[:, u, :])
+        late = rows("late", 2, tag="h_sb3")
+        for u in (4, 5):
+            gated(u, late[:, u - 4, :])
+        turned_sum(1, e1, held(1))
+        for u in (4, 5):
+            c = UNITS[u][0]
+            zero = o_sb[c][:, 0:1]
+            nc.vector.scalar_tensor_tensor(pre[:, c, :], xn_bank[u][:], zero, late[:, c, :], ALU.add, ALU.add)
+            nc.scalar.activation(late[:, c, :], pre[:, c, :], ACT.Tanh, bias=bn_sb[:, c : c + 1])
+        scatter(0)
+        scatter(1)
+        hn67 = rows("hn67", 2)
+        for u in (6, 7):
+            memory(u)
+            nc.scalar.copy(hn67[:, u - 6, :], hn_bank[u][:])
+        kept6 = weighted[:, 1, :]
         nc.scalar.activation(kept6, z[:, 6, :], ACT.Copy, bias=1.0, scale=-1.0)
-        pre67 = pair(z, 4)
-        nc.gpsimd.tensor_tensor(pre67, pair(weighted, 1), late[:], ALU.add)
-        nc.gpsimd.tensor_tensor(late[:, 0, :], kept6, held(6), ALU.mult)
+        turned_sum(2, xn23[:, 0, :], held(2))
+        scatter(2)
+        xn67 = pair(weighted, 2)
+        empty_message(6, xn67[:, 0, :])
+        d45 = pair(z, 2)
+        difference(d45, late[:], state(4, 2))
+        product(d45[:, 0, :], d45[:, 0, :], z[:, 4, :])
+        turned_sum(3, xn23[:, 1, :], held(3))
+        scatter(3)
+        empty_message(7, xn67[:, 1, :])
+        pre6 = z[:, 4, :]
+        product(pre6, hn67[:, 0, :], z[:, 6, :])
+        add(pre6, pre6, xn67[:, 0, :])
+        e5 = xn67[:, 0, :]
+        product(e5, d45[:, 1, :], z[:, 5, :])
+        product(z[:, 5, :], kept6, held(6))
         turned_sum(4, d45[:, 0, :], held(4))
+        scatter(4)
         new6 = weighted[:, 4, :]
-        nc.scalar.activation(new6, pre67[:, 0, :], ACT.Tanh)
-        nc.gpsimd.tensor_tensor(new6, new6, z[:, 6, :], ALU.mult)
-        turned_sum(5, d45[:, 1, :], held(5))
-        e7 = weighted[:, 5, :]
-        nc.scalar.activation(e7, pre67[:, 1, :], ACT.Tanh)
-        nc.gpsimd.tensor_tensor(e7, e7, held(LAST), ALU.subtract)
-        turned_sum(6, new6, late[:, 0, :])
+        nc.scalar.activation(new6, pre6, ACT.Tanh)
+        product(new6, new6, z[:, 6, :])
+        pre7 = z[:, 6, :]
+        product(pre7, hn67[:, 1, :], z[:, LAST, :])
+        add(pre7, pre7, xn67[:, 1, :])
+        turned_sum(5, e5, held(5))
+        scatter(5)
+        kept7 = weighted[:, 5, :]
+        nc.scalar.activation(kept7, z[:, LAST, :], ACT.Copy, bias=1.0, scale=-1.0)
+        product(xn67[:, 1, :], kept7, held(LAST))
+        turned_sum(6, new6, z[:, 5, :])
+        scatter(6)
         s7 = weighted[:, 6, :]
-        nc.gpsimd.tensor_tensor(s7, e7, z[:, LAST, :], ALU.mult)
-        nc.gpsimd.tensor_tensor(s7, s7, held(LAST), ALU.add)
+        nc.scalar.activation(s7, pre7, ACT.Tanh)
+        product(s7, s7, z[:, LAST, :])
+        add(s7, s7, xn67[:, 1, :])
         c, h = UNITS[LAST]
-        nc.vector.tensor_tensor(o_sb[c % 3][:].indirect(entries(h)), s7, wgo_last[:], ALU.mult)
+        nc.vector.tensor_tensor(o_sb[c][:].indirect(entries(h)), s7, wgo_last[:], ALU.mult)
         store_if_complete(LAST)

@@ -27,6 +27,7 @@ LIST_GROUP = 16
 XP = 256
 UNITS = [(c, h) for h in range(HALVES) for c in range(CHUNKS)]
 LAST = len(UNITS) - 1
+ZERO_SPLIT = 768
 
 
 def tile_list_tgn_mgu_kernel(
@@ -80,10 +81,11 @@ def tile_list_tgn_mgu_kernel(
         def load_x(a):
             nc.sync.dma_start(x_raw[a][:], x_rows[:, :, a * XP : (a + 1) * XP])
 
-        o_sb = [keep.tile([P, T], F32, name=f"o_sb{c}") for c in range(2)]
+        o_sb = [keep.tile([P, T], F32, name=f"o_sb{c}") for c in range(CHUNKS - 1)]
         nc.gpsimd.memset(weight_s[:], 0)
         zero_on_vector(tab_s, 0)
         zero_on_vector(o_sb[0], 0.0)
+        zero_on_vector(o_sb[1][:, 0:ZERO_SPLIT], 0.0)
 
         load_words(tab_w, tab_words)
         load_scale_rows(nc.sync, tab_s, tab_scales, range(0, 4))
@@ -107,10 +109,9 @@ def tile_list_tgn_mgu_kernel(
         load_state(3)
         nc.sync.dma_start(wgo_last[:], wgo[:, JH:J])
         load_scale_rows(nc.gpsimd, un_s, un_scales, range(0, 4))
-        nc.gpsimd.memset(o_sb[1][:], 0.0)
+        nc.gpsimd.memset(o_sb[1][:, ZERO_SPLIT:T], 0.0)
+        nc.gpsimd.memset(o_sb[2][:], 0.0)
 
-        ident = keep.tile([P, P], F32, name="ident")
-        make_identity(nc, ident[:])
         warm = keep.tile([P, 1], F32, name="warm")
         nc.scalar.activation(warm[:], o_sb[0][:, 0:1], ACT.Sigmoid)
 
@@ -142,16 +143,16 @@ def tile_list_tgn_mgu_kernel(
 
         bank = [psum.tile([P, JH], F32, name=f"bank{i}") for i in range(8)]
         sz_bank = [bank[u % 2] for u in range(8)]
-        hn_bank = [bank[2 + u % 3] for u in range(6)] + bank[3:5]
-        xn_bank = [bank[5 + u % 3] for u in range(6)] + bank[6:8]
-        turned, way_back = bank[2], bank[5]
+        hn_bank = [bank[b] for b in (2, 3, 4, 2, 7, 5, 7, 5)]
+        xn_bank = [bank[b] for b in (5, 6, 7, 5, 3, 4, 3, 4)]
+        turned, way_back = bank[2], bank[6]
 
         def rows(name, count, tag=None):
             return keep.tile([P, count, JH], F32, name=name, tag=tag or name)
 
         xq, vq = {}, {}
-        z = rows("z", 8)
-        pre = rows("pre", 2)
+        z = rows("z", 6)
+        pre = rows("pre", 4)
         picked = keep.tile([P, CHUNKS, J], F32, name="picked")
 
         def state(u, count=1):
@@ -161,11 +162,14 @@ def tile_list_tgn_mgu_kernel(
         def mx(dst, lw, ls, operand, start, stop):
             nc.tensor.matmul_mx(out=dst[:], lhsT=lw, lhsT_scale=ls, rhs=operand[0], rhs_scale=operand[1], start=start, stop=stop)
 
-        def gate(u):
+        def gate(u, dst=None):
             c, h = UNITS[u]
-            mx(sz_bank[u], fp8_cols(uz_w, c), scale_cols(uz_s, c), vq[h], True, False)
-            mx(sz_bank[u], fp4_cols(wz_w, c), scale_cols(wz_s, c), xq[h], False, True)
-            nc.scalar.activation(z[:, u, :], sz_bank[u][:], ACT.Sigmoid, bias=bz_sb[:, c : c + 1])
+            dst = z[:, u, :] if dst is None else dst
+            passes = [(fp8_cols(uz_w, c), scale_cols(uz_s, c), vq[h]), (fp4_cols(wz_w, c), scale_cols(wz_s, c), xq[h])]
+            first, second = passes[::-1] if h else passes
+            mx(sz_bank[u], *first, True, False)
+            mx(sz_bank[u], *second, False, True)
+            nc.scalar.activation(dst, sz_bank[u][:], ACT.Sigmoid, bias=bz_sb[:, c : c + 1])
 
         def memory(u):
             c, h = UNITS[u]
@@ -198,15 +202,16 @@ def tile_list_tgn_mgu_kernel(
             nc.vector.tensor_copy(scales[:], tab_s[:].bitcast(U8).indirect(entries(h)))
             vq[h] = (words[:].bitcast(FP8X4), scales[:])
         xb = [
-            reuse.tile([P, JH, PACK], BF16, name="xb0", align_bytes=64, offset=4 * T - 4 * JH),
+            reuse.tile([P, JH, PACK], BF16, name="xb0", align_bytes=64, offset=0),
             keep.tile([P, JH, PACK], BF16, name="xb1", tag="xb1", align_bytes=64),
         ]
         cast_x(0, xb[0], nc.scalar.copy)
         cast_x(1, xb[0], nc.scalar.copy)
         xq[0] = quantise_x(0, xb[0])
-        for a in range(2):
-            o_sb.append(reuse.tile([P, T], F32, name=f"o_late{a}", align_bytes=64, offset=4 * T * a))
-            nc.gpsimd.memset(o_sb[-1][:], 0.0)
+        ident = reuse.tile([P, P], F32, name="ident", align_bytes=64, offset=0)
+        make_identity(nc, ident[:])
+        o_sb.append(reuse.tile([P, T], F32, name="o_late", align_bytes=64, offset=4 * P))
+        nc.gpsimd.memset(o_sb[-1][:], 0.0)
 
         def pair(tile, u):
             return tile[:, u : u + 2, :]
@@ -266,10 +271,12 @@ def tile_list_tgn_mgu_kernel(
             candidate(u, early[:, u, :])
         nc.tensor.transpose(bank[6][:, 0:P], wgo_rows[:], ident[:])
         nc.scalar.copy(w_cols[:], bank[6][:, 0 : J // P])
-        difference(early[:, 0, :], early[:, 0, :], held(0))
-        product(early[:, 0, :], early[:, 0, :], z[:, 0, :])
+        kept01 = rows("kept01", 2)
+        nc.gpsimd.tensor_scalar(kept01[:], pair(z, 0), -1.0, 1.0, ALU.mult, ALU.add)
+        product(kept01[:, 0, :], kept01[:, 0, :], held(0))
+        product(early[:], early[:], pair(z, 0))
         gather_block(1)
-        difference(early[:, 1, :], early[:, 1, :], held(1))
+        product(kept01[:, 1, :], kept01[:, 1, :], held(1))
         t23 = rows("t23", 2, tag="h_sb1")
         for u in (2, 3):
             gate(u)
@@ -278,81 +285,89 @@ def tile_list_tgn_mgu_kernel(
         cast_x(2, xb[1], nc.scalar.copy)
         cast_x(3, xb[1], nc.scalar.copy)
         xq[1] = quantise_x(1, xb[1])
-        after_cast = rows("after_cast", 3, tag="x_raw3")
+        after_cast = rows("after_cast", 4, tag="x_raw3")
         xn23 = after_cast[:, 0:2, :]
         for u in (2, 3):
             empty_message(u, xn23[:, u - 2, :])
         pre23 = keep.tile([P, 2, JH], F32, name="pre23", tag="xb1", align_bytes=64)
         add(pre23[:], xn23, t23[:])
-        e1 = t23[:, 0, :]
-        product(e1, early[:, 1, :], z[:, 1, :])
-        turn(0, early[:, 0, :], held(0), after_cast[:, 2, :])
+        kept2 = after_cast[:, 3, :]
+        nc.scalar.activation(kept2, z[:, 2, :], ACT.Copy, bias=1.0, scale=-1.0)
+        turn(0, early[:, 0, :], kept01[:, 0, :], after_cast[:, 2, :])
         for u in (4, 5):
             gate(u)
-        turn_back(0, after_cast[:, 2, :])
         nc.scalar.activation(xn23, pre23[:], ACT.Tanh)
+        turn_back(0, after_cast[:, 2, :])
+        turned_sum(1, early[:, 1, :], kept01[:, 1, :])
+        nc.scalar.activation(pre23[:, 1, :], z[:, 3, :], ACT.Copy, bias=1.0, scale=-1.0)
         for u in (4, 5):
             memory(u)
             message(u)
-        for u in (6, 7):
-            gate(u)
         gather_block(2)
         gather_block(3)
-        difference(xn23, xn23, state(2, 2))
-        for u in (2, 3):
-            product(xn23[:, u - 2, :], xn23[:, u - 2, :], z[:, u, :])
+        product(kept2, kept2, held(2))
+        product(xn23, xn23, pair(z, 2))
+        product(pre23[:, 1, :], pre23[:, 1, :], held(3))
         late = rows("late", 2, tag="h_sb3")
         for u in (4, 5):
             gated(u, late[:, u - 4, :])
-        turned_sum(1, e1, held(1))
         for u in (4, 5):
             c = UNITS[u][0]
             zero = o_sb[c][:, 0:1]
-            nc.vector.scalar_tensor_tensor(pre[:, c, :], xn_bank[u][:], zero, late[:, c, :], ALU.add, ALU.add)
-            nc.scalar.activation(late[:, c, :], pre[:, c, :], ACT.Tanh, bias=bn_sb[:, c : c + 1])
+            nc.vector.scalar_tensor_tensor(pre[:, u - 2, :], xn_bank[u][:], zero, late[:, c, :], ALU.add, ALU.add)
+            nc.scalar.activation(late[:, c, :], pre[:, u - 2, :], ACT.Tanh, bias=bn_sb[:, c : c + 1])
         scatter(0)
         scatter(1)
-        hn67 = rows("hn67", 2)
-        for u in (6, 7):
-            memory(u)
-            nc.scalar.copy(hn67[:, u - 6, :], hn_bank[u][:])
-        kept6 = weighted[:, 1, :]
-        nc.scalar.activation(kept6, z[:, 6, :], ACT.Copy, bias=1.0, scale=-1.0)
-        turned_sum(2, xn23[:, 0, :], held(2))
+        z6 = pre[:, 3, :]
+        gate(6, z6)
+        memory(6)
+        hn6 = pre[:, 2, :]
+        nc.scalar.copy(hn6, hn_bank[6][:])
+        z7 = weighted[:, 1, :]
+        gate(LAST, z7)
+        turned_sum(2, xn23[:, 0, :], kept2)
         scatter(2)
-        xn67 = pair(weighted, 2)
-        empty_message(6, xn67[:, 0, :])
+        xn6 = weighted[:, 2, :]
+        empty_message(6, xn6)
         d45 = pair(z, 2)
         difference(d45, late[:], state(4, 2))
         product(d45[:, 0, :], d45[:, 0, :], z[:, 4, :])
-        turned_sum(3, xn23[:, 1, :], held(3))
+        turn(3, xn23[:, 1, :], pre23[:, 1, :], weighted[:, 3, :])
+        xn7 = xn23[:, 1, :]
+        empty_message(LAST, xn7)
+        turn_back(3, weighted[:, 3, :])
         scatter(3)
-        empty_message(7, xn67[:, 1, :])
+        kept6 = weighted[:, 3, :]
+        nc.scalar.activation(kept6, z6, ACT.Copy, bias=1.0, scale=-1.0)
         pre6 = z[:, 4, :]
-        product(pre6, hn67[:, 0, :], z[:, 6, :])
-        add(pre6, pre6, xn67[:, 0, :])
-        e5 = xn67[:, 0, :]
+        product(pre6, hn6, z6)
+        add(pre6, pre6, xn6)
+        e5 = xn6
         product(e5, d45[:, 1, :], z[:, 5, :])
         product(z[:, 5, :], kept6, held(6))
-        turned_sum(4, d45[:, 0, :], held(4))
+        turn(4, d45[:, 0, :], held(4), weighted[:, 4, :])
+        memory(LAST)
+        hn7 = d45[:, 0, :]
+        nc.scalar.copy(hn7, hn_bank[LAST][:])
+        turn_back(4, weighted[:, 4, :])
         scatter(4)
         new6 = weighted[:, 4, :]
         nc.scalar.activation(new6, pre6, ACT.Tanh)
-        product(new6, new6, z[:, 6, :])
-        pre7 = z[:, 6, :]
-        product(pre7, hn67[:, 1, :], z[:, LAST, :])
-        add(pre7, pre7, xn67[:, 1, :])
+        product(new6, new6, z6)
         turned_sum(5, e5, held(5))
         scatter(5)
+        pre7 = z6
+        product(pre7, hn7, z7)
+        add(pre7, pre7, xn7)
         kept7 = weighted[:, 5, :]
-        nc.scalar.activation(kept7, z[:, LAST, :], ACT.Copy, bias=1.0, scale=-1.0)
-        product(xn67[:, 1, :], kept7, held(LAST))
+        nc.scalar.activation(kept7, z7, ACT.Copy, bias=1.0, scale=-1.0)
+        product(xn7, kept7, held(LAST))
         turned_sum(6, new6, z[:, 5, :])
         scatter(6)
         s7 = weighted[:, 6, :]
         nc.scalar.activation(s7, pre7, ACT.Tanh)
-        product(s7, s7, z[:, LAST, :])
-        add(s7, s7, xn67[:, 1, :])
+        product(s7, s7, z7)
+        add(s7, s7, xn7)
         c, h = UNITS[LAST]
         nc.vector.tensor_tensor(o_sb[c][:].indirect(entries(h)), s7, wgo_last[:], ALU.mult)
         store_if_complete(LAST)

@@ -20,11 +20,12 @@ ALU = mybir.AluOpType
 P = 128
 PACK = 4
 QUADRANTS = 4
+BANKS = 8
 JH = 512
 HALVES = J // JH
 CHUNKS = N // P
 LIST_GROUP = 16
-XP = 256
+X_PIECE = JH // 2
 UNITS = [(c, h) for h in range(HALVES) for c in range(CHUNKS)]
 LAST = len(UNITS) - 1
 ZERO_SPLIT = 768
@@ -52,7 +53,7 @@ def tile_list_tgn_mgu_kernel(
         wn_w = keep.tile([P, N // 2], I32, name="wn_w", align_bytes=64)
         un_w = keep.tile([P, N], I32, name="un_w", align_bytes=64)
         x_rows = x.rearrange("(p i) j -> p i j", i=PACK)
-        x_raw = [keep.tile([P, PACK, XP], F32, name=f"x_raw{a}", tag=f"x_raw{a}") for a in range(J // XP)]
+        x_raw = [keep.tile([P, PACK, X_PIECE], F32, name=f"x_raw{a}", tag=f"x_raw{a}") for a in range(J // X_PIECE)]
         h_sb = [keep.tile([P, T], F32, name=f"h_sb{c}", tag=f"h_sb{c}") for c in range(CHUNKS)]
         wgo_last = keep.tile([P, JH], F32, name="wgo_last")
         wgo_rows = keep.tile([P, P], F32, name="wgo_rows")
@@ -64,12 +65,15 @@ def tile_list_tgn_mgu_kernel(
             nc.vector.memset(tile[:, 0 : width - 1], zero)
             nc.vector.memset(tile[:, width - 1 : width], zero)
 
-        def load_scale_rows(queue, scales, rows, quadrants):
-            for q in quadrants:
+        def load_scales(queue, scales, rows):
+            for q in range(QUADRANTS):
                 queue.dma_start(scales[32 * q : 32 * q + 4, :], rows[0, 4 * q : 4 * q + 4, :].bitcast(I32))
 
-        def load_words(tile, words):
+        def load_fp8_words(tile, words):
             nc.sync.dma_start(tile[:], words[0].rearrange("p n i -> p (n i)").bitcast(I32))
+
+        def load_fp4_words(tile, words):
+            nc.sync.dma_start(tile[:], words[0].bitcast(I32))
 
         def load_bias(tile, vec):
             with nc.allow_non_contiguous_dma(reason="one bias value to a partition"):
@@ -79,7 +83,7 @@ def tile_list_tgn_mgu_kernel(
             nc.sync.dma_start(h_sb[c][:], hT[c * P : (c + 1) * P, :])
 
         def load_x(a):
-            nc.sync.dma_start(x_raw[a][:], x_rows[:, :, a * XP : (a + 1) * XP])
+            nc.sync.dma_start(x_raw[a][:], x_rows[:, :, a * X_PIECE : (a + 1) * X_PIECE])
 
         o_sb = [keep.tile([P, T], F32, name=f"o_sb{c}") for c in range(CHUNKS - 1)]
         nc.gpsimd.memset(weight_s[:], 0)
@@ -87,28 +91,28 @@ def tile_list_tgn_mgu_kernel(
         zero_on_vector(o_sb[0], 0.0)
         zero_on_vector(o_sb[1][:, 0:ZERO_SPLIT], 0.0)
 
-        load_words(tab_w, tab_words)
-        load_scale_rows(nc.sync, tab_s, tab_scales, range(0, 4))
+        load_fp8_words(tab_w, tab_words)
+        load_scales(nc.sync, tab_s, tab_scales)
         load_x(0)
         load_x(1)
-        load_words(uz_w, uz_words)
-        load_scale_rows(nc.sync, uz_s, uz_scales, range(0, 4))
+        load_fp8_words(uz_w, uz_words)
+        load_scales(nc.sync, uz_s, uz_scales)
         load_state(0)
-        load_scale_rows(nc.sync, wz_s, wz_scales, range(0, 4))
-        nc.sync.dma_start(wz_w[:], wz_words[0].bitcast(I32))
+        load_scales(nc.sync, wz_s, wz_scales)
+        load_fp4_words(wz_w, wz_words)
         load_bias(bz_sb, bz)
-        load_words(un_w, un_words)
-        nc.sync.dma_start(wn_w[:], wn_words[0].bitcast(I32))
-        load_scale_rows(nc.sync, wn_s, wn_scales, range(0, 4))
+        load_fp8_words(un_w, un_words)
+        load_fp4_words(wn_w, wn_words)
+        load_scales(nc.sync, wn_s, wn_scales)
         load_bias(bn_sb, bn)
-        nc.sync.dma_start(wgo_rows[:], wgo[0 : P * P // J, :].rearrange("a (b j) -> (a b) j", j=P))
         load_state(1)
+        nc.sync.dma_start(wgo_rows[:], wgo[0 : P * P // J, :].rearrange("a (b j) -> (a b) j", j=P))
         load_x(2)
         load_x(3)
         load_state(2)
         load_state(3)
         nc.sync.dma_start(wgo_last[:], wgo[:, JH:J])
-        load_scale_rows(nc.gpsimd, un_s, un_scales, range(0, 4))
+        load_scales(nc.gpsimd, un_s, un_scales)
         nc.gpsimd.memset(o_sb[1][:, ZERO_SPLIT:T], 0.0)
         nc.gpsimd.memset(o_sb[2][:], 0.0)
 
@@ -119,10 +123,10 @@ def tile_list_tgn_mgu_kernel(
             width = JH // LIST_GROUP
             return offsets[:, h * width : (h + 1) * width]
 
-        def cast_x(a, xb, copy):
-            cols = slice((a * XP) % JH, (a * XP) % JH + XP)
-            copy(
-                out=xb[:, cols, :].rearrange("p (a b) i -> p a i b", b=4),
+        def cast_x(a, xb):
+            first = (a * X_PIECE) % JH
+            nc.scalar.copy(
+                out=xb[:, first : first + X_PIECE, :].rearrange("p (a b) i -> p a i b", b=4),
                 in_=x_raw[a][:].rearrange("p i (a b) -> p a i b", b=4),
             )
 
@@ -141,53 +145,74 @@ def tile_list_tgn_mgu_kernel(
         def scale_cols(scales, c):
             return scales[:, (P // 4) * c : (P // 4) * (c + 1)].bitcast(U8)
 
-        bank = [psum.tile([P, JH], F32, name=f"bank{i}") for i in range(8)]
-        sz_bank = [bank[u % 2] for u in range(8)]
-        hn_bank = [bank[b] for b in (2, 3, 4, 2, 7, 5, 7, 5)]
-        xn_bank = [bank[b] for b in (5, 6, 7, 5, 3, 4, 3, 4)]
+        bank = [psum.tile([P, JH], F32, name=f"bank{i}") for i in range(BANKS)]
+        sz_bank = [bank[u % 2] for u in range(len(UNITS))]
+        xn_first = [bank[5 + u % 3] for u in range(CHUNKS)]
+        hn_bank = [bank[2 + u % 3] for u in range(CHUNKS)] + 2 * xn_first[2:4]
+        xn_bank = xn_first + 2 * bank[3:5]
         turned, way_back = bank[2], bank[6]
 
         def rows(name, count, tag=None):
             return keep.tile([P, count, JH], F32, name=name, tag=tag or name)
+
+        def pair(tile, first):
+            return tile[:, first : first + 2, :]
 
         xq, vq = {}, {}
         z = rows("z", 6)
         pre = rows("pre", 4)
         picked = keep.tile([P, CHUNKS, J], F32, name="picked")
 
-        def state(u, count=1):
+        def state(u):
             c, h = UNITS[u]
-            return picked[:, c : c + count, h * JH : (h + 1) * JH]
+            return picked[:, c, h * JH : (h + 1) * JH]
 
         def mx(dst, lw, ls, operand, start, stop):
             nc.tensor.matmul_mx(out=dst[:], lhsT=lw, lhsT_scale=ls, rhs=operand[0], rhs_scale=operand[1], start=start, stop=stop)
 
-        def gate(u, dst=None):
+        def gate(u, dst):
             c, h = UNITS[u]
-            dst = z[:, u, :] if dst is None else dst
             passes = [(fp8_cols(uz_w, c), scale_cols(uz_s, c), vq[h]), (fp4_cols(wz_w, c), scale_cols(wz_s, c), xq[h])]
             first, second = passes[::-1] if h else passes
             mx(sz_bank[u], *first, True, False)
             mx(sz_bank[u], *second, False, True)
             nc.scalar.activation(dst, sz_bank[u][:], ACT.Sigmoid, bias=bz_sb[:, c : c + 1])
 
-        def memory(u):
+        def multiply_hn(u):
             c, h = UNITS[u]
             mx(hn_bank[u], fp8_cols(un_w, c), scale_cols(un_s, c), vq[h], True, True)
 
-        def message(u):
+        def multiply_xn(u):
             c, h = UNITS[u]
             mx(xn_bank[u], fp4_cols(wn_w, c), scale_cols(wn_s, c), xq[h], True, True)
 
-        def empty_message(u, dst):
+        def hn_to_sbuf(u, dst):
+            multiply_hn(u)
+            nc.scalar.copy(dst, hn_bank[u][:])
+
+        def xn_bn_to_sbuf(u, dst):
             c = UNITS[u][0]
-            message(u)
+            multiply_xn(u)
             nc.scalar.activation(dst, xn_bank[u][:], ACT.Identity, bias=bn_sb[:, c : c + 1])
 
-        def gated(u, dst):
+        def z_hn_on_vector(u, dst):
             nc.vector.tensor_tensor(dst, hn_bank[u][:], z[:, u, :], ALU.mult)
 
-        def gather_block(c):
+        def cd_from_bank(u, row, argument):
+            c = UNITS[u][0]
+            nc.vector.tensor_tensor(argument, xn_bank[u][:], row, ALU.add)
+            nc.scalar.activation(row, argument, ACT.Tanh, bias=bn_sb[:, c : c + 1])
+
+        def one_minus(dst, gate_row):
+            nc.scalar.activation(dst, gate_row, ACT.Copy, bias=1.0, scale=-1.0)
+
+        def product(dst, a, b):
+            nc.gpsimd.tensor_tensor(dst, a, b, ALU.mult)
+
+        def add(dst, a, b):
+            nc.gpsimd.tensor_tensor(dst, a, b, ALU.add)
+
+        def gather_state(c):
             nc.vector.tensor_copy(picked[:, c, :], h_sb[c][:].indirect(offsets[:]))
 
         def store_if_complete(u):
@@ -205,45 +230,25 @@ def tile_list_tgn_mgu_kernel(
             reuse.tile([P, JH, PACK], BF16, name="xb0", align_bytes=64, offset=0),
             keep.tile([P, JH, PACK], BF16, name="xb1", tag="xb1", align_bytes=64),
         ]
-        cast_x(0, xb[0], nc.scalar.copy)
-        cast_x(1, xb[0], nc.scalar.copy)
+        cast_x(0, xb[0])
+        cast_x(1, xb[0])
         xq[0] = quantise_x(0, xb[0])
         ident = reuse.tile([P, P], F32, name="ident", align_bytes=64, offset=0)
         make_identity(nc, ident[:])
         o_sb.append(reuse.tile([P, T], F32, name="o_late", align_bytes=64, offset=4 * P))
         nc.gpsimd.memset(o_sb[-1][:], 0.0)
 
-        def pair(tile, u):
-            return tile[:, u : u + 2, :]
-
-        def held(u):
-            return state(u)[:, 0, :]
-
-        def candidate(u, t_row):
-            c = UNITS[u][0]
-            gate(u)
-            memory(u)
-            message(u)
-            gated(u, t_row)
-            nc.vector.tensor_tensor(pre[:, u, :], xn_bank[u][:], t_row, ALU.add)
-            nc.scalar.activation(t_row, pre[:, u, :], ACT.Tanh, bias=bn_sb[:, c : c + 1])
-
-        def difference(dst, cand, h_rows):
-            nc.gpsimd.tensor_tensor(dst, cand, h_rows, ALU.subtract)
-
-        def product(dst, a, b):
-            nc.gpsimd.tensor_tensor(dst, a, b, ALU.mult)
-
         w_cols = keep.tile([P, J // P], F32, name="w_cols")
         weighted = rows("weighted", LAST)
-        result = rows("result", LAST)
+        later_results = rows("later_results", LAST - 1)
+        result = {u: later_results[:, u - 1, :] for u in range(1, LAST)}
         blocks = [slice(b * P, (b + 1) * P) for b in range(JH // P)]
 
-        def turn(u, step, kept, scaled):
+        def turn(u, term_a, term_b, scaled):
             h = UNITS[u][1]
             for cols in blocks:
-                nc.tensor.matmul(turned[:, cols], step[:, cols], ident[:], start=True, stop=False, is_transpose=True)
-                nc.tensor.matmul(turned[:, cols], kept[:, cols], ident[:], start=False, stop=True, is_transpose=True)
+                nc.tensor.matmul(turned[:, cols], term_a[:, cols], ident[:], start=True, stop=False, is_transpose=True)
+                nc.tensor.matmul(turned[:, cols], term_b[:, cols], ident[:], start=False, stop=True, is_transpose=True)
             for b, cols in enumerate(blocks):
                 col = h * len(blocks) + b
                 nc.scalar.activation(scaled[:, cols], turned[:, cols], ACT.Copy, scale=w_cols[:, col : col + 1])
@@ -251,123 +256,121 @@ def tile_list_tgn_mgu_kernel(
         def turn_back(u, scaled):
             for cols in blocks:
                 nc.tensor.transpose(way_back[:, cols], scaled[:, cols], ident[:])
-            nc.scalar.copy(result[:, u, :], way_back[:])
+            nc.scalar.copy(result[u], way_back[:])
 
-        def turned_sum(u, step, kept):
-            turn(u, step, kept, weighted[:, u, :])
+        def turn_both_ways(u, term_a, term_b):
+            turn(u, term_a, term_b, weighted[:, u, :])
             turn_back(u, weighted[:, u, :])
 
         def scatter(u):
             c, h = UNITS[u]
-            nc.vector.tensor_copy(o_sb[c][:].indirect(entries(h)), result[:, u, :])
+            nc.vector.tensor_copy(o_sb[c][:].indirect(entries(h)), result[u])
             store_if_complete(u)
 
-        def add(dst, a, b):
-            nc.gpsimd.tensor_tensor(dst, a, b, ALU.add)
-
-        early = rows("early", 2)
-        gather_block(0)
+        new01 = rows("new01", 2)
+        gather_state(0)
         for u in (0, 1):
-            candidate(u, early[:, u, :])
-        nc.tensor.transpose(bank[6][:, 0:P], wgo_rows[:], ident[:])
-        nc.scalar.copy(w_cols[:], bank[6][:, 0 : J // P])
-        kept01 = rows("kept01", 2)
-        nc.gpsimd.tensor_scalar(kept01[:], pair(z, 0), -1.0, 1.0, ALU.mult, ALU.add)
-        product(kept01[:, 0, :], kept01[:, 0, :], held(0))
-        product(early[:], early[:], pair(z, 0))
-        gather_block(1)
-        product(kept01[:, 1, :], kept01[:, 1, :], held(1))
-        t23 = rows("t23", 2, tag="h_sb1")
+            gate(u, z[:, u, :])
+            multiply_hn(u)
+            multiply_xn(u)
+            z_hn_on_vector(u, new01[:, u, :])
+            cd_from_bank(u, new01[:, u, :], pre[:, u, :])
+        nc.tensor.transpose(way_back[:, 0:P], wgo_rows[:], ident[:])
+        nc.scalar.copy(w_cols[:], way_back[:, 0 : J // P])
+        rest01 = rows("rest01", 2)
+        nc.gpsimd.tensor_scalar(rest01[:], pair(z, 0), -1.0, 1.0, ALU.mult, ALU.add)
+        kept0 = rest01[:, 0, :]
+        product(kept0, kept0, state(0))
+        product(new01[:], new01[:], pair(z, 0))
+
+        gather_state(1)
+        zhn23 = rows("zhn23", 2, tag="h_sb1")
         for u in (2, 3):
-            gate(u)
-            memory(u)
-            gated(u, t23[:, u - 2, :])
-        cast_x(2, xb[1], nc.scalar.copy)
-        cast_x(3, xb[1], nc.scalar.copy)
+            gate(u, z[:, u, :])
+            multiply_hn(u)
+            z_hn_on_vector(u, zhn23[:, u - 2, :])
+        cast_x(2, xb[1])
+        cast_x(3, xb[1])
         xq[1] = quantise_x(1, xb[1])
         after_cast = rows("after_cast", 4, tag="x_raw3")
-        xn23 = after_cast[:, 0:2, :]
+        new23, weighted0, kept2 = pair(after_cast, 0), after_cast[:, 2, :], after_cast[:, 3, :]
         for u in (2, 3):
-            empty_message(u, xn23[:, u - 2, :])
-        pre23 = keep.tile([P, 2, JH], F32, name="pre23", tag="xb1", align_bytes=64)
-        add(pre23[:], xn23, t23[:])
-        kept2 = after_cast[:, 3, :]
-        nc.scalar.activation(kept2, z[:, 2, :], ACT.Copy, bias=1.0, scale=-1.0)
-        turn(0, early[:, 0, :], kept01[:, 0, :], after_cast[:, 2, :])
+            xn_bn_to_sbuf(u, new23[:, u - 2, :])
+        after_x = keep.tile([P, 3, JH], F32, name="after_x", tag="xb1", align_bytes=64)
+        pre23, kept1 = pair(after_x, 0), after_x[:, 2, :]
+        product(kept1, rest01[:, 1, :], state(1))
+        add(pre23, new23, zhn23[:])
+        one_minus(kept2, z[:, 2, :])
+        turn(0, new01[:, 0, :], kept0, weighted0)
         for u in (4, 5):
-            gate(u)
-        nc.scalar.activation(xn23, pre23[:], ACT.Tanh)
-        turn_back(0, after_cast[:, 2, :])
-        turned_sum(1, early[:, 1, :], kept01[:, 1, :])
-        nc.scalar.activation(pre23[:, 1, :], z[:, 3, :], ACT.Copy, bias=1.0, scale=-1.0)
+            gate(u, z[:, u, :])
+        nc.scalar.activation(new23, pre23, ACT.Tanh)
+        gather_state(2)
+        gather_state(3)
+        after_state = rows("after_state", 3, tag="h_sb3")
+        cd45, result[0] = pair(after_state, 0), after_state[:, 2, :]
+        turn_back(0, weighted0)
+        turn_both_ways(1, new01[:, 1, :], kept1)
+        kept3 = pre23[:, 1, :]
+        one_minus(kept3, z[:, 3, :])
         for u in (4, 5):
-            memory(u)
-            message(u)
-        gather_block(2)
-        gather_block(3)
-        product(kept2, kept2, held(2))
-        product(xn23, xn23, pair(z, 2))
-        product(pre23[:, 1, :], pre23[:, 1, :], held(3))
-        late = rows("late", 2, tag="h_sb3")
+            multiply_hn(u)
+            multiply_xn(u)
+        product(kept2, kept2, state(2))
+        product(new23, new23, pair(z, 2))
+        product(kept3, kept3, state(3))
+
         for u in (4, 5):
-            gated(u, late[:, u - 4, :])
+            z_hn_on_vector(u, cd45[:, u - 4, :])
         for u in (4, 5):
-            c = UNITS[u][0]
-            zero = o_sb[c][:, 0:1]
-            nc.vector.scalar_tensor_tensor(pre[:, u - 2, :], xn_bank[u][:], zero, late[:, c, :], ALU.add, ALU.add)
-            nc.scalar.activation(late[:, c, :], pre[:, u - 2, :], ACT.Tanh, bias=bn_sb[:, c : c + 1])
+            cd_from_bank(u, cd45[:, u - 4, :], pre[:, u - 2, :])
         scatter(0)
         scatter(1)
-        z6 = pre[:, 3, :]
+
+        turn(2, new23[:, 0, :], kept2, weighted[:, 2, :])
+        z6, xn7 = kept2, new23[:, 0, :]
         gate(6, z6)
-        memory(6)
-        hn6 = pre[:, 2, :]
-        nc.scalar.copy(hn6, hn_bank[6][:])
-        z7 = weighted[:, 1, :]
-        gate(LAST, z7)
-        turned_sum(2, xn23[:, 0, :], kept2)
+        xn_bn_to_sbuf(LAST, xn7)
+        turn_back(2, weighted[:, 2, :])
         scatter(2)
-        xn6 = weighted[:, 2, :]
-        empty_message(6, xn6)
-        d45 = pair(z, 2)
-        difference(d45, late[:], state(4, 2))
-        product(d45[:, 0, :], d45[:, 0, :], z[:, 4, :])
-        turn(3, xn23[:, 1, :], pre23[:, 1, :], weighted[:, 3, :])
-        xn7 = xn23[:, 1, :]
-        empty_message(LAST, xn7)
+        hn6 = weighted[:, 2, :]
+        hn_to_sbuf(6, hn6)
+        step45 = pair(z, 2)
+        nc.gpsimd.tensor_tensor(step45, cd45, picked[:, 0:2, JH:J], ALU.subtract)
+        product(step45, step45, pair(z, 4))
+        turn(3, new23[:, 1, :], kept3, weighted[:, 3, :])
+        xn6, z7 = new23[:, 1, :], kept3
+        xn_bn_to_sbuf(6, xn6)
+        gate(LAST, z7)
         turn_back(3, weighted[:, 3, :])
         scatter(3)
-        kept6 = weighted[:, 3, :]
-        nc.scalar.activation(kept6, z6, ACT.Copy, bias=1.0, scale=-1.0)
-        pre6 = z[:, 4, :]
+
+        rest6, pre6, kept6 = weighted[:, 3, :], z[:, 4, :], xn6
+        one_minus(rest6, z6)
         product(pre6, hn6, z6)
         add(pre6, pre6, xn6)
-        e5 = xn6
-        product(e5, d45[:, 1, :], z[:, 5, :])
-        product(z[:, 5, :], kept6, held(6))
-        turn(4, d45[:, 0, :], held(4), weighted[:, 4, :])
-        memory(LAST)
-        hn7 = d45[:, 0, :]
-        nc.scalar.copy(hn7, hn_bank[LAST][:])
+        product(kept6, rest6, state(6))
+        turn(4, step45[:, 0, :], state(4), weighted[:, 4, :])
+        hn7 = step45[:, 0, :]
+        hn_to_sbuf(LAST, hn7)
         turn_back(4, weighted[:, 4, :])
         scatter(4)
         new6 = weighted[:, 4, :]
         nc.scalar.activation(new6, pre6, ACT.Tanh)
         product(new6, new6, z6)
-        turned_sum(5, e5, held(5))
+        turn_both_ways(5, step45[:, 1, :], state(5))
         scatter(5)
-        pre7 = z6
+        rest7, pre7, kept7 = weighted[:, 5, :], z6, xn7
         product(pre7, hn7, z7)
         add(pre7, pre7, xn7)
-        kept7 = weighted[:, 5, :]
-        nc.scalar.activation(kept7, z7, ACT.Copy, bias=1.0, scale=-1.0)
-        product(xn7, kept7, held(LAST))
-        turned_sum(6, new6, z[:, 5, :])
+        one_minus(rest7, z7)
+        product(kept7, rest7, state(LAST))
+        turn_both_ways(6, new6, kept6)
         scatter(6)
-        s7 = weighted[:, 6, :]
-        nc.scalar.activation(s7, pre7, ACT.Tanh)
-        product(s7, s7, z7)
-        add(s7, s7, xn7)
+        blend7 = weighted[:, 6, :]
+        nc.scalar.activation(blend7, pre7, ACT.Tanh)
+        product(blend7, blend7, z7)
+        add(blend7, blend7, kept7)
         c, h = UNITS[LAST]
-        nc.vector.tensor_tensor(o_sb[c][:].indirect(entries(h)), s7, wgo_last[:], ALU.mult)
+        nc.vector.tensor_tensor(o_sb[c][:].indirect(entries(h)), blend7, wgo_last[:], ALU.mult)
         store_if_complete(LAST)

@@ -246,17 +246,17 @@ def tile_list_tgn_mgu_kernel(
 
         def turn(u, term_a, term_b, scaled):
             h = UNITS[u][1]
-            for cols in blocks:
-                nc.tensor.matmul(turned[:, cols], term_a[:, cols], ident[:], start=True, stop=False, is_transpose=True)
-                nc.tensor.matmul(turned[:, cols], term_b[:, cols], ident[:], start=False, stop=True, is_transpose=True)
+            passes = [(term, cols) for term in (term_b, term_a) for cols in blocks]
+            for n, (term, cols) in enumerate(passes):
+                nc.tensor.matmul(turned[:, cols], term[:, cols], ident[:], start=n == 0, stop=n == len(passes) - 1, is_transpose=True)
             for b, cols in enumerate(blocks):
                 col = h * len(blocks) + b
                 nc.scalar.activation(scaled[:, cols], turned[:, cols], ACT.Copy, scale=w_cols[:, col : col + 1])
 
-        def turn_back(u, scaled):
+        def turn_back(u, scaled, through=way_back):
             for cols in blocks:
-                nc.tensor.transpose(way_back[:, cols], scaled[:, cols], ident[:])
-            nc.scalar.copy(result[u], way_back[:])
+                nc.tensor.transpose(through[:, cols], scaled[:, cols], ident[:])
+            nc.scalar.copy(result[u], through[:])
 
         def turn_both_ways(u, term_a, term_b):
             turn(u, term_a, term_b, weighted[:, u, :])
@@ -304,33 +304,38 @@ def tile_list_tgn_mgu_kernel(
         turn(0, new01[:, 0, :], kept0, weighted0)
         for u in (4, 5):
             gate(u, z[:, u, :])
+        xn5 = pre[:, 0, :]
+        xn_bn_to_sbuf(5, xn5)
+        multiply_hn(4)
+        multiply_hn(5)
+        multiply_xn(4)
         nc.scalar.activation(new23, pre23, ACT.Tanh)
         gather_state(2)
         gather_state(3)
-        after_state = rows("after_state", 3, tag="h_sb3")
-        cd45, result[0] = pair(after_state, 0), after_state[:, 2, :]
+        after_state = rows("after_state", 4, tag="h_sb3")
+        zhn45, result[0], result[1] = pair(after_state, 0), after_state[:, 2, :], after_state[:, 3, :]
         turn_back(0, weighted0)
-        turn_both_ways(1, new01[:, 1, :], kept1)
-        kept3 = pre23[:, 1, :]
-        one_minus(kept3, z[:, 3, :])
-        for u in (4, 5):
-            multiply_hn(u)
-            multiply_xn(u)
+        turn(1, new01[:, 1, :], kept1, weighted[:, 1, :])
+        turn_back(1, weighted[:, 1, :], sz_bank[5])
+        rest3, kept3 = pre23[:, 1, :], xn5
+        one_minus(rest3, z[:, 3, :])
         product(kept2, kept2, state(2))
         product(new23, new23, pair(z, 2))
-        product(kept3, kept3, state(3))
 
         for u in (4, 5):
-            z_hn_on_vector(u, cd45[:, u - 4, :])
-        for u in (4, 5):
-            cd_from_bank(u, cd45[:, u - 4, :], pre[:, u - 2, :])
+            z_hn_on_vector(u, zhn45[:, u - 4, :])
+        cd45 = pair(weighted, 0)
+        nc.vector.tensor_tensor(pre[:, 2, :], xn_bank[4][:], zhn45[:, 0, :], ALU.add)
+        nc.scalar.activation(cd45[:, 0, :], pre[:, 2, :], ACT.Tanh, bias=bn_sb[:, 0:1])
+        add(pre[:, 3, :], xn5, zhn45[:, 1, :])
+        product(kept3, rest3, state(3))
+        nc.scalar.activation(cd45[:, 1, :], pre[:, 3, :], ACT.Tanh)
         scatter(0)
         scatter(1)
 
         turn(2, new23[:, 0, :], kept2, weighted[:, 2, :])
-        z6, xn7 = kept2, new23[:, 0, :]
+        z6 = kept2
         gate(6, z6)
-        xn_bn_to_sbuf(LAST, xn7)
         turn_back(2, weighted[:, 2, :])
         scatter(2)
         hn6 = weighted[:, 2, :]
@@ -339,9 +344,8 @@ def tile_list_tgn_mgu_kernel(
         nc.gpsimd.tensor_tensor(step45, cd45, picked[:, 0:2, JH:J], ALU.subtract)
         product(step45, step45, pair(z, 4))
         turn(3, new23[:, 1, :], kept3, weighted[:, 3, :])
-        xn6, z7 = new23[:, 1, :], kept3
+        xn6 = new23[:, 1, :]
         xn_bn_to_sbuf(6, xn6)
-        gate(LAST, z7)
         turn_back(3, weighted[:, 3, :])
         scatter(3)
 
@@ -351,19 +355,25 @@ def tile_list_tgn_mgu_kernel(
         add(pre6, pre6, xn6)
         product(kept6, rest6, state(6))
         turn(4, step45[:, 0, :], state(4), weighted[:, 4, :])
-        hn7 = step45[:, 0, :]
-        hn_to_sbuf(LAST, hn7)
+        z7 = step45[:, 0, :]
+        gate(LAST, z7)
+        rest7 = rest3
         turn_back(4, weighted[:, 4, :])
         scatter(4)
         new6 = weighted[:, 4, :]
         nc.scalar.activation(new6, pre6, ACT.Tanh)
         product(new6, new6, z6)
-        turn_both_ways(5, step45[:, 1, :], state(5))
+        one_minus(rest7, z7)
+        turn(5, step45[:, 1, :], state(5), weighted[:, 5, :])
+        hn7 = step45[:, 1, :]
+        hn_to_sbuf(LAST, hn7)
+        turn_back(5, weighted[:, 5, :])
         scatter(5)
-        rest7, pre7, kept7 = weighted[:, 5, :], z6, xn7
+        xn7, pre7 = weighted[:, 5, :], z6
+        xn_bn_to_sbuf(LAST, xn7)
         product(pre7, hn7, z7)
         add(pre7, pre7, xn7)
-        one_minus(rest7, z7)
+        kept7 = xn7
         product(kept7, rest7, state(LAST))
         turn_both_ways(6, new6, kept6)
         scatter(6)

@@ -28,7 +28,7 @@ LIST_GROUP = 16
 X_PIECE = JH // 2
 UNITS = [(c, h) for h in range(HALVES) for c in range(CHUNKS)]
 LAST = len(UNITS) - 1
-ZERO_SPLIT = 768
+ZERO_SPLIT = 640
 
 
 def tile_list_tgn_mgu_kernel(
@@ -42,7 +42,6 @@ def tile_list_tgn_mgu_kernel(
         psum = ctx.enter_context(tc.psum_pool(name="psum", bufs=1))
 
         offsets = keep.tile([P, J // LIST_GROUP], U16, name="offsets")
-        nc.sync.dma_start(offsets[:], offs)
 
         tab_s = keep.tile([P, T // 4], I32, name="tab_s", align_bytes=64)
         tab_w = keep.tile([P, T], I32, name="tab_w", align_bytes=64)
@@ -88,10 +87,12 @@ def tile_list_tgn_mgu_kernel(
         o_sb = [keep.tile([P, T], F32, name=f"o_sb{c}") for c in range(CHUNKS - 1)]
         nc.gpsimd.memset(weight_s[:], 0)
         zero_on_vector(tab_s, 0)
+        zero_on_vector(wgo_rows, 0.0)
         zero_on_vector(o_sb[0], 0.0)
         zero_on_vector(o_sb[1][:, 0:ZERO_SPLIT], 0.0)
 
         load_fp8_words(tab_w, tab_words)
+        nc.sync.dma_start(offsets[:], offs)
         load_scales(nc.sync, tab_s, tab_scales)
         load_x(0)
         load_x(1)
@@ -106,7 +107,7 @@ def tile_list_tgn_mgu_kernel(
         load_scales(nc.sync, wn_s, wn_scales)
         load_bias(bn_sb, bn)
         load_state(1)
-        nc.sync.dma_start(wgo_rows[:], wgo[0 : P * P // J, :].rearrange("a (b j) -> (a b) j", j=P))
+        nc.sync.dma_start(wgo_rows[0 : J // P, :], wgo[0].rearrange("(b j) -> b j", j=P))
         load_x(2)
         load_x(3)
         load_state(2)
@@ -146,8 +147,8 @@ def tile_list_tgn_mgu_kernel(
             return scales[:, (P // 4) * c : (P // 4) * (c + 1)].bitcast(U8)
 
         bank = [psum.tile([P, JH], F32, name=f"bank{i}") for i in range(BANKS)]
-        sz_bank = [bank[u % 2] for u in range(len(UNITS))]
-        xn_first = [bank[5 + u % 3] for u in range(CHUNKS)]
+        sz_bank = [bank[b] for b in (0, 1, 7, 0, 0, 7, 0, 7)]
+        xn_first = [bank[b] for b in (5, 6, 1, 5)]
         hn_bank = [bank[2 + u % 3] for u in range(CHUNKS)] + 2 * xn_first[2:4]
         xn_bank = xn_first + 2 * bank[3:5]
         turned, way_back = bank[2], bank[6]
@@ -198,10 +199,12 @@ def tile_list_tgn_mgu_kernel(
         def z_hn_on_vector(u, dst):
             nc.vector.tensor_tensor(dst, hn_bank[u][:], z[:, u, :], ALU.mult)
 
-        def cd_from_bank(u, row, argument):
+        def add_xn_on_vector(u, z_hn, dst):
+            nc.vector.tensor_tensor(dst, xn_bank[u][:], z_hn, ALU.add)
+
+        def tanh_with_bn(u, dst, argument):
             c = UNITS[u][0]
-            nc.vector.tensor_tensor(argument, xn_bank[u][:], row, ALU.add)
-            nc.scalar.activation(row, argument, ACT.Tanh, bias=bn_sb[:, c : c + 1])
+            nc.scalar.activation(dst, argument, ACT.Tanh, bias=bn_sb[:, c : c + 1])
 
         def one_minus(dst, gate_row):
             nc.scalar.activation(dst, gate_row, ACT.Copy, bias=1.0, scale=-1.0)
@@ -238,7 +241,6 @@ def tile_list_tgn_mgu_kernel(
         o_sb.append(reuse.tile([P, T], F32, name="o_late", align_bytes=64, offset=4 * P))
         nc.gpsimd.memset(o_sb[-1][:], 0.0)
 
-        w_cols = keep.tile([P, J // P], F32, name="w_cols")
         weighted = rows("weighted", LAST)
         later_results = rows("later_results", LAST - 1)
         result = {u: later_results[:, u - 1, :] for u in range(1, LAST)}
@@ -272,110 +274,116 @@ def tile_list_tgn_mgu_kernel(
         for u in (0, 1):
             gate(u, z[:, u, :])
             multiply_hn(u)
-            multiply_xn(u)
             z_hn_on_vector(u, new01[:, u, :])
-            cd_from_bank(u, new01[:, u, :], pre[:, u, :])
-        nc.tensor.transpose(way_back[:, 0:P], wgo_rows[:], ident[:])
-        nc.scalar.copy(w_cols[:], way_back[:, 0 : J // P])
+        for u in (0, 1):
+            gate(u + 2, z[:, u + 2, :])
+            multiply_xn(u)
+            add_xn_on_vector(u, new01[:, u, :], pre[:, u, :])
+            tanh_with_bn(u, new01[:, u, :], pre[:, u, :])
+        nc.tensor.transpose(sz_bank[2][:, 0:P], wgo_rows[:], ident[:])
         rest01 = rows("rest01", 2)
         nc.gpsimd.tensor_scalar(rest01[:], pair(z, 0), -1.0, 1.0, ALU.mult, ALU.add)
         kept0 = rest01[:, 0, :]
         product(kept0, kept0, state(0))
-        product(new01[:], new01[:], pair(z, 0))
+        for u in (0, 1):
+            product(new01[:, u, :], new01[:, u, :], z[:, u, :])
 
-        gather_state(1)
-        zhn23 = rows("zhn23", 2, tag="h_sb1")
+        zhn23 = rows("zhn23", 2)
         for u in (2, 3):
-            gate(u, z[:, u, :])
             multiply_hn(u)
             z_hn_on_vector(u, zhn23[:, u - 2, :])
+        for u in (2, 3):
+            multiply_xn(u)
+            add_xn_on_vector(u, zhn23[:, u - 2, :], pre[:, u, :])
+        gather_state(1)
         cast_x(2, xb[1])
         cast_x(3, xb[1])
         xq[1] = quantise_x(1, xb[1])
-        after_cast = rows("after_cast", 4, tag="x_raw3")
-        new23, weighted0, kept2 = pair(after_cast, 0), after_cast[:, 2, :], after_cast[:, 3, :]
+        after_cast = rows("after_cast", 6, tag="x_raw3")
+        cd23, rest23, weighted0 = pair(after_cast, 0), pair(after_cast, 2), after_cast[:, 4, :]
+        w_cols = after_cast[:, 5, 0 : J // P]
+        nc.scalar.copy(w_cols, sz_bank[2][:, 0 : J // P])
         for u in (2, 3):
-            xn_bn_to_sbuf(u, new23[:, u - 2, :])
+            tanh_with_bn(u, cd23[:, u - 2, :], pre[:, u, :])
         after_x = keep.tile([P, 3, JH], F32, name="after_x", tag="xb1", align_bytes=64)
-        pre23, kept1 = pair(after_x, 0), after_x[:, 2, :]
+        new23, kept1 = pair(after_x, 0), after_x[:, 2, :]
         product(kept1, rest01[:, 1, :], state(1))
-        add(pre23, new23, zhn23[:])
-        one_minus(kept2, z[:, 2, :])
+        product(new23, cd23, pair(z, 2))
         turn(0, new01[:, 0, :], kept0, weighted0)
+        one_minus(rest23, pair(z, 2))
         for u in (4, 5):
             gate(u, z[:, u, :])
-        xn5 = pre[:, 0, :]
-        xn_bn_to_sbuf(5, xn5)
-        multiply_hn(4)
-        multiply_hn(5)
-        multiply_xn(4)
-        nc.scalar.activation(new23, pre23, ACT.Tanh)
+        pre45 = pair(pre, 0)
+        for u in (4, 5):
+            xn_bn_to_sbuf(u, pre45[:, u - 4, :])
+        for u in (4, 5):
+            multiply_hn(u)
         gather_state(2)
         gather_state(3)
-        after_state = rows("after_state", 4, tag="h_sb3")
+        after_state = rows("after_state", 5, tag="h_sb3")
         zhn45, result[0], result[1] = pair(after_state, 0), after_state[:, 2, :], after_state[:, 3, :]
+        weighted2 = after_state[:, 4, :]
         turn_back(0, weighted0)
         turn(1, new01[:, 1, :], kept1, weighted[:, 1, :])
         turn_back(1, weighted[:, 1, :], sz_bank[5])
-        rest3, kept3 = pre23[:, 1, :], xn5
-        one_minus(rest3, z[:, 3, :])
+        kept2 = rest23[:, 0, :]
         product(kept2, kept2, state(2))
-        product(new23, new23, pair(z, 2))
 
         for u in (4, 5):
             z_hn_on_vector(u, zhn45[:, u - 4, :])
-        cd45 = pair(weighted, 0)
-        nc.vector.tensor_tensor(pre[:, 2, :], xn_bank[4][:], zhn45[:, 0, :], ALU.add)
-        nc.scalar.activation(cd45[:, 0, :], pre[:, 2, :], ACT.Tanh, bias=bn_sb[:, 0:1])
-        add(pre[:, 3, :], xn5, zhn45[:, 1, :])
-        product(kept3, rest3, state(3))
-        nc.scalar.activation(cd45[:, 1, :], pre[:, 3, :], ACT.Tanh)
         scatter(0)
         scatter(1)
+        turn(2, kept2, new23[:, 0, :], weighted2)
+        add(pre45, pre45, zhn45)
+        kept3 = zhn45[:, 0, :]
+        product(kept3, rest23[:, 1, :], state(3))
+        cd45 = pair(weighted, 0)
+        nc.scalar.activation(cd45, pre45, ACT.Tanh)
 
-        turn(2, new23[:, 0, :], kept2, weighted[:, 2, :])
-        z6 = kept2
-        gate(6, z6)
-        turn_back(2, weighted[:, 2, :])
+        turn_back(2, weighted2)
         scatter(2)
-        hn6 = weighted[:, 2, :]
-        hn_to_sbuf(6, hn6)
+        z6 = weighted2
+        gate(6, z6)
         step45 = pair(z, 2)
         nc.gpsimd.tensor_tensor(step45, cd45, picked[:, 0:2, JH:J], ALU.subtract)
-        product(step45, step45, pair(z, 4))
-        turn(3, new23[:, 1, :], kept3, weighted[:, 3, :])
-        xn6 = new23[:, 1, :]
-        xn_bn_to_sbuf(6, xn6)
+        for u in (4, 5):
+            product(step45[:, u - 4, :], step45[:, u - 4, :], z[:, u, :])
+        turn(3, kept3, new23[:, 1, :], weighted[:, 3, :])
+        hn6 = kept3
+        hn_to_sbuf(6, hn6)
         turn_back(3, weighted[:, 3, :])
         scatter(3)
+        xn6 = weighted[:, 3, :]
+        xn_bn_to_sbuf(6, xn6)
 
-        rest6, pre6, kept6 = weighted[:, 3, :], z[:, 4, :], xn6
-        one_minus(rest6, z6)
+        pre6, kept6 = z[:, 4, :], xn6
         product(pre6, hn6, z6)
         add(pre6, pre6, xn6)
-        product(kept6, rest6, state(6))
         turn(4, step45[:, 0, :], state(4), weighted[:, 4, :])
-        z7 = step45[:, 0, :]
-        gate(LAST, z7)
-        rest7 = rest3
+        rest6 = step45[:, 0, :]
+        one_minus(rest6, z6)
+        product(kept6, rest6, state(6))
         turn_back(4, weighted[:, 4, :])
         scatter(4)
-        new6 = weighted[:, 4, :]
+        z7 = weighted[:, 4, :]
+        gate(LAST, z7)
+        turn(5, step45[:, 1, :], state(5), weighted[:, 5, :])
+        new6 = step45[:, 1, :]
         nc.scalar.activation(new6, pre6, ACT.Tanh)
         product(new6, new6, z6)
-        one_minus(rest7, z7)
-        turn(5, step45[:, 1, :], state(5), weighted[:, 5, :])
-        hn7 = step45[:, 1, :]
-        hn_to_sbuf(LAST, hn7)
         turn_back(5, weighted[:, 5, :])
         scatter(5)
-        xn7, pre7 = weighted[:, 5, :], z6
-        xn_bn_to_sbuf(LAST, xn7)
+        hn7, pre7 = weighted[:, 5, :], z6
+        hn_to_sbuf(LAST, hn7)
         product(pre7, hn7, z7)
+        xn7 = pre6
+        xn_bn_to_sbuf(LAST, xn7)
         add(pre7, pre7, xn7)
-        kept7 = xn7
+        turn(6, new6, kept6, weighted[:, 6, :])
+        rest7, kept7 = new6, xn7
+        one_minus(rest7, z7)
         product(kept7, rest7, state(LAST))
-        turn_both_ways(6, new6, kept6)
+        turn_back(6, weighted[:, 6, :])
         scatter(6)
         blend7 = weighted[:, 6, :]
         nc.scalar.activation(blend7, pre7, ACT.Tanh)

@@ -65,8 +65,8 @@ def tile_list_tgn_mgu_kernel(
             nc.vector.memset(tile[:, width - 1 : width], zero)
 
         def load_scales(queue, scales, rows):
-            for q in range(QUADRANTS):
-                queue.dma_start(scales[32 * q : 32 * q + 4, :], rows[0, 4 * q : 4 * q + 4, :].bitcast(I32))
+            for r in range(QUADRANTS):
+                queue.dma_start(scales[r:P:32, :], rows[0, r:16:4, :].bitcast(I32))
 
         def load_fp8_words(tile, words):
             nc.sync.dma_start(tile[:], words[0].rearrange("p n i -> p (n i)").bitcast(I32))
@@ -148,9 +148,8 @@ def tile_list_tgn_mgu_kernel(
 
         bank = [psum.tile([P, JH], F32, name=f"bank{i}") for i in range(BANKS)]
         sz_bank = [bank[b] for b in (0, 1, 7, 0, 0, 7, 0, 7)]
-        xn_first = [bank[b] for b in (5, 6, 1, 5)]
-        hn_bank = [bank[2 + u % 3] for u in range(CHUNKS)] + 2 * xn_first[2:4]
-        xn_bank = xn_first + 2 * bank[3:5]
+        hn_bank = [bank[b] for b in (2, 3, 4, 2, 1, 5, 1, 5)]
+        xn_bank = [bank[b] for b in (5, 6, 1, 5, 3, 4, 3, 4)]
         turned, way_back = bank[2], bank[6]
 
         def rows(name, count, tag=None):
@@ -246,9 +245,9 @@ def tile_list_tgn_mgu_kernel(
         result = {u: later_results[:, u - 1, :] for u in range(1, LAST)}
         blocks = [slice(b * P, (b + 1) * P) for b in range(JH // P)]
 
-        def turn(u, term_a, term_b, scaled):
+        def turn(u, late_term, early_term, scaled):
             h = UNITS[u][1]
-            passes = [(term, cols) for term in (term_b, term_a) for cols in blocks]
+            passes = [(term, cols) for term in (early_term, late_term) for cols in blocks]
             for n, (term, cols) in enumerate(passes):
                 nc.tensor.matmul(turned[:, cols], term[:, cols], ident[:], start=n == 0, stop=n == len(passes) - 1, is_transpose=True)
             for b, cols in enumerate(blocks):
@@ -259,10 +258,6 @@ def tile_list_tgn_mgu_kernel(
             for cols in blocks:
                 nc.tensor.transpose(through[:, cols], scaled[:, cols], ident[:])
             nc.scalar.copy(result[u], through[:])
-
-        def turn_both_ways(u, term_a, term_b):
-            turn(u, term_a, term_b, weighted[:, u, :])
-            turn_back(u, weighted[:, u, :])
 
         def scatter(u):
             c, h = UNITS[u]

@@ -294,9 +294,9 @@ def tile_list_tgn_mgu_kernel(
         cast_x(2, xb[1])
         cast_x(3, xb[1])
         xq[1] = quantise_x(1, xb[1])
-        after_cast = rows("after_cast", 6, tag="x_raw3")
-        cd23, rest23, weighted0 = pair(after_cast, 0), pair(after_cast, 2), after_cast[:, 4, :]
-        w_cols = after_cast[:, 5, 0 : J // P]
+        after_cast = rows("after_cast", 5, tag="x_raw3")
+        cd23, kept2, weighted0 = pair(after_cast, 0), after_cast[:, 2, :], after_cast[:, 3, :]
+        w_cols = after_cast[:, 4, 0 : J // P]
         nc.scalar.copy(w_cols, sz_bank[2][:, 0 : J // P])
         for u in (2, 3):
             tanh_with_bn(u, cd23[:, u - 2, :], pre[:, u, :])
@@ -305,7 +305,7 @@ def tile_list_tgn_mgu_kernel(
         product(kept1, rest01[:, 1, :], state(1))
         product(new23, cd23, pair(z, 2))
         turn(0, new01[:, 0, :], kept0, weighted0)
-        one_minus(rest23, pair(z, 2))
+        one_minus(kept2, z[:, 2, :])
         for u in (4, 5):
             gate(u, z[:, u, :])
         pre45 = pair(pre, 0)
@@ -315,13 +315,13 @@ def tile_list_tgn_mgu_kernel(
             multiply_hn(u)
         gather_state(2)
         gather_state(3)
-        after_state = rows("after_state", 5, tag="h_sb3")
+        after_state = rows("after_state", 6, tag="h_sb3")
         zhn45, result[0], result[1] = pair(after_state, 0), after_state[:, 2, :], after_state[:, 3, :]
-        weighted2 = after_state[:, 4, :]
+        weighted2, rest3 = after_state[:, 4, :], after_state[:, 5, :]
         turn_back(0, weighted0)
         turn(1, new01[:, 1, :], kept1, weighted[:, 1, :])
         turn_back(1, weighted[:, 1, :], sz_bank[5])
-        kept2 = rest23[:, 0, :]
+        one_minus(rest3, z[:, 3, :])
         product(kept2, kept2, state(2))
 
         for u in (4, 5):
@@ -331,7 +331,7 @@ def tile_list_tgn_mgu_kernel(
         turn(2, kept2, new23[:, 0, :], weighted2)
         add(pre45, pre45, zhn45)
         kept3 = zhn45[:, 0, :]
-        product(kept3, rest23[:, 1, :], state(3))
+        product(kept3, rest3, state(3))
         cd45 = pair(weighted, 0)
         nc.scalar.activation(cd45, pre45, ACT.Tanh)
 

@@ -88,6 +88,8 @@ def tile_list_tgn_mgu_kernel(
         nc.gpsimd.memset(weight_s[:], 0)
         zero_on_vector(tab_s, 0)
         zero_on_vector(wgo_rows, 0.0)
+        warm = keep.tile([P, 1], F32, name="warm")
+        nc.scalar.activation(warm[:], wgo_rows[:, 0:1], ACT.Sigmoid)
         zero_on_vector(o_sb[0], 0.0)
         zero_on_vector(o_sb[1][:, 0:ZERO_SPLIT], 0.0)
 
@@ -116,9 +118,6 @@ def tile_list_tgn_mgu_kernel(
         load_scales(nc.gpsimd, un_s, un_scales)
         nc.gpsimd.memset(o_sb[1][:, ZERO_SPLIT:T], 0.0)
         nc.gpsimd.memset(o_sb[2][:], 0.0)
-
-        warm = keep.tile([P, 1], F32, name="warm")
-        nc.scalar.activation(warm[:], o_sb[0][:, 0:1], ACT.Sigmoid)
 
         def entries(h):
             width = JH // LIST_GROUP

from contextlib import ExitStack

import concourse.mybir as mybir
from concourse.masks import make_identity

K, M, N, T, J = 512, 512, 512, 2048, 1024
FLOPS = 2 * (2 * K + 2 * M) * N * J

F32 = mybir.dt.float32
BF16 = mybir.dt.bfloat16
I32 = mybir.dt.int32
U32 = mybir.dt.uint32
U16 = mybir.dt.uint16
U8 = mybir.dt.uint8
FP8X4 = mybir.dt.float8_e4m3fn_x4
FP4X4 = mybir.dt.float4_e2m1fn_x4
ACT = mybir.ActivationFunctionType
ALU = mybir.AluOpType

P = 128
PACK = 4
QUADRANTS = 4
BANKS = 8
JH = 512
HALVES = J // JH
CHUNKS = N // P
LIST_GROUP = 16
X_PIECE = JH // 2
UNITS = [(c, h) for h in range(HALVES) for c in range(CHUNKS)]
LAST = len(UNITS) - 1
ZERO_SPLIT = 640


def tile_list_tgn_mgu_kernel(
    tc, x, tab_words, tab_scales, wz_words, wz_scales, uz_words, uz_scales,
    wn_words, wn_scales, un_words, un_scales, bz, bn, hT, wgo, offs, out,
):
    nc = tc.nc
    with ExitStack() as ctx:
        keep = ctx.enter_context(tc.tile_pool(name="keep", bufs=1))
        reuse = ctx.enter_context(tc.tile_pool(name="reuse", bufs=1))
        psum = ctx.enter_context(tc.psum_pool(name="psum", bufs=1))

        offsets = keep.tile([P, J // LIST_GROUP], U16, name="offsets")

        tab_s = keep.tile([P, T // 4], I32, name="tab_s", align_bytes=64)
        tab_w = keep.tile([P, T], I32, name="tab_w", align_bytes=64)
        weight_s = keep.tile([P, N], I32, name="weight_s", align_bytes=64)
        uz_s, wz_s, un_s, wn_s = [weight_s[:, a * (N // 4) : (a + 1) * (N // 4)] for a in range(4)]
        wz_w = keep.tile([P, N // 2], I32, name="wz_w", align_bytes=64)
        uz_w = keep.tile([P, N], I32, name="uz_w", align_bytes=64)
        wn_w = keep.tile([P, N // 2], I32, name="wn_w", align_bytes=64)
        un_w = keep.tile([P, N], I32, name="un_w", align_bytes=64)
        x_rows = x.rearrange("(p i) j -> p i j", i=PACK)
        x_raw = [keep.tile([P, PACK, X_PIECE], F32, name=f"x_raw{a}", tag=f"x_raw{a}") for a in range(J // X_PIECE)]
        h_sb = [keep.tile([P, T], F32, name=f"h_sb{c}", tag=f"h_sb{c}") for c in range(CHUNKS)]
        wgo_last = keep.tile([P, JH], F32, name="wgo_last")
        wgo_rows = keep.tile([P, P], F32, name="wgo_rows")
        bz_sb = keep.tile([P, CHUNKS], F32, name="bz_sb")
        bn_sb = keep.tile([P, CHUNKS], F32, name="bn_sb")

        def zero_on_vector(tile, zero):
            width = tile.shape[1]
            nc.vector.memset(tile[:, 0 : width - 1], zero)
            nc.vector.memset(tile[:, width - 1 : width], zero)

        def load_scales(queue, scales, rows):
            for r in range(QUADRANTS):
                queue.dma_start(scales[r:P:32, :], rows[0, r:16:4, :].bitcast(I32))

        def load_fp8_words(tile, words):
            nc.sync.dma_start(tile[:], words[0].rearrange("p n i -> p (n i)").bitcast(I32))

        def load_fp4_words(tile, words):
            nc.sync.dma_start(tile[:], words[0].bitcast(I32))

        def load_bias(tile, vec):
            with nc.allow_non_contiguous_dma(reason="one bias value to a partition"):
                nc.sync.dma_start(tile[:], vec.rearrange("(c p) -> p c", p=P))

        def load_state(c):
            nc.sync.dma_start(h_sb[c][:], hT[c * P : (c + 1) * P, :])

        def load_x(a):
            nc.sync.dma_start(x_raw[a][:], x_rows[:, :, a * X_PIECE : (a + 1) * X_PIECE])

        o_sb = [keep.tile([P, T], F32, name=f"o_sb{c}") for c in range(CHUNKS - 1)]
        nc.gpsimd.memset(weight_s[:], 0)
        zero_on_vector(tab_s, 0)
        zero_on_vector(wgo_rows, 0.0)
        warm = keep.tile([P, 1], F32, name="warm")
        nc.scalar.activation(warm[:], wgo_rows[:, 0:1], ACT.Sigmoid)
        zero_on_vector(o_sb[0], 0.0)
        zero_on_vector(o_sb[1][:, 0:ZERO_SPLIT], 0.0)

        load_fp8_words(tab_w, tab_words)
        nc.sync.dma_start(offsets[:], offs)
        load_scales(nc.sync, tab_s, tab_scales)
        load_x(0)
        load_x(1)
        load_fp8_words(uz_w, uz_words)
        load_scales(nc.sync, uz_s, uz_scales)
        load_state(0)
        load_scales(nc.sync, wz_s, wz_scales)
        load_fp4_words(wz_w, wz_words)
        load_bias(bz_sb, bz)
        load_fp8_words(un_w, un_words)
        load_fp4_words(wn_w, wn_words)
        load_scales(nc.sync, wn_s, wn_scales)
        load_bias(bn_sb, bn)
        load_state(1)
        nc.sync.dma_start(wgo_rows[0 : J // P, :], wgo[0].rearrange("(b j) -> b j", j=P))
        load_x(2)
        load_x(3)
        load_state(2)
        load_state(3)
        nc.sync.dma_start(wgo_last[:], wgo[:, JH:J])
        load_scales(nc.gpsimd, un_s, un_scales)
        nc.gpsimd.memset(o_sb[1][:, ZERO_SPLIT:T], 0.0)
        nc.gpsimd.memset(o_sb[2][:], 0.0)

        def entries(h):
            width = JH // LIST_GROUP
            return offsets[:, h * width : (h + 1) * width]

        def cast_x(a, xb):
            first = (a * X_PIECE) % JH
            nc.scalar.copy(
                out=xb[:, first : first + X_PIECE, :].rearrange("p (a b) i -> p a i b", b=4),
                in_=x_raw[a][:].rearrange("p i (a b) -> p a i b", b=4),
            )

        def quantise_x(h, xb):
            words = keep.tile([P, JH], U32, name=f"x_w{h}", align_bytes=64)
            scales = keep.tile([P, JH], U8, name=f"x_s{h}", align_bytes=64)
            nc.vector.quantize_mx(out=words[:].bitcast(FP8X4), scales=scales[:], in_=xb[:].rearrange("p j i -> p (j i)"))
            return words[:].bitcast(FP8X4), scales[:]

        def fp4_cols(words, c):
            return words[:, (P // 2) * c : (P // 2) * (c + 1)].bitcast(FP4X4)

        def fp8_cols(words, c):
            return words[:, P * c : P * (c + 1)].bitcast(FP8X4)

        def scale_cols(scales, c):
            return scales[:, (P // 4) * c : (P // 4) * (c + 1)].bitcast(U8)

        bank = [psum.tile([P, JH], F32, name=f"bank{i}") for i in range(BANKS)]
        sz_bank = [bank[b] for b in (0, 1, 7, 0, 0, 7, 0, 7)]
        hn_bank = [bank[b] for b in (2, 3, 4, 2, 1, 5, 1, 5)]
        xn_bank = [bank[b] for b in (5, 6, 1, 5, 3, 4, 3, 4)]
        turned, way_back = bank[2], bank[6]

        def rows(name, count, tag=None):
            return keep.tile([P, count, JH], F32, name=name, tag=tag or name)

        def pair(tile, first):
            return tile[:, first : first + 2, :]

        xq, vq = {}, {}
        z = rows("z", 6)
        pre = rows("pre", 4)
        picked = keep.tile([P, CHUNKS, J], F32, name="picked")

        def state(u):
            c, h = UNITS[u]
            return picked[:, c, h * JH : (h + 1) * JH]

        def mx(dst, lw, ls, operand, start, stop):
            nc.tensor.matmul_mx(out=dst[:], lhsT=lw, lhsT_scale=ls, rhs=operand[0], rhs_scale=operand[1], start=start, stop=stop)

        def gate(u, dst):
            c, h = UNITS[u]
            passes = [(fp8_cols(uz_w, c), scale_cols(uz_s, c), vq[h]), (fp4_cols(wz_w, c), scale_cols(wz_s, c), xq[h])]
            first, second = passes[::-1] if h else passes
            mx(sz_bank[u], *first, True, False)
            mx(sz_bank[u], *second, False, True)
            nc.scalar.activation(dst, sz_bank[u][:], ACT.Sigmoid, bias=bz_sb[:, c : c + 1])

        def multiply_hn(u):
            c, h = UNITS[u]
            mx(hn_bank[u], fp8_cols(un_w, c), scale_cols(un_s, c), vq[h], True, True)

        def multiply_xn(u):
            c, h = UNITS[u]
            mx(xn_bank[u], fp4_cols(wn_w, c), scale_cols(wn_s, c), xq[h], True, True)

        def hn_to_sbuf(u, dst):
            multiply_hn(u)
            nc.scalar.copy(dst, hn_bank[u][:])

        def xn_bn_to_sbuf(u, dst):
            c = UNITS[u][0]
            multiply_xn(u)
            nc.scalar.activation(dst, xn_bank[u][:], ACT.Identity, bias=bn_sb[:, c : c + 1])

        def z_hn_on_vector(u, dst):
            nc.vector.tensor_tensor(dst, hn_bank[u][:], z[:, u, :], ALU.mult)

        def add_xn_on_vector(u, z_hn, dst):
            nc.vector.tensor_tensor(dst, xn_bank[u][:], z_hn, ALU.add)

        def tanh_with_bn(u, dst, argument):
            c = UNITS[u][0]
            nc.scalar.activation(dst, argument, ACT.Tanh, bias=bn_sb[:, c : c + 1])

        def one_minus(dst, gate_row):
            nc.scalar.activation(dst, gate_row, ACT.Copy, bias=1.0, scale=-1.0)

        def product(dst, a, b):
            nc.gpsimd.tensor_tensor(dst, a, b, ALU.mult)

        def add(dst, a, b):
            nc.gpsimd.tensor_tensor(dst, a, b, ALU.add)

        def gather_state(c):
            nc.vector.tensor_copy(picked[:, c, :], h_sb[c][:].indirect(offsets[:]))

        def store_if_complete(u):
            c, h = UNITS[u]
            if h == HALVES - 1:
                nc.sync.dma_start(out[c * P : (c + 1) * P, :], o_sb[c][:])

        for h in range(HALVES):
            words = keep.tile([P, JH], U32, name=f"v_w{h}", align_bytes=64)
            scales = keep.tile([P, JH], U8, name=f"v_s{h}", align_bytes=64)
            nc.vector.tensor_copy(words[:], tab_w[:].bitcast(U32).indirect(entries(h)))
            nc.vector.tensor_copy(scales[:], tab_s[:].bitcast(U8).indirect(entries(h)))
            vq[h] = (words[:].bitcast(FP8X4), scales[:])
        xb = [
            reuse.tile([P, JH, PACK], BF16, name="xb0", align_bytes=64, offset=0),
            keep.tile([P, JH, PACK], BF16, name="xb1", tag="xb1", align_bytes=64),
        ]
        cast_x(0, xb[0])
        cast_x(1, xb[0])
        xq[0] = quantise_x(0, xb[0])
        ident = reuse.tile([P, P], F32, name="ident", align_bytes=64, offset=0)
        make_identity(nc, ident[:])
        o_sb.append(reuse.tile([P, T], F32, name="o_late", align_bytes=64, offset=4 * P))
        nc.gpsimd.memset(o_sb[-1][:], 0.0)

        weighted = rows("weighted", LAST)
        later_results = rows("later_results", LAST - 1)
        result = {u: later_results[:, u - 1, :] for u in range(1, LAST)}
        blocks = [slice(b * P, (b + 1) * P) for b in range(JH // P)]

        def turn(u, late_term, early_term, scaled):
            h = UNITS[u][1]
            passes = [(term, cols) for term in (early_term, late_term) for cols in blocks]
            for n, (term, cols) in enumerate(passes):
                nc.tensor.matmul(turned[:, cols], term[:, cols], ident[:], start=n == 0, stop=n == len(passes) - 1, is_transpose=True)
            for b, cols in enumerate(blocks):
                col = h * len(blocks) + b
                nc.scalar.activation(scaled[:, cols], turned[:, cols], ACT.Copy, scale=w_cols[:, col : col + 1])

        def turn_back(u, scaled, through=way_back):
            for cols in blocks:
                nc.tensor.transpose(through[:, cols], scaled[:, cols], ident[:])
            nc.scalar.copy(result[u], through[:])

        def scatter(u):
            c, h = UNITS[u]
            nc.vector.tensor_copy(o_sb[c][:].indirect(entries(h)), result[u])
            store_if_complete(u)

        new01 = rows("new01", 2)
        gather_state(0)
        for u in (0, 1):
            gate(u, z[:, u, :])
            multiply_hn(u)
            z_hn_on_vector(u, new01[:, u, :])
        for u in (0, 1):
            gate(u + 2, z[:, u + 2, :])
            multiply_xn(u)
            add_xn_on_vector(u, new01[:, u, :], pre[:, u, :])
            tanh_with_bn(u, new01[:, u, :], pre[:, u, :])
        nc.tensor.transpose(sz_bank[2][:, 0:P], wgo_rows[:], ident[:])
        rest01 = rows("rest01", 2)
        nc.gpsimd.tensor_scalar(rest01[:], pair(z, 0), -1.0, 1.0, ALU.mult, ALU.add)
        kept0 = rest01[:, 0, :]
        product(kept0, kept0, state(0))
        for u in (0, 1):
            product(new01[:, u, :], new01[:, u, :], z[:, u, :])

        zhn23 = rows("zhn23", 2)
        for u in (2, 3):
            multiply_hn(u)
            z_hn_on_vector(u, zhn23[:, u - 2, :])
        for u in (2, 3):
            multiply_xn(u)
            add_xn_on_vector(u, zhn23[:, u - 2, :], pre[:, u, :])
        gather_state(1)
        cast_x(2, xb[1])
        cast_x(3, xb[1])
        xq[1] = quantise_x(1, xb[1])
        after_cast = rows("after_cast", 5, tag="x_raw3")
        cd23, kept2, weighted0 = pair(after_cast, 0), after_cast[:, 2, :], after_cast[:, 3, :]
        w_cols = after_cast[:, 4, 0 : J // P]
        nc.scalar.copy(w_cols, sz_bank[2][:, 0 : J // P])
        for u in (2, 3):
            tanh_with_bn(u, cd23[:, u - 2, :], pre[:, u, :])
        after_x = keep.tile([P, 3, JH], F32, name="after_x", tag="xb1", align_bytes=64)
        new23, kept1 = pair(after_x, 0), after_x[:, 2, :]
        product(kept1, rest01[:, 1, :], state(1))
        product(new23, cd23, pair(z, 2))
        turn(0, new01[:, 0, :], kept0, weighted0)
        one_minus(kept2, z[:, 2, :])
        for u in (4, 5):
            gate(u, z[:, u, :])
        pre45 = pair(pre, 0)
        for u in (4, 5):
            xn_bn_to_sbuf(u, pre45[:, u - 4, :])
        for u in (4, 5):
            multiply_hn(u)
        gather_state(2)
        gather_state(3)
        after_state = rows("after_state", 6, tag="h_sb3")
        zhn45, result[0], result[1] = pair(after_state, 0), after_state[:, 2, :], after_state[:, 3, :]
        weighted2, rest3 = after_state[:, 4, :], after_state[:, 5, :]
        turn_back(0, weighted0)
        turn(1, new01[:, 1, :], kept1, weighted[:, 1, :])
        turn_back(1, weighted[:, 1, :], sz_bank[5])
        one_minus(rest3, z[:, 3, :])
        product(kept2, kept2, state(2))

        for u in (4, 5):
            z_hn_on_vector(u, zhn45[:, u - 4, :])
        scatter(0)
        scatter(1)
        turn(2, kept2, new23[:, 0, :], weighted2)
        add(pre45, pre45, zhn45)
        kept3 = zhn45[:, 0, :]
        product(kept3, rest3, state(3))
        cd45 = pair(weighted, 0)
        nc.scalar.activation(cd45, pre45, ACT.Tanh)

        turn_back(2, weighted2)
        scatter(2)
        z6 = weighted2
        gate(6, z6)
        step45 = pair(z, 2)
        nc.gpsimd.tensor_tensor(step45, cd45, picked[:, 0:2, JH:J], ALU.subtract)
        for u in (4, 5):
            product(step45[:, u - 4, :], step45[:, u - 4, :], z[:, u, :])
        turn(3, kept3, new23[:, 1, :], weighted[:, 3, :])
        hn6 = kept3
        hn_to_sbuf(6, hn6)
        turn_back(3, weighted[:, 3, :])
        scatter(3)
        xn6 = weighted[:, 3, :]
        xn_bn_to_sbuf(6, xn6)

        pre6, kept6 = z[:, 4, :], xn6
        product(pre6, hn6, z6)
        add(pre6, pre6, xn6)
        turn(4, step45[:, 0, :], state(4), weighted[:, 4, :])
        rest6 = step45[:, 0, :]
        one_minus(rest6, z6)
        product(kept6, rest6, state(6))
        turn_back(4, weighted[:, 4, :])
        scatter(4)
        z7 = weighted[:, 4, :]
        gate(LAST, z7)
        turn(5, step45[:, 1, :], state(5), weighted[:, 5, :])
        new6 = step45[:, 1, :]
        nc.scalar.activation(new6, pre6, ACT.Tanh)
        product(new6, new6, z6)
        turn_back(5, weighted[:, 5, :])
        scatter(5)
        hn7, pre7 = weighted[:, 5, :], z6
        hn_to_sbuf(LAST, hn7)
        product(pre7, hn7, z7)
        xn7 = pre6
        xn_bn_to_sbuf(LAST, xn7)
        add(pre7, pre7, xn7)
        turn(6, new6, kept6, weighted[:, 6, :])
        rest7, kept7 = new6, xn7
        one_minus(rest7, z7)
        product(kept7, rest7, state(LAST))
        turn_back(6, weighted[:, 6, :])
        scatter(6)
        blend7 = weighted[:, 6, :]
        nc.scalar.activation(blend7, pre7, ACT.Tanh)
        product(blend7, blend7, z7)
        add(blend7, blend7, kept7)
        c, h = UNITS[LAST]
        nc.vector.tensor_tensor(o_sb[c][:].indirect(entries(h)), blend7, wgo_last[:], ALU.mult)
        store_if_complete(LAST)
